import numpy as np, ml_dtypes
CORES = [5,29,101,125,133,157,229,253]
N = 8
BF = ml_dtypes.bfloat16
def gentries(a):
    return np.ascontiguousarray(a.reshape(8, 16, -1).transpose(0, 2, 1)).reshape(8, -1)
def gtable(e):
    e = np.asarray(e); return np.ascontiguousarray(e.reshape(8, -1, 16).transpose(0, 2, 1)).reshape(128, -1).astype(np.int32)
C, M, G, T, TH, S = 4096, 512, 256, 4, 11, 16
def parts(rng):
    R = rng.integers(0, 256, (N, 8, 16, C)); P = rng.integers(0, M, (N, 8, 16, M)); O = rng.integers(0, M, (N, 8, 16, M))
    z = (256 * rng.choice(np.array([0.6, 0.8, 1.0]), (N, 8, 1, G)) * rng.random((N, 8, 16, G))).astype(np.int64)
    return R, P, O, z, rng.integers(0, M, (N, 8, G)), rng.integers(1, 257, (N, 8, 16))
def pack(R, P, O, z, mv, w):
    P = np.array(P); O = np.array(O); P[:, :, 0] = np.arange(M); O[:, :, 0] = np.arange(M)
    return {"strat": R.reshape(N, 128, C).astype(np.float32).astype(BF), "vp": P.reshape(N, 128, M).astype(np.int32), "vo": O.reshape(N, 128, M).astype(np.int32),
            "z0": z.reshape(N, 128, G).astype(np.float32).astype(BF), "mv": np.stack([gtable(a) for a in mv]), "wt": w.reshape(N, 128, 1).astype(np.int32)}
def plant(rng, R, P, O, z, mv, w):
    h = 17 - TH; m = np.arange(M)
    w[:, :, 13] = 16; w[:, :, 14] = 1; w[:, 2, :13] = np.maximum(w[:, 2, :13], 160)
    for r in range(N):
        q = (r + 1) % N
        for g in range(8):
            own = rng.permutation(M)[:12]; i = 1 + rng.permutation(G - 17)[:5]; wq = w[q, g]
            for e in range(4):
                a = int(i[e]); mv[r, g, a] = own[e]; P[r, g, 3 + 4 * e, own[e]] = M - 1
                z[r, g, :h, a] = 255; z[r, g, 13:15, a] = 0
                d = (4065 - int(np.sum(wq * z[r, g, :, a]))) & 4095
                z[r, g, 13, a] = d >> 4; z[r, g, 14, a] = d & 15
            if g == 2:
                left = 2 ** 19
                for j in list(range(13)) + [15, 13, 14]:
                    n = min(255, left // int(wq[j])); z[r, g, j, int(i[4])] = n; left -= n * int(wq[j])
            end = G - 15 + 2 * np.arange(8); mv[r, g, end] = own[4:]
            z[r, g, :h, G - 15::2] = 255
            u = np.sum(wq[:, None] * z[r, g], axis=0) & 4095; p0 = int(u[0]) & (S - 1)
            R[q, g, :, p0] = 255 * rng.integers(0, 2, 16)
            ad = (((m[:, None] * u[end][None, :]) >> 5) + m[:, None] + 37 * 15) & (C - 1)
            for e in range(8):
                good = np.flatnonzero(ad[:, e] == p0)
                if len(good): P[r, g, 15, own[4 + e]] = rng.choice(good)
    return R, P, O, z, mv, w
def setup_inputs(rng):
    return pack(*plant(rng, *parts(rng)))
def corner(rng, first):
    R, P, O, z, mv, w = parts(rng); R = np.maximum(R, 1); m = np.arange(M)[None, :]; j = np.arange(16)[:, None]
    forms = [m + 0 * j, np.maximum(m - j, 0), np.minimum(m + j, M - 1), np.where((m + j) % 2 == 0, 0, M - 1)]
    P = np.stack([np.stack([forms[(g + r) % 4] for g in range(8)]) for r in range(N)])
    O = np.stack([np.stack([forms[(g + r + 1 + g // 4) % 4] for g in range(8)]) for r in range(N)])
    cnt = np.array([255, 256, 1024, 512, 257, 511, 1, 8 * G - 1, 8 * G, 0, 1536, 4 * G, 6 * G, 8 * G - 256, 1023, 1025])[first * N:first * N + N]
    cnt = np.roll(cnt, int(rng.integers(0, N)))
    for r in range(N):
        for g in range(8):
            e = (g + r) % 3
            if e == 0: mv[r, g] = rng.choice(np.array([0, M - 1]), G)
            elif e == 1: mv[r, g] = rng.integers(0, M)
            else: mv[r, g] = rng.permutation(M)[:G]
        hit = np.zeros(8 * G, bool); hit[rng.permutation(8 * G)[:int(cnt[r])]] = True
        z[r] = np.where(hit.reshape(8, 1, G), 0, 255)
    w[:, 1] = 1; w[:, 5] = 256
    return pack(R, P, O, z, mv, w)
def setup_inputs_corners(rng):
    return corner(rng, 0)
def setup_inputs_corners_two(rng):
    return corner(rng, 1)
def setup_inputs_ends(rng):
    R = np.where(rng.random((N, 8, 16, C)) < rng.choice(np.array([0.1, 0.5, 0.75, 0.9]), (N, 8, 1, C)), 255, 0)
    z = np.where(rng.random((N, 8, 16, G)) < rng.choice(np.array([0.05, 0.3, 0.8]), (N, 8, 1, G)), 255, 0)
    P = (M - 1) * rng.integers(0, 2, (N, 8, 16, M)); O = (M - 1) * rng.integers(0, 2, (N, 8, 16, M)); mv = (M - 1) * rng.integers(0, 2, (N, 8, G))
    w = np.where(rng.random((N, 8, 16)) < 0.5, 256, 1)
    mv[:, :, G - 1] = M - 1; P[:, :, 15, M - 1] = M - 1; O[:, :, 15, M - 1] = M - 1
    w[:, 0] = 256; R[:, 0] = np.where(rng.random((N, 1, C)) < 0.5, 255, 0); z[:, 0, :, G - 1] = 255; z[:, 0, :, 0] = 0
    w[:, 5:] = 256; w[:, 5:, 15] = 1
    c = np.zeros(16, np.int64); c[3] = 255; c[15] = 255
    x8 = np.array([0, 1, 2, 4, 5, 6, 7, 8]); y4 = np.array([9, 10, 11, 12])
    for g in (6, 7):
        hot = ((np.arange(C) >> 7) + g) % 2 == 1
        R[:, g] = c[None, :, None]
        R[:, g, x8] = np.where(hot, 192, 64 * rng.integers(0, 2, (N, 1, C))); R[:, g, y4] = np.where(hot, 128, 0)
        z[:, g, :, 1::2] = c[None, :, None]; z[:, g, :, G - 1] = c[None, :]
    R[:, 5] = 0; R[:, 5, 15] = 255; R[:, 5, y4] = 128 * rng.integers(0, 2, (N, 1, C))
    R[:, 5, x8, C - 1] = 192; R[:, 5, y4, C - 1] = 128
    z[:, 5] = 0; z[:, 5, 15] = 255
    m = np.arange(M); f = ((m * 255) >> 5) + m
    for j in range(1, 14):
        near = m[((f + 37 * (j + 1)) & (C - 1)) >= C - 256]
        P[:, 5, j] = rng.choice(near, (N, M)); O[:, 5, j] = rng.choice(near, (N, M))
    P[:, 5, 14:] = rng.integers(0, M, (N, 2, M)); O[:, 5, 14:] = rng.integers(0, M, (N, 2, M))
    mv[:, 5] = np.argsort(rng.random((N, M)), axis=1)[:, :G]; mv[:, 5, G - 1] = M - 1
    keep = np.array(R[3, 5])
    z[1, :, :17 - TH] = 255; z[2, :, :TH] = 0; R[3, :, :TH] = 255
    a0 = f[mv[2, 5]] & (C - 1); keep[np.ix_(x8, a0)] = 192; keep[np.ix_(y4, a0)] = 128; R[3, 5] = keep
    return pack(R, P, O, z, mv, w)
def setup_inputs_spread(rng):
    R = np.minimum((np.exp2(8 * rng.random((N, 8, 1, C))) * rng.random((N, 8, 16, C))).astype(np.int64), 255)
    z = np.minimum((np.exp2(8 * rng.random((N, 8, 1, G))) * rng.random((N, 8, 16, G))).astype(np.int64), 255)
    P = np.minimum((M * rng.random((N, 8, 16, M)) ** 3).astype(np.int64), M - 1); O = np.minimum((M * rng.random((N, 8, 16, M)) ** 3).astype(np.int64), M - 1)
    mv = np.minimum((M * rng.random((N, 8, G)) ** 2).astype(np.int64), M - 1)
    w = np.minimum(np.maximum(np.rint(np.exp2(8 * rng.random((N, 8, 16)))).astype(np.int64), 1), 256)
    v0 = [v for v in range(M + G * (T - 2), M + G * (T - 1)) if (-(2 ** 22)) % v < 32][0]
    u0 = (2 ** 22 + v0 - 1) // v0 - 32
    r = int(rng.integers(0, N)); q = (r + 1 + (T - 1) % (N - 1)) % N; p = (r + 1 + (T - 2) % (N - 1)) % N
    R[q, :, :17 - TH] = 0
    for g in (1, 3, 4, 6):
        w[q, g, 13] = 16; w[q, g, 14] = 1
        c = rng.integers(0, 256, 16); c[13:15] = 0
        d = (u0 - int(np.sum(w[q, g] * c))) & 4095
        c[13] = d >> 4; c[14] = d & 15
        R[p, g] = c[:, None]
        R[q, g, 15] = 0; R[q, g, 15, 0] = 255
    return pack(R, P, O, z, mv, w)
def setup_inputs_ties(rng):
    R, P, O, z, mv, w = parts(rng)
    b = rng.integers(0, 255, (8, 16)); b[0] = 0; b[6] = 254
    share = rng.permutation(np.array([0.02, 0.04, 0.07, 0.1, 0.15, 0.2, 0.3, 0.5])).reshape(1, 8, 1, 1)
    cnt = np.where(rng.random((N, 8, 1, C)) < share, rng.choice(np.array([TH, TH, TH, TH + 1, 16]), (N, 8, 1, C)), rng.choice(np.array([TH - 1, TH - 1, TH - 1, 0]), (N, 8, 1, C)))
    R = b[None, :, :, None] + (np.argsort(rng.random((N, 8, 16, C)), axis=2) < cnt)
    z = b[None, :, :, None] + (rng.random((N, 8, 1, G)) < 0.125) + np.zeros((N, 8, 16, G), np.int64)
    return pack(R, P, O, z, mv, w)
def check_inputs(d):
    bad = []
    for k, lo, hi in (("strat", 0, 255), ("vp", 0, M - 1), ("vo", 0, M - 1), ("z0", 0, 255), ("mv", 0, M - 1), ("wt", 1, 256)):
        a = np.asarray(d[k]).astype(np.float64)
        if not (np.min(a) >= lo and np.max(a) <= hi): bad.append("range of " + k)
        elif np.any(a != np.floor(a)): bad.append("whole numbers in " + k)
    for k in ("vp", "vo"):
        if np.any(np.asarray(d[k]).reshape(-1, 8, 16, M)[:, :, 0] != np.arange(M)): bad.append("row 0 of the views in " + k)
    return bad
def reference(strat, vp, vo, z0, mv, wt):
    R = strat.astype(np.float32).astype(np.int32).reshape(N, 8, 16, C); z = z0.astype(np.float32).astype(np.int32).reshape(N, 8, 16, G)
    w = wt.astype(np.int32).reshape(N, 8, 16, 1); v = np.stack([gentries(a) for a in mv]).astype(np.int64)
    room = np.zeros((N, 8, 16, G * T), np.int32)
    views = [np.concatenate([a.astype(np.int32).reshape(N, 8, 16, M), room], axis=3) for a in (vp, vo)]
    count = np.zeros(N, np.int64); kk = np.arange(16)[None, None, :, None]; verdicts = np.zeros((N, 8, T, G), np.int64)
    for t in range(T):
        mover, other = views[t % 2], views[1 - t % 2]
        q = (np.arange(N) + 1 + t % (N - 1)) % N
        L = np.take_along_axis(mover, v[:, :, None, :], 3).astype(np.int64)
        u = np.add.reduce(w[q] * z, axis=2).astype(np.int64) & 4095
        ad = (((L * u[:, :, None, :]) >> 5) + L + 37 * kk + (count[q] & 255)[:, None, None, None]) & (C - 1)
        Y = np.take_along_axis(R[q], ad.reshape(N, 8, 1, 16 * G), 3).reshape(N, 8, 16, 16, G)
        hit = np.add.reduce((Y > z[:, :, :, None, :]).astype(np.int32), axis=2) >= TH
        hit[:, :, 15] = True
        kap = np.argmax(hit, axis=2)
        use = (kk <= kap[:, :, None, :])[:, :, None]
        z = (np.maximum.reduce(np.where(use, Y, 0), axis=3) + np.minimum.reduce(np.where(use, Y, 255), axis=3)) >> 1
        z = z.astype(np.int32)
        if t < T - 1:
            place = S * np.arange(G) + (u & (S - 1))
            for r in range(N):
                ix = np.repeat(place[r][:, None, :], 16, axis=1); mine = R[int(q[r])]
                np.put_along_axis(mine, ix, (np.take_along_axis(mine, ix, 2) + z[r]) >> 1, 2)
        count[q] = np.add.reduce((kap < 15).reshape(N, 8 * G).astype(np.int64), axis=1)
        named = np.take_along_axis(L, kap[:, :, None, :], 2)
        resumed = np.take_along_axis(other, named, 3)
        n0 = M + G * t; n = np.zeros((N, 8, 1, G), np.int64) + n0 + np.arange(G)
        mover[..., n0:n0 + G] = np.concatenate([n, L[:, :, :15]], axis=2)
        other[..., n0:n0 + G] = np.concatenate([n, resumed[:, :, :15]], axis=2)
        v = n[:, :, 0]; verdicts[:, :, t] = kap
    e = M + G * (T - 1)
    return {"yp": views[0][..., e:e + G].reshape(N, 128, G).astype(np.float32), "yo": views[1][..., e:e + G].reshape(N, 128, G).astype(np.float32),
            "yz": z.reshape(N, 128, G).astype(np.float32).astype(BF), "yk": verdicts.reshape(N, 8, T * G).astype(np.float32)}

@@ -1,0 +1,676 @@
+from concourse.mybir import AluOpType as A, ActivationFunctionType as F
+
+N, TURNS, H = 8, 4, 128
+RW = 4096 + 816
+GS = (64, 96)
+CUTS = (56, 96)
+KS = (9, 7)
+M35, M23 = 1.5 * 2.0 ** 35, 1.5 * 2.0 ** 23
+
+SCRATCH = {
+    "RT": ("sbuf", [128, RW], "bfloat16"),
+    "VP32": ("sbuf", [128, 512], "int32"), "VO32": ("sbuf", [128, 512], "int32"),
+    "MV32": ("sbuf", [128, 16], "int32"), "MV16": ("sbuf", [128, 16], "uint16"),
+    "Z0B": ("sbuf", [128, 256], "bfloat16"), "WT32": ("sbuf", [128, 1], "int32"), "WTF": ("sbuf", [128, 1], "float32"),
+    "PV": ("sbuf", [128, 512], "float16"), "OV": ("sbuf", [128, 512], "float16"),
+    "HL1": ("sbuf", [128, 256], "float16"), "HL3": ("sbuf", [128, 256], "float16"),
+    "HB2": ("sbuf", [128, 256], "float16"), "HB3": ("sbuf", [128, 256], "float16"), "L3I": ("sbuf", [128, 256], "float16"),
+    "MX": ("sbuf", [128, 2048], "bfloat16"), "MN": ("sbuf", [128, 2048], "bfloat16"),
+    "DIF": ("sbuf", [128, 128], "float32"), "DB": ("sbuf", [128, 128], "float32"), "JI": ("sbuf", [128, 128], "int32"),
+    "JS": ("sbuf", [128, 128], "int32"), "JM": ("sbuf", [128, 128], "int32"), "PI": ("sbuf", [128, 1], "int32"),
+    "PG": ("sbuf", [128, 1], "int32"), "PK": ("sbuf", [128, 1], "int32"), "COL": ("sbuf", [128, 16], "float32"),
+    "BLK": ("sbuf", [128, 128], "bfloat16"), "T0": ("sbuf", [128, 128], "bfloat16"), "T1": ("sbuf", [128, 128], "bfloat16"),
+    "IB": ("sbuf", [128, 128], "bfloat16"), "NIB": ("sbuf", [128, 128], "bfloat16"), "IH": ("sbuf", [128, 128], "float16"),
+    "NH": ("sbuf", [128, 128], "float16"), "B14": ("sbuf", [128, 128], "bfloat16"),
+    "BF": ("sbuf", [128, 128], "float16"), "S0": ("sbuf", [128, 128], "float16"), "WB": ("sbuf", [128, 128], "float16"),
+    "DLM": ("sbuf", [128, 128], "float16"), "SH1": ("sbuf", [128, 128], "float16"), "SH2": ("sbuf", [128, 128], "float16"),
+    "MK": ("sbuf", [128, 256], "float16"), "MB": ("sbuf", [128, 128], "float16"), "QH": ("sbuf", [128, 8], "float16"),
+    "QF": ("sbuf", [128, 8], "float32"), "QB": ("sbuf", [128, 8], "bfloat16"), "QBH": ("sbuf", [128, 8], "bfloat16"),
+    "Q8": ("sbuf", [128, 8], "bfloat16"), "R14": ("sbuf", [128, 128], "float32"), "ROW0": ("sbuf", [128, 128], "float16"),
+    "ROW1": ("sbuf", [128, 128], "float16"), "ONE": ("sbuf", [128, 128], "float16"), "C32": ("sbuf", [128, 128], "float16"),
+    "CU": ("sbuf", [128, 128], "float16"), "NF": ("sbuf", [128, 256], "float32"), "PB": ("sbuf", [128, 16], "int32"),
+    "PB0": ("sbuf", [128, 16], "int32"), "PLI": ("sbuf", [128, 16], "int32"), "PLA": ("sbuf", [128, 16], "int32"),
+    "PLB": ("sbuf", [128, 16], "int32"), "PL": ("sbuf", [128, 16], "uint16"),
+    "AI": ("sbuf", [128, 1], "int32"), "AJ": ("sbuf", [128, 1], "int32"),
+    "YKS": ("sbuf", [8, 1024], "float32"), "YOS": ("sbuf", [128, 256], "float32"),
+    "ZO": ("sbuf", [128, 256], "bfloat16"), "ZF": ("sbuf", [128, 256], "bfloat16"),
+    "EO": ("sbuf", [128, 256], "float32"), "EF": ("sbuf", [128, 256], "float32"),
+    "pU": ("psum", [128, 512], "float32"), "pZ0": ("psum", [128, 512], "float32"), "pZ1": ("psum", [128, 512], "float32"),
+    "pD0": ("psum", [128, 512], "float32"), "pD1": ("psum", [128, 512], "float32"), "pC": ("psum", [128, 512], "float32"),
+    "pR": ("psum", [128, 512], "float32"), "pW": ("psum", [128, 512], "float32"),
+    "MI": ("sbuf", [128, 2560], "float16"),
+    "MO": ("sbuf", [128, 2560], "float16"),
+}
+for _t in range(4):
+    SCRATCH["VI%d" % _t] = ("sbuf", [128, 512], "float16")
+    SCRATCH["TAB%d" % _t] = ("sbuf", [128, 512 + 256 * _t], "float32")
+    SCRATCH["NC%d" % _t] = ("sbuf", [128, 256], "float16")
+    SCRATCH["RUN%d" % _t] = ("sbuf", [128, 256], "bfloat16")
+    SCRATCH["KI%d" % _t] = ("sbuf", [128, 256], "bfloat16")
+ALIAS = {}
+for _c in range(2):
+    for _t in range(5):
+        ALIAS["MI%d%d" % (_t, _c)] = ("MI", 256 * (2 * _t + _c))
+        ALIAS["MO%d%d" % (_t, _c)] = ("MO", 256 * (2 * _t + _c))
+for _n, _w, _d in (("Y", 2048, "bfloat16"), ("B", 2048, "bfloat16"), ("HI", 2048, "bfloat16"), ("LO", 2048, "bfloat16"),
+                   ("U1", 128, "float32"), ("U2", 128, "bfloat16"), ("AT", 128, "int32"), ("AS", 128, "int32"), ("OF", 128, "uint16"),
+                   ("CM", 128, "bfloat16"), ("RN", 128, "bfloat16"), ("P", 128, "float16"), ("ZM", 256, "float16"), ("ZU", 128, "float32"),
+                   ("LS", 16, "uint16"), ("HG", 128, "float32"), ("SM", 128, "float32"), ("RY", 128, "int32"), ("RZ", 128, "int32"),
+                   ("ACC", 1, "float32"), ("C8", 128, "float16")):
+    SCRATCH[_n] = ("sbuf", [128, 2 * _w], _d)
+    for _c in range(2):
+        ALIAS["%s%d" % (_n, _c)] = (_n, _w * _c)
+
+SEMAPHORES = (["qg", "qt", "qv", "qs", "ls"] + ["d%d" % i for i in range(28)]
+              + ["m%d%d" % (t, c) for t in range(5) for c in range(2)] + ["v%d" % t for t in range(4)]
+              + ["h%d%d" % (t, c) for t in range(4) for c in range(2)] + ["y%d%d" % (t, c) for t in range(4) for c in range(2)] + ["w0", "w1", "z00", "z01", "e40", "e41"])
+
+
+def real(o):
+    if o[0] in ALIAS:
+        n, a = ALIAS[o[0]]
+        return (n, o[1] + a, o[2] + a) + tuple(o[3:])
+    return o
+
+
+def bits(m):
+    return bin(m).count("1")
+
+
+def relay_of(src, dst, n, near, topo):
+    if topo.may_write(src, dst):
+        return None
+    c = [x for x in topo.cores_of(src) if x != src and topo.may_write(x, dst)]
+    c = [x for x in c if (topo.die(x) == topo.die(src)) == near]
+    return c[n % len(c)]
+
+
+def messages(core, T, topo):
+    r = T.rank_of(core)
+    out = []
+
+    def add(sem, off, buf, a, b, n, near):
+        dst = T.cores[(r + off) % N]
+        buf, a, b = real((buf, a, b))
+        out.append((sem, dst, relay_of(core, dst, n, near, topo), buf, a, b))
+    for c in range(2):
+        add("z0%d" % c, 1, "MI0%d" % c, 0, 128, c, True)
+    for c in range(2):
+        add("m0%d" % c, 1, "MI0%d" % c, 128, 256, c, True)
+    add("v0", 1, "VI0", 0, 512, 0, False)
+    add("v1", 2, "VI1", 0, 512, 0, False)
+    add("v2", 3, "VI2", 0, 512, 1, False)
+    add("v3", 4, "VI3", 0, 512, 0, False)
+    for c in range(2):
+        add("h1%d" % c, 2, "HL1", 128 * c, 128 * c + 128, 0, False)
+        add("h0%d" % c, 4, "HL3", 128 * c, 128 * c + 128, 0, False)
+    for t in range(4):
+        for c in range(2):
+            if t < 3:
+                add("m%d%d" % (t + 1, c), 1, "MI%d%d" % (t + 1, c), 0, 256, c, True)
+            else:
+                add("m4%d" % c, -4, "ZF", 128 * c, 128 * c + 128, 0, True)
+                add("e4%d" % c, -4, "EF", 128 * c, 128 * c + 128, 0, True)
+            if t < 2:
+                add("h%d%d" % (t + 2, c), 2, "HB%d" % (t + 2), 128 * c, 128 * c + 128, 0, False)
+            if t == 3:
+                add("w%d" % c, -4, "L3I", 128 * c, 128 * c + 128, 0, False)
+            add("y%d%d" % (t, c), -1 - t, "KI%d" % t, 128 * c, 128 * c + 128, c, False)
+    return out
+
+
+def mask_of(src, dst, topo):
+    return sum(1 << x for x in topo.engines(src, dst)[:8])
+
+
+def hand_on(g, core, T, topo):
+    own = [x for x in topo.cores_of(core) if T.rank_of(x) is not None]
+    n = 0
+    for rc in own:
+        for sem, dst, rel, buf, a, b in messages(rc, T, topo):
+            if rel == core:
+                g.wait_ge(T.sem[sem], bits(mask_of(rc, core, topo)))
+                m = mask_of(core, dst, topo)
+                rid, pid = topo.addr(dst, core)
+                g.remote_dma(T[buf][:, a:b], T[buf][:, a:b], T.sem[sem], T.sem.ls, pid, rid, m)
+                n += bits(m)
+    if n:
+        g.wait_ge(T.sem.ls, n)
+
+
+def rank_program(g, core, T, topo):
+    rank = T.rank_of(core)
+    if rank is None:
+        hand_on(g, core, T, topo)
+        return
+    Q = {"g": g, "t": g.tensor, "v": g.vector, "s": g.scalar, "d": g.sync}
+    cnt = {"g": 0, "t": 0, "v": 0, "s": 0}
+    known = {q: {} for q in Q}
+    acc, bank, used = {}, {}, {}
+    state = {"d": 0, "ls": 0}
+
+    def need(q, tok):
+        sem, val, clk = tok
+        k = known[q]
+        if k.get(sem, 0) < val:
+            Q[q].wait_ge(T.sem[sem], val)
+            k[sem] = val
+        for s2 in clk:
+            if k.get(s2, 0) < clk[s2]:
+                k[s2] = clk[s2]
+
+    def deps(q, reads, writes):
+        toks = []
+        for w, lst in ((False, reads), (True, writes)):
+            for nm, lo, hi in lst:
+                if nm[0] == "p":
+                    for q2 in bank.get(nm, {}):
+                        if q2 != q:
+                            toks.append(bank[nm][q2])
+                    continue
+                for lo2, hi2, w2, q2, tok in acc.get(nm, []):
+                    if lo < hi2 and lo2 < hi and (w or w2) and not (q2 == q and w and not w2 and q in cnt):
+                        toks.append(tok)
+        best = {}
+        for tok in toks:
+            if tok[0] not in best or best[tok[0]][1] < tok[1]:
+                best[tok[0]] = tok
+        for tok in sorted(best.values(), key=lambda x: -len(x[2])):
+            need(q, tok)
+
+    def note(q, reads, writes, tok):
+        for w, lst in ((False, reads), (True, writes)):
+            for nm, lo, hi in lst:
+                if nm[0] == "p":
+                    bank.setdefault(nm, {})[q] = tok
+                    continue
+                l = acc.setdefault(nm, [])
+                if w:
+                    l[:] = [e for e in l if not (lo <= e[0] and e[1] <= hi)]
+                l.append((lo, hi, w, q, tok))
+
+    def op(q, fn, args, reads, writes):
+        deps(q, reads, writes)
+        fn(**args).then_inc(T.sem["q" + q], 1)
+        cnt[q] += 1
+        used["q" + q] = cnt[q]
+        note(q, reads, writes, ("q" + q, cnt[q], dict(known[q])))
+
+    def dma(q, out, in_, reads, writes):
+        deps(q, reads, writes)
+        s = "d%d" % state["d"]
+        state["d"] += 1
+        Q[q].dma_start(out, in_).then_inc(T.sem[s], 16)
+        used[s] = 16
+        note(q, reads, writes, (s, 16, dict(known[q])))
+
+    def arrives(sem, src_off, buf, a, b):
+        src = T.cores[(rank + src_off) % N]
+        for s2, dst, rel, bf, _a, _b in messages(src, T, topo):
+            if s2 == sem and dst == core:
+                v = bits(mask_of(rel if rel is not None else src, core, topo))
+                used[sem] = v
+                note("x", [], [real((buf, a, b))], (sem, v, {}))
+
+    plan = {m[0]: m for m in messages(core, T, topo)}
+
+    def send(sem, buf, a, b):
+        _, dst, rel, ob, oa, oe = plan[sem]
+        buf, a, b = real((buf, a, b))
+        deps("g", [(buf, a, b)], [])
+        to = dst if rel is None else rel
+        m = mask_of(core, to, topo)
+        rid, pid = topo.addr(to, core)
+        g.remote_dma(T[ob][:, oa:oe], T[buf][:, a:b], T.sem[sem], T.sem.ls, pid, rid, m)
+        state["ls"] += bits(m)
+
+    def ap(o):
+        o = real(o)
+        if len(o) == 4:
+            return T[o[0]][:, o[1]:o[2]:o[3]]
+        return T[o[0]][:, o[1]:o[2]]
+
+    def rg(o):
+        return real(o)[:3]
+
+    def ind(win, off):
+        return ap(win).indirect(ap(off))
+
+    def full(n, w=128):
+        return (n, 0, w)
+
+    def mm(out, l, r, start, stop):
+        op("t", g.tensor.matmul, dict(out=ap(out), lhsT=ap(l), rhs=ap(r), start=start, stop=stop), [rg(l), rg(r)], [rg(out)])
+
+    def mm1(out, l, r, start, stop):
+        op("t", g.tensor.matmul, dict(out=ap(out), lhsT=T[l[0]][0:1, l[1]:l[2]], rhs=T[r[0]][0:1, r[1]:r[2]], start=start, stop=stop), [rg(l), rg(r)], [rg(out)])
+
+    def tt(out, a, b, o):
+        op("v", g.vector.tensor_tensor, dict(out=ap(out), in0=ap(a), in1=ap(b), op=o), [rg(a), rg(b)], [rg(out)])
+
+    def tti(out, win, off, b, o):
+        op("v", g.vector.tensor_tensor, dict(out=ap(out), in0=ind(win, off), in1=ap(b), op=o), [rg(win), rg(off), rg(b)], [rg(out)])
+
+    def ts(out, a, s1, o1, s2=None, o2=None):
+        rd = [rg(a)]
+        sc = []
+        for s in (s1, s2):
+            if isinstance(s, tuple):
+                rd.append(rg(s))
+                sc.append(ap(s))
+            else:
+                sc.append(s)
+        d = dict(out=ap(out), in0=ap(a), scalar1=sc[0], scalar2=sc[1], op0=o1)
+        if o2 is not None:
+            d["op1"] = o2
+        op("v", g.vector.tensor_scalar, d, rd, [rg(out)])
+
+    def tc(out, a):
+        op("v", g.vector.tensor_copy, dict(out=ap(out), in_=ap(a)), [rg(a)], [rg(out)])
+
+    def ms(out, v):
+        op("v", g.vector.memset, dict(ap=ap(out), constant=v), [], [rg(out)])
+
+    def act(out, a, f, bias=None, scale=None, accum=None):
+        d = dict(out=ap(out), in_=ap(a), func=f)
+        wr = [rg(out)]
+        if bias is not None:
+            d["bias"] = bias
+        if scale is not None:
+            d["scale"] = scale
+        if accum is not None:
+            d["accum_out"] = ap(accum)
+            wr.append(rg(accum))
+        op("s", g.scalar.activation, d, [rg(a)], wr)
+
+    def acti(out, win, off, f, bias=None, scale=None):
+        d = dict(out=ap(out), in_=ind(win, off), func=f)
+        if bias is not None:
+            d["bias"] = bias
+        if scale is not None:
+            d["scale"] = scale
+        op("s", g.scalar.activation, d, [rg(win), rg(off)], [rg(out)])
+
+    dma("d", T.VP32[:], T.vp[:], [], [("VP32", 0, 512)])
+    dma("s", T.MV32[:], T.mv[:], [], [("MV32", 0, 16)])
+    dma("s", T.Z0B[:], T.z0[:], [], [("Z0B", 0, 256)])
+    dma("s", T.WT32[:], T.wt[:], [], [("WT32", 0, 1)])
+    dma("d", T.RT[:, 0:4096], T.strat[:], [], [("RT", 0, 4096)])
+
+    big = dict(allow_small_or_imprecise_dtypes=True)
+    op("g", g.iota, dict(out=T.PI[:], pattern=[[0, 1]], base=0, channel_multiplier=1), [], [("PI", 0, 1)])
+    op("g", g.iota, dict(out=T.JI[:], pattern=[[1, 128]], base=0, channel_multiplier=0), [], [("JI", 0, 128)])
+    op("g", g.iota, dict(out=T.DIF[:], pattern=[[1, 128]], base=0, channel_multiplier=-1, **big), [], [("DIF", 0, 128)])
+    op("g", g.iota, dict(out=T.PB0[:], pattern=[[0, 2], [256, 8]], base=0, channel_multiplier=0), [], [("PB0", 0, 16)])
+    op("g", g.iota, dict(out=T.NF[:], pattern=[[1, 256]], base=512, channel_multiplier=0, **big), [], [("NF", 0, 256)])
+
+    GP, KK, P16, K0, K14, KL, K37, E16, AK = [("COL", i, i + 1) for i in range(9)]
+    ts(full("PG", 1), full("PI", 1), 4, A.arith_shift_right)
+    ts(full("PK", 1), full("PI", 1), 15, A.bitwise_and)
+    ts(full("JS"), full("JI"), 4, A.arith_shift_right)
+    tc(GP, full("PG", 1))
+    tc(KK, full("PK", 1))
+    ts(K37, KK, 37.0, A.mult)
+    ts(full("BLK"), full("JS"), GP, A.is_equal)
+    ts(full("IH"), full("DIF"), 0.0, A.is_equal, 0.5, A.mult)
+    ts(full("T1"), full("BLK"), 1000.0, A.mult, 1000.0, A.subtract)
+    ms(full("ONE"), 1.0)
+    ms(full("C32"), 0.25)
+    tt(full("DB"), full("DIF"), full("T1"), A.add)
+    op("v", g.vector.memset, dict(ap=T.CU[0:64, :], constant=-32.0), [], [("CU", 0, 64)])
+    op("v", g.vector.memset, dict(ap=T.CU[64:128, :], constant=0.0078125), [], [("CU", 64, 128)])
+    ts(full("T0"), full("DB"), -1.0, A.is_equal)
+    ts(full("IB"), full("DIF"), 0.0, A.is_equal)
+
+    tc(full("MV16", 16), full("MV32", 16))
+    for c in range(2):
+        mo = "MO0%d" % c
+        tc((mo, 0, 128), ("Z0B", 128 * c, 128 * c + 128))
+        if c == 0:
+            send("z00", mo, 0, 128)
+    for c in range(2):
+        mo, off = "MO0%d" % c, ("MV16", 8 * c, 8 * c + 8)
+        op("v", g.vector.tensor_copy, dict(out=ap((mo, 128, 256)), in_=ind(("VP32", 0, 512), off)), [("VP32", 0, 512), off], [rg((mo, 128, 256))])
+        send("m0%d" % c, mo, 128, 256)
+        if c == 0:
+            send("z01", "MO01", 0, 128)
+    dma("d", T.VO32[:], T.vo[:], [("MO", 384, 512)], [("VO32", 0, 512)])
+    tt(full("DLM"), full("T0"), full("IB"), A.subtract)
+    ts(full("NIB"), full("DIF"), 0.0, A.is_equal, -1.0, A.mult)
+    tc(full("WTF", 1), full("WT32", 1))
+    ts(full("WB"), full("BLK"), full("WTF", 1), A.mult)
+    ms(full("MX", 2048), 1.0)
+    op("v", g.vector.memset, dict(ap=T.MX[:, 0:2048:16], constant=0.0), [], [("MX", 0, 2048)])
+    act(full("MN", 2048), full("MX", 2048), F.Identity, bias=512.0, scale=-512.0)
+    act(("RT", 4096, RW), ("RT", 0, RW - 4096), F.Copy)
+    tc(full("PV", 512), full("VP32", 512))
+
+    def const_a():
+        ts(full("NH"), full("DIF"), 0.0, A.is_equal, -0.5, A.mult)
+        ts(full("JM"), full("JI"), 15, A.bitwise_and)
+        ts(full("QB", 8), ("JI", 0, 8), GP, A.is_equal)
+        ts(full("QBH", 8), ("JI", 0, 8), GP, A.is_equal, 0.5, A.mult)
+        for c in range(2):
+            ts(full("C8%d" % c), full("JM"), KS[c] - 0.5, A.is_gt, 0.0625, A.mult)
+        ts(KL, KK, 15.0, A.is_lt)
+        ts(K0, KK, 0.0, A.is_equal)
+        ts(P16, full("PI", 1), 16.0, A.mult)
+        ts(K14, KK, 14.0, A.is_equal)
+        ts(E16, KK, 16.0, A.mult)
+        ts(full("B14"), full("BLK"), KL, A.mult)
+
+    def const_b():
+        ts(full("SH1"), full("DB"), 1.0, A.is_equal)
+        ts(full("BF"), full("BLK"), KL, A.mult)
+        ts(full("S0"), full("BLK"), K0, A.mult)
+        for i in range(2):
+            ts(("MK", 128 * i, 128 * i + 128), full("JM"), KK, A.is_equal)
+        ts(full("QF", 8), ("JI", 0, 8), GP, A.is_equal)
+        ts(full("QH", 8), ("JI", 0, 8), GP, A.is_equal)
+        ts(full("MB"), ("MK", 0, 128), P16, A.mult)
+        ts(full("NC0", 256), full("NF", 256), 0.0, A.add, K0, A.mult)
+        ts(full("PB", 16), full("PB0", 16), E16, A.add)
+
+    def const_c():
+        for t in range(1, 4):
+            ts(full("NC%d" % t, 256), full("NF", 256), 256.0 * t, A.add, K0, A.mult)
+        ts(full("SH2"), full("DB"), 2.0, A.is_equal)
+        ts(full("R14"), full("DIF"), 0.0, A.mult, K14, A.add)
+        ts(full("ROW1"), full("JM"), 1.0, A.is_equal)
+
+    def const_d():
+        ts(full("ROW0"), full("JM"), 0.0, A.is_equal)
+        ts(full("Q8", 8), ("JI", 0, 8), GP, A.is_equal, KL, A.mult)
+
+    for t in range(4):
+        for c in range(2):
+            arrives("m%d%d" % (t, c), -1, "MI%d%d" % (t, c), 0 if t else 128, 256)
+            arrives("y%d%d" % (t, c), 1 + t, "KI%d" % t, 128 * c, 128 * c + 128)
+            if t == 1:
+                arrives("h1%d" % c, -2, "HL1", 128 * c, 128 * c + 128)
+            if t >= 2:
+                arrives("h%d%d" % (t, c), -2, "HB%d" % t, 128 * c, 128 * c + 128)
+        arrives("v%d" % t, -1 - t, "VI%d" % t, 0, 512)
+    for c in range(2):
+        arrives("h0%d" % c, -4, "HL3", 128 * c, 128 * c + 128)
+        arrives("w%d" % c, 4, "L3I", 128 * c, 128 * c + 128)
+        arrives("z0%d" % c, -1, "MI0%d" % c, 0, 128)
+        arrives("m4%d" % c, 4, "ZF", 128 * c, 128 * c + 128)
+        arrives("e4%d" % c, 4, "EF", 128 * c, 128 * c + 128)
+
+    def pre_u(t, c):
+        z, l, pz = ("MI%d%d" % (t, c), 0, 128), ("MI%d%d" % (t, c), 128, 256), "pZ%d" % c
+        u, um = ("pU", 0, 128), ("pU", 128, 256)
+        mm(u, full("WB"), z, True, False)
+        mm(u, full("CU"), full("ONE"), False, True)
+        act(full("U1%d" % c), u, F.Identity, bias=M35)
+        act(full("U2%d" % c), full("U1%d" % c), F.Identity, bias=-M35)
+        mm((pz, 0, 128), full("IH"), z, True, True)
+        mm((pz, 128, 256), full("DLM"), l, True, True)
+        mm(um, full("WB"), z, True, False)
+        mm(um, full("C32"), full("ONE"), False, False)
+        mm(um, full("NIB"), full("U2%d" % c), False, True)
+        if t < TURNS - 1:
+            mm((pz, 256, 384), z, full("WB"), True, True)
+
+    def offs(t, c):
+        ts(full("OF%d" % c), full("AS%d" % c), K37 if t == 0 else AK, A.add)
+
+    def place_u(t, c):
+        if t < TURNS - 1:
+            tt(full("ZU%d" % c), ("pZ%d" % c, 256, 384), ("MK", 0, 128), A.mult)
+            mm(("pU", 400 + 8 * c, 408 + 8 * c), full("ZU%d" % c), full("QF", 8), True, True)
+
+    def place_steps():
+        return [lambda: tc(full("PLI", 16), ("pU", 400, 416)), lambda: ts(full("PLA", 16), full("PLI", 16), 15, A.bitwise_and),
+                lambda: tt(full("PLB", 16), full("PLA", 16), full("PB", 16), A.add), lambda: tc(full("PL", 16), full("PLB", 16))]
+
+    def gather(c, a, b, q):
+        if a >= b:
+            return
+        y, of, w = ("Y%d" % c, 16 * a, 16 * b), ("OF%d" % c, a, b), ("RT", 0, RW)
+        if q == "s":
+            acti(y, w, of, F.Copy, scale=0.5)
+        else:
+            op("v", g.vector.tensor_scalar, dict(out=ap(y), in0=ind(w, of), scalar1=0.5, scalar2=None, op0=A.mult), [w, rg(of)], [rg(y)])
+
+    def compare_s(t, c):
+        y, b, z = "Y%d" % c, "B%d" % c, ("MI%d%d" % (t, c), 0, 128)
+        for i, k0 in enumerate(range(KS[c], 16, 4)):
+            k1 = min(k0 + 4, 16)
+            pd = "pD%d" % (i % 2)
+            for k in range(k0, k1):
+                o = (pd, 128 * (k - k0), 128 * (k - k0) + 128)
+                mm(o, full("IB"), (y, k, 2048, 16), True, False)
+                mm(o, full("NH"), z, False, True)
+            act((b, 128 * k0, 128 * k1), (pd, 0, 128 * (k1 - k0)), F.Sign, bias=-0.25)
+
+    def compare_v(t, c):
+        for k in range(KS[c]):
+            tt(("B%d" % c, 128 * k, 128 * k + 128), ("Y%d" % c, k, 2048, 16), ("pZ%d" % c, 0, 128), A.is_gt)
+
+    def beats(c):
+        mm(("pC", 0, 128), full("ONE"), full("C8%d" % c), True, False)
+        for k in range(16):
+            mm(("pC", k, 128, 16), ("B%d" % c, 128 * k, 128 * k + 128), full("QB" if k < KS[c] else "QBH", 8), False, k == 15)
+
+    def scan(c, hi):
+        o, y = full(("HI%d" if hi else "LO%d") % c, 2048), full("Y%d" % c, 2048)
+        m = full("MX" if hi else "MN", 2048)
+        op("v", g.vector.tensor_tensor_scan, dict(out=ap(o), data0=ap(m), data1=ap(y), initial=0.0,
+                                                  op0=A.mult if hi else A.add, op1=A.max if hi else A.min), [m, rg(y)], [rg(o)])
+
+    def verdict_v(c):
+        o, m = full("CM%d" % c), full("MX")
+        op("v", g.vector.tensor_tensor_scan, dict(out=ap(o), data0=ap(m), data1=ap(("pC", 0, 128)), initial=0.0, op0=A.mult, op1=A.max),
+           [m, ("pC", 0, 128)], [rg(o)])
+        ts(full("RN%d" % c), o, 10.5, A.is_lt)
+        mm(("pC", 128, 256), full("RN%d" % c), full("IB"), True, True)
+
+    def verdict_s(t, c):
+        run = ("RUN%d" % t, 128 * c, 128 * c + 128)
+        act(run, ("pC", 128, 256), F.Copy, accum=full("ACC%d" % c, 1))
+        mm(("pR", 128, 256), run, full("B14"), True, True)
+
+    def named(t, c):
+        run = ("RUN%d" % t, 128 * c, 128 * c + 128)
+        tt(full("P%d" % c), run, ("pZ%d" % c, 128, 256), A.mult)
+        mm(("pR", 0, 128), ("MI%d%d" % (t, c), 128, 256), full("S0"), True, False)
+        mm(("pR", 0, 128), full("P%d" % c), full("BF"), False, True)
+
+    def lists(t, c):
+        zm = "ZM%d" % c
+        tt(full(zm, 256), ("pR", 0, 256), full("MK", 256), A.mult)
+        mm(("pR", 256, 264), (zm, 0, 128), full("QH", 8), True, True)
+        mm(("pR", 264, 272), (zm, 128, 256), full("QH", 8), True, False)
+        mm(("pR", 264, 272), full("MB"), full("QH", 8), False, True)
+
+    def lists_out(t, c):
+        tc(full("LS%d" % c, 16), ("pR", 256, 272))
+
+    def select_hi(t, c):
+        acti(full("HG%d" % c), full("HI%d" % c, 2048), ("LS%d" % c, 8, 16), F.Identity, bias=-0.25)
+
+    def select_steps(t, c):
+        kap, nam = ("LS%d" % c, 8, 16), ("LS%d" % c, 0, 8)
+        mo = "MO%d%d" % (t + 1, c)
+        half = (128 * c, 128 * c + 128)
+        z, l = ((mo, 0, 128), (mo, 128, 256)) if t < TURNS - 1 else (("ZO",) + half, ("EO",) + half)
+
+        def views():
+            tti(l, full("TAB%d" % t, 512 + 256 * t), nam, ("NC%d" % t,) + half, A.add)
+            if t == TURNS - 1:
+                send("e4%d" % c, *l)
+
+        def out():
+            ts(z, full("SM%d" % c), M23, A.add, M23, A.subtract)
+            if t == TURNS - 1:
+                send("m4%d" % c, *z)
+                return
+            send("m%d%d" % (t + 1, c), mo, 0, 256)
+            if t < 2:
+                send("h%d%d" % (t + 2, c), *l)
+        return [views, lambda: tti(full("SM%d" % c), full("LO%d" % c, 2048), kap, full("HG%d" % c), A.add), out]
+
+    def update_steps(t, c):
+        win, off = ("RT", 2048 * c, 2048 * c + 2048), ("PL", 8 * c, 8 * c + 8)
+
+        def out():
+            op("v", g.vector.tensor_copy, dict(out=ind(win, off), in_=ap(full("RZ%d" % c))), [off, rg(full("RZ%d" % c))], [win])
+            if c == 0:
+                act(("RT", 4096, RW), ("RT", 0, RW - 4096), F.Copy)
+        return [lambda: tti(full("RY%d" % c), win, off, ("MO%d%d" % (t + 1, c), 0, 128), A.add),
+                lambda: ts(full("RZ%d" % c), full("RY%d" % c), 1, A.arith_shift_right), out]
+
+    def count_t():
+        for c in range(2):
+            mm(("pC", 256, 257), full("R14"), full("ACC%d" % c, 1), c == 0, c == 1)
+
+    def count_steps():
+        return [lambda: ts(full("AI", 1), ("pC", 256, 257), -1.0, A.mult), lambda: ts(full("AJ", 1), full("AI", 1), 255, A.bitwise_and),
+                lambda: ts(AK, full("AJ", 1), K37, A.add)]
+
+    def pre_steps(t, c):
+        return [lambda: tt(full("AT%d" % c), ("MI%d%d" % (t, c), 128, 256), ("pU", 128, 256), A.mult),
+                lambda: ts(full("AS%d" % c), full("AT%d" % c), 5, A.arith_shift_right, 4095, A.bitwise_and), lambda: offs(t, c)]
+
+    def pre_v(t, c):
+        for f in pre_steps(t, c)[:2]:
+            f()
+
+    def select(t, c):
+        for f in select_steps(t, c):
+            f()
+
+    parts = {(0, 0): [(0, 0, "VI0", 1, 0)], (0, 1): [(1, 0, "VI1", 1, 0)], (1, 0): [(1, 512, "HL1", 2, 0), (3, 512, "HL3", 2, 0)],
+             (1, 1): [(2, 0, "VI2", 1, 0)], (2, 0): [(2, 512, "HB2", 1, 0), (2, 768, "HB2", 2, 1)], (2, 1): [(3, 0, "VI3", 1, 0)],
+             (3, 0): [(3, 768, "HB3", 1, 0), (3, 1024, "HB3", 2, 2)]}
+
+    def table_t(key):
+        a = 0
+        for tb, c0, src, sh, n in parts.get(key, []):
+            wd = 512 if src[0] == "V" else 256
+            w = ("pW", a, a + wd)
+            mm(w, full("SH%d" % sh), full(src, wd), True, sh == 1)
+            if sh == 2:
+                mm1(w, full("ROW1"), full("NC%d" % n, 256), False, True)
+            a += wd
+
+    def table_s(key):
+        a = 0
+        for tb, c0, src, sh, n in parts.get(key, []):
+            wd = 512 if src[0] == "V" else 256
+            act(("TAB%d" % tb, c0, c0 + wd), ("pW", a, a + wd), F.Copy)
+            a += wd
+
+    def run_out(t, c):
+        send("y%d%d" % (t, c), "RUN%d" % t, 128 * c, 128 * c + 128)
+
+    def turn(t):
+        last = t == TURNS - 1
+        gather(0, 0, GS[0], "s")
+        gather(0, GS[0], H, "v")
+        compare_s(t, 0)
+        pre_u(t, 1)
+        compare_v(t, 0)
+        beats(0)
+        scan(0, True)
+        scan(0, False)
+        pre_v(t, 1)
+        offs(t, 1)
+        gather(1, 0, CUTS[0], "s")
+        gather(1, GS[1], H, "v")
+        table_t((t, 0))
+        verdict_v(0)
+        place_u(t, 0)
+        verdict_s(t, 0)
+        named(t, 0)
+        gather(1, CUTS[0], CUTS[1], "s")
+        table_s((t, 0))
+        lists(t, 0)
+        place_u(t, 1)
+        lists_out(t, 0)
+        select_hi(t, 0)
+        gather(1, CUTS[1], GS[1], "s")
+        select(t, 0)
+        run_out(t, 0)
+        if last:
+            for c in range(2):
+                send("w%d" % c, "MI3%d" % c, 128, 256)
+        compare_s(t, 1)
+        compare_v(t, 1)
+        beats(1)
+        table_t((t, 1))
+        scan(1, True)
+        scan(1, False)
+        verdict_v(1)
+        verdict_s(t, 1)
+        pl = [] if last else place_steps()
+        for f in pl[:2]:
+            f()
+        named(t, 1)
+        table_s((t, 1))
+        for f in pl[2:]:
+            f()
+        lists(t, 1)
+        if not last:
+            u0 = update_steps(t, 0)
+            u0[0]()
+            u0[1]()
+        lists_out(t, 1)
+        select_hi(t, 1)
+        if last:
+            run_out(t, 1)
+            select(t, 1)
+            return
+        count_t()
+        pre_u(t + 1, 0)
+        z = select_steps(t, 1)
+        u = update_steps(t, 1)
+        n = count_steps()
+        for f in (z[0], n[0], z[1], n[1], z[2], n[2], u0[2], u[0]):
+            f()
+        p = pre_steps(t + 1, 0)
+        for f in (p[0], u[1], p[1], u[2], p[2]):
+            f()
+        run_out(t, 1)
+
+    const_a()
+    const_b()
+    tc(full("OV", 512), full("VO32", 512))
+    send("v0", "OV", 0, 512)
+    send("v1", "PV", 0, 512)
+    for c in range(2):
+        send("h1%d" % c, "MO0%d" % c, 128, 256)
+    send("v2", "OV", 0, 512)
+    send("v3", "PV", 0, 512)
+    for c in range(2):
+        send("h0%d" % c, "MO0%d" % c, 128, 256)
+    const_c()
+    const_d()
+    pre_u(0, 0)
+    pre_v(0, 0)
+    offs(0, 0)
+    for t in range(TURNS):
+        turn(t)
+
+    for t in range(TURNS):
+        w = T.pW[0:8, 0:256]
+        op("t", g.tensor.matmul, dict(out=w, lhsT=T.Q8[:], rhs=T["KI%d" % t][:], start=True, stop=True),
+           [full("Q8", 8), full("KI%d" % t, 256)], [("pW", 0, 256)])
+        op("s", g.scalar.activation, dict(out=T.YKS[:, 256 * t:256 * t + 256], in_=w, func=F.Copy), [("pW", 0, 256)], [("YKS", 256 * t, 256 * t + 256)])
+        if t == 2:
+            dma("d", T.yk[:, 0:768], T.YKS[:, 0:768], [("YKS", 0, 768)], [("yk", 0, 768)])
+            mm(("pC", 0, 256), full("SH1"), full("L3I", 256), True, False)
+            mm1(("pC", 0, 256), full("ROW0"), full("NC3", 256), False, True)
+            act(full("YOS", 256), ("pC", 0, 256), F.Copy)
+            dma("d", T.yo[:], T.YOS[:], [full("YOS", 256)], [("yo", 0, 256)])
+    dma("d", T.yk[:, 768:1024], T.YKS[:, 768:1024], [("YKS", 768, 1024)], [("yk", 768, 1024)])
+    for c in range(2):
+        a, b = 128 * c, 128 * c + 128
+        dma("d", T.yp[:, a:b], T.EF[:, a:b], [("EF", a, b)], [("yp", a, b)])
+        dma("s", T.yz[:, a:b], T.ZF[:, a:b], [("ZF", a, b)], [("yz", a, b)])
+    used["ls"] = state["ls"]
+    for s in sorted(used):
+        if known["g"].get(s, 0) < used[s]:
+            g.wait_ge(T.sem[s], used[s])

@@ -3,9 +3,10 @@ from concourse.mybir import AluOpType as A, ActivationFunctionType as F
 N, TURNS, H = 8, 4, 128
 RW = 4096 + 816
 GS = (64, 96)
-CUTS = (56, 96)
-KS = (9, 7)
-M35, M23 = 1.5 * 2.0 ** 35, 1.5 * 2.0 ** 23
+KS = (6, 6)
+FIRST = 2
+M31, M27, M23 = 1.5 * 2.0 ** 31, 1.5 * 2.0 ** 27, 1.5 * 2.0 ** 23
+BIG = 2.0 ** 17
 
 SCRATCH = {
     "RT": ("sbuf", [128, RW], "bfloat16"),
@@ -19,51 +20,51 @@ SCRATCH = {
     "DIF": ("sbuf", [128, 128], "float32"), "DB": ("sbuf", [128, 128], "float32"), "JI": ("sbuf", [128, 128], "int32"),
     "JS": ("sbuf", [128, 128], "int32"), "JM": ("sbuf", [128, 128], "int32"), "PI": ("sbuf", [128, 1], "int32"),
     "PG": ("sbuf", [128, 1], "int32"), "PK": ("sbuf", [128, 1], "int32"), "COL": ("sbuf", [128, 16], "float32"),
-    "BLK": ("sbuf", [128, 128], "bfloat16"), "T0": ("sbuf", [128, 128], "bfloat16"), "T1": ("sbuf", [128, 128], "bfloat16"),
-    "IB": ("sbuf", [128, 128], "bfloat16"), "NIB": ("sbuf", [128, 128], "bfloat16"), "IH": ("sbuf", [128, 128], "float16"),
-    "NH": ("sbuf", [128, 128], "float16"), "B14": ("sbuf", [128, 128], "bfloat16"),
-    "BF": ("sbuf", [128, 128], "float16"), "S0": ("sbuf", [128, 128], "float16"), "WB": ("sbuf", [128, 128], "float16"),
-    "DLM": ("sbuf", [128, 128], "float16"), "SH1": ("sbuf", [128, 128], "float16"), "SH2": ("sbuf", [128, 128], "float16"),
-    "MK": ("sbuf", [128, 256], "float16"), "MB": ("sbuf", [128, 128], "float16"), "QH": ("sbuf", [128, 8], "float16"),
-    "QF": ("sbuf", [128, 8], "float32"), "QB": ("sbuf", [128, 8], "bfloat16"), "QBH": ("sbuf", [128, 8], "bfloat16"),
-    "Q8": ("sbuf", [128, 8], "bfloat16"), "R14": ("sbuf", [128, 128], "float32"), "ROW0": ("sbuf", [128, 128], "float16"),
-    "ROW1": ("sbuf", [128, 128], "float16"), "ONE": ("sbuf", [128, 128], "float16"), "C32": ("sbuf", [128, 128], "float16"),
-    "CU": ("sbuf", [128, 128], "float16"), "NF": ("sbuf", [128, 256], "float32"), "PB": ("sbuf", [128, 16], "int32"),
-    "PB0": ("sbuf", [128, 16], "int32"), "PLI": ("sbuf", [128, 16], "int32"), "PLA": ("sbuf", [128, 16], "int32"),
-    "PLB": ("sbuf", [128, 16], "int32"), "PL": ("sbuf", [128, 16], "uint16"),
-    "AI": ("sbuf", [128, 1], "int32"), "AJ": ("sbuf", [128, 1], "int32"),
+    "BLK": ("sbuf", [128, 128], "bfloat16"), "T1": ("sbuf", [128, 128], "bfloat16"), "EPI": ("sbuf", [128, 128], "float32"),
+    "IB": ("sbuf", [128, 128], "bfloat16"), "I4": ("sbuf", [128, 128], "bfloat16"), "IH": ("sbuf", [128, 128], "float16"),
+    "NH": ("sbuf", [128, 128], "float16"), "NI4": ("sbuf", [128, 128], "float16"), "NIF": ("sbuf", [128, 128], "float32"),
+    "WB": ("sbuf", [128, 128], "float16"), "REV": ("sbuf", [128, 128], "float16"), "KC": ("sbuf", [128, 128], "float16"),
+    "SH1": ("sbuf", [128, 128], "float16"), "SH2": ("sbuf", [128, 128], "float16"), "EP": ("sbuf", [128, 128], "bfloat16"),
+    "MK": ("sbuf", [128, 128], "float32"), "NM": ("sbuf", [128, 128], "bfloat16"),
+    "QF": ("sbuf", [128, 32], "float32"), "QB": ("sbuf", [128, 8], "bfloat16"), "QBH": ("sbuf", [128, 8], "bfloat16"),
+    "RC": ("sbuf", [128, 24], "float16"), "PC": ("sbuf", [128, 16], "float16"), "CA": ("sbuf", [128, 2], "float16"),
+    "H5": ("sbuf", [128, 128], "float32"), "ROW0": ("sbuf", [128, 128], "float16"), "ROW1": ("sbuf", [128, 128], "float16"),
+    "ONE": ("sbuf", [128, 128], "float16"), "ONB": ("sbuf", [128, 128], "bfloat16"), "CB": ("sbuf", [128, 128], "bfloat16"),
+    "C5": ("sbuf", [128, 128], "float16"), "C10": ("sbuf", [128, 128], "float16"),
+    "NF": ("sbuf", [128, 256], "float32"), "NC": ("sbuf", [128, 1024], "float16"),
+    "ELI": ("sbuf", [128, 8], "int32"), "EL": ("sbuf", [128, 8], "uint16"),
+    "RR": ("sbuf", [128, 32], "float32"), "PL": ("sbuf", [128, 16], "uint16"),
+    "SG": ("sbuf", [128, 16], "bfloat16"), "ACC": ("sbuf", [128, 1], "float32"),
     "YKS": ("sbuf", [8, 1024], "float32"), "YOS": ("sbuf", [128, 256], "float32"),
-    "ZO": ("sbuf", [128, 256], "bfloat16"), "ZF": ("sbuf", [128, 256], "bfloat16"),
+    "KO": ("sbuf", [128, 64], "bfloat16"), "KI": ("sbuf", [128, 64], "bfloat16"),
+    "ZL": ("sbuf", [128, 256], "bfloat16"), "ZF": ("sbuf", [128, 256], "bfloat16"),
     "EO": ("sbuf", [128, 256], "float32"), "EF": ("sbuf", [128, 256], "float32"),
-    "pU": ("psum", [128, 512], "float32"), "pZ0": ("psum", [128, 512], "float32"), "pZ1": ("psum", [128, 512], "float32"),
-    "pD0": ("psum", [128, 512], "float32"), "pD1": ("psum", [128, 512], "float32"), "pC": ("psum", [128, 512], "float32"),
-    "pR": ("psum", [128, 512], "float32"), "pW": ("psum", [128, 512], "float32"),
-    "MI": ("sbuf", [128, 2560], "float16"),
-    "MO": ("sbuf", [128, 2560], "float16"),
+    "ZI": ("sbuf", [128, 1024], "float16"), "LI": ("sbuf", [128, 1024], "float16"),
+    "ZO": ("sbuf", [128, 1280], "float16"), "LU": ("sbuf", [128, 1024], "float16"),
 }
+for _n in ("pU", "pZ", "pD0", "pD1", "pC", "pR", "pW", "pX"):
+    SCRATCH[_n] = ("psum", [128, 512], "float32")
 for _t in range(4):
     SCRATCH["VI%d" % _t] = ("sbuf", [128, 512], "float16")
     SCRATCH["TAB%d" % _t] = ("sbuf", [128, 512 + 256 * _t], "float32")
-    SCRATCH["NC%d" % _t] = ("sbuf", [128, 256], "float16")
-    SCRATCH["RUN%d" % _t] = ("sbuf", [128, 256], "bfloat16")
-    SCRATCH["KI%d" % _t] = ("sbuf", [128, 256], "bfloat16")
 ALIAS = {}
-for _c in range(2):
-    for _t in range(5):
-        ALIAS["MI%d%d" % (_t, _c)] = ("MI", 256 * (2 * _t + _c))
-        ALIAS["MO%d%d" % (_t, _c)] = ("MO", 256 * (2 * _t + _c))
+for _t in range(5):
+    ALIAS["NC%d" % _t] = ("NC", 256 * _t)
+    for _c in range(2):
+        for _n in ("ZI", "LI", "ZO", "LU"):
+            ALIAS["%s%d%d" % (_n, _t, _c)] = (_n, 256 * _t + 128 * _c)
 for _n, _w, _d in (("Y", 2048, "bfloat16"), ("B", 2048, "bfloat16"), ("HI", 2048, "bfloat16"), ("LO", 2048, "bfloat16"),
-                   ("U1", 128, "float32"), ("U2", 128, "bfloat16"), ("AT", 128, "int32"), ("AS", 128, "int32"), ("OF", 128, "uint16"),
-                   ("CM", 128, "bfloat16"), ("RN", 128, "bfloat16"), ("P", 128, "float16"), ("ZM", 256, "float16"), ("ZU", 128, "float32"),
-                   ("LS", 16, "uint16"), ("HG", 128, "float32"), ("SM", 128, "float32"), ("RY", 128, "int32"), ("RZ", 128, "int32"),
-                   ("ACC", 1, "float32"), ("C8", 128, "float16")):
+                   ("U2", 128, "float16"), ("AT", 128, "int32"), ("AS", 128, "int32"), ("OF", 128, "uint16"),
+                   ("BT", 128, "float32"), ("PS", 128, "float32"), ("KX", 128, "float32"), ("ZU", 128, "float32"),
+                   ("LK", 8, "uint16"), ("LN", 8, "uint16"), ("HG", 128, "float32"), ("OLD", 128, "float16"), ("RZ", 128, "int32"),
+                   ("C8", 128, "float16")):
     SCRATCH[_n] = ("sbuf", [128, 2 * _w], _d)
     for _c in range(2):
         ALIAS["%s%d" % (_n, _c)] = (_n, _w * _c)
 
 SEMAPHORES = (["qg", "qt", "qv", "qs", "ls"] + ["d%d" % i for i in range(28)]
-              + ["m%d%d" % (t, c) for t in range(5) for c in range(2)] + ["v%d" % t for t in range(4)]
-              + ["h%d%d" % (t, c) for t in range(4) for c in range(2)] + ["y%d%d" % (t, c) for t in range(4) for c in range(2)] + ["w0", "w1", "z00", "z01", "e40", "e41"])
+              + ["%s%d%d" % (n, t, c) for n in "zl" for t in range(5) for c in range(2)] + ["v%d" % t for t in range(4)]
+              + ["h%d" % t for t in range(4)] + ["y0", "y1", "y2", "y30", "y31", "w"])
 
 
 def real(o):
@@ -92,45 +93,47 @@ def messages(core, T, topo):
     def add(sem, off, buf, a, b, n, near):
         dst = T.cores[(r + off) % N]
         buf, a, b = real((buf, a, b))
-        out.append((sem, dst, relay_of(core, dst, n, near, topo), buf, a, b))
+        out.append((sem, dst, relay_of(core, dst, n, near, topo), buf, a, b, n))
     for c in range(2):
-        add("z0%d" % c, 1, "MI0%d" % c, 0, 128, c, True)
-    for c in range(2):
-        add("m0%d" % c, 1, "MI0%d" % c, 128, 256, c, True)
+        add("z0%d" % c, 1, "ZI0%d" % c, 0, 128, 0, True)
+        add("l0%d" % c, 1, "LI0%d" % c, 0, 128, 1, True)
     add("v0", 1, "VI0", 0, 512, 0, False)
     add("v1", 2, "VI1", 0, 512, 0, False)
     add("v2", 3, "VI2", 0, 512, 1, False)
     add("v3", 4, "VI3", 0, 512, 0, False)
-    for c in range(2):
-        add("h1%d" % c, 2, "HL1", 128 * c, 128 * c + 128, 0, False)
-        add("h0%d" % c, 4, "HL3", 128 * c, 128 * c + 128, 0, False)
+    add("h1", 2, "HL1", 0, 256, 0, False)
+    add("h0", 4, "HL3", 0, 256, 0, False)
     for t in range(4):
         for c in range(2):
             if t < 3:
-                add("m%d%d" % (t + 1, c), 1, "MI%d%d" % (t + 1, c), 0, 256, c, True)
+                add("z%d%d" % (t + 1, c), 1, "ZI%d%d" % (t + 1, c), 0, 128, 0, True)
+                add("l%d%d" % (t + 1, c), 1, "LI%d%d" % (t + 1, c), 0, 128, 1, True)
             else:
-                add("m4%d" % c, -4, "ZF", 128 * c, 128 * c + 128, 0, True)
-                add("e4%d" % c, -4, "EF", 128 * c, 128 * c + 128, 0, True)
-            if t < 2:
-                add("h%d%d" % (t + 2, c), 2, "HB%d" % (t + 2), 128 * c, 128 * c + 128, 0, False)
-            if t == 3:
-                add("w%d" % c, -4, "L3I", 128 * c, 128 * c + 128, 0, False)
-            add("y%d%d" % (t, c), -1 - t, "KI%d" % t, 128 * c, 128 * c + 128, c, False)
+                add("z4%d" % c, -4, "ZF", 128 * c, 128 * c + 128, 0, True)
+                add("l4%d" % c, -4, "EF", 128 * c, 128 * c + 128, 0, True)
+                add("y3%d" % c, -4, "KI", 48 + 8 * c, 56 + 8 * c, 0, False)
+        if t < 2:
+            add("h%d" % (t + 2), 2, "HB%d" % (t + 2), 0, 256, 0, False)
+        if t < 3:
+            add("y%d" % t, -1 - t, "KI", 16 * t, 16 * t + 16, 0, False)
+    add("w", -4, "L3I", 0, 256, 0, False)
     return out
 
 
-def mask_of(src, dst, topo):
-    return sum(1 << x for x in topo.engines(src, dst)[:8])
+def mask_of(src, dst, n, topo):
+    e = topo.engines(src, dst)
+    a = (8 * n) % len(e)
+    return sum(1 << x for x in e[a:a + 8])
 
 
 def hand_on(g, core, T, topo):
     own = [x for x in topo.cores_of(core) if T.rank_of(x) is not None]
     n = 0
     for rc in own:
-        for sem, dst, rel, buf, a, b in messages(rc, T, topo):
+        for sem, dst, rel, buf, a, b, es in messages(rc, T, topo):
             if rel == core:
-                g.wait_ge(T.sem[sem], bits(mask_of(rc, core, topo)))
-                m = mask_of(core, dst, topo)
+                g.wait_ge(T.sem[sem], bits(mask_of(rc, core, es, topo)))
+                m = mask_of(core, dst, es, topo)
                 rid, pid = topo.addr(dst, core)
                 g.remote_dma(T[buf][:, a:b], T[buf][:, a:b], T.sem[sem], T.sem.ls, pid, rid, m)
                 n += bits(m)
@@ -204,22 +207,21 @@ def rank_program(g, core, T, topo):
         used[s] = 16
         note(q, reads, writes, (s, 16, dict(known[q])))
 
-    def arrives(sem, src_off, buf, a, b):
-        src = T.cores[(rank + src_off) % N]
-        for s2, dst, rel, bf, _a, _b in messages(src, T, topo):
-            if s2 == sem and dst == core:
-                v = bits(mask_of(rel if rel is not None else src, core, topo))
-                used[sem] = v
-                note("x", [], [real((buf, a, b))], (sem, v, {}))
+    for off in range(1, N):
+        src = T.cores[(rank + off) % N]
+        for sem, dst, rel, bf, a, b, es in messages(src, T, topo):
+            if dst == core:
+                used[sem] = bits(mask_of(rel if rel is not None else src, core, es, topo))
+                note("x", [], [(bf, a, b)], (sem, used[sem], {}))
 
     plan = {m[0]: m for m in messages(core, T, topo)}
 
     def send(sem, buf, a, b):
-        _, dst, rel, ob, oa, oe = plan[sem]
+        _, dst, rel, ob, oa, oe, es = plan[sem]
         buf, a, b = real((buf, a, b))
         deps("g", [(buf, a, b)], [])
         to = dst if rel is None else rel
-        m = mask_of(core, to, topo)
+        m = mask_of(core, to, es, topo)
         rid, pid = topo.addr(to, core)
         g.remote_dma(T[ob][:, oa:oe], T[buf][:, a:b], T.sem[sem], T.sem.ls, pid, rid, m)
         state["ls"] += bits(m)
@@ -243,7 +245,8 @@ def rank_program(g, core, T, topo):
         op("t", g.tensor.matmul, dict(out=ap(out), lhsT=ap(l), rhs=ap(r), start=start, stop=stop), [rg(l), rg(r)], [rg(out)])
 
     def mm1(out, l, r, start, stop):
-        op("t", g.tensor.matmul, dict(out=ap(out), lhsT=T[l[0]][0:1, l[1]:l[2]], rhs=T[r[0]][0:1, r[1]:r[2]], start=start, stop=stop), [rg(l), rg(r)], [rg(out)])
+        l, r = real(l), real(r)
+        op("t", g.tensor.matmul, dict(out=ap(out), lhsT=T[l[0]][0:1, l[1]:l[2]], rhs=T[r[0]][0:1, r[1]:r[2]], start=start, stop=stop), [l, r], [rg(out)])
 
     def tt(out, a, b, o):
         op("v", g.vector.tensor_tensor, dict(out=ap(out), in0=ap(a), in1=ap(b), op=o), [rg(a), rg(b)], [rg(out)])
@@ -251,302 +254,316 @@ def rank_program(g, core, T, topo):
     def tti(out, win, off, b, o):
         op("v", g.vector.tensor_tensor, dict(out=ap(out), in0=ind(win, off), in1=ap(b), op=o), [rg(win), rg(off), rg(b)], [rg(out)])
 
+    def columns(*xs):
+        return [rg(x) for x in xs if isinstance(x, tuple)], [ap(x) if isinstance(x, tuple) else x for x in xs]
+
     def ts(out, a, s1, o1, s2=None, o2=None):
-        rd = [rg(a)]
-        sc = []
-        for s in (s1, s2):
-            if isinstance(s, tuple):
-                rd.append(rg(s))
-                sc.append(ap(s))
-            else:
-                sc.append(s)
+        rd, sc = columns(s1, s2)
         d = dict(out=ap(out), in0=ap(a), scalar1=sc[0], scalar2=sc[1], op0=o1)
         if o2 is not None:
             d["op1"] = o2
-        op("v", g.vector.tensor_scalar, d, rd, [rg(out)])
+        op("v", g.vector.tensor_scalar, d, rd + [rg(a)], [rg(out)])
 
     def tc(out, a):
         op("v", g.vector.tensor_copy, dict(out=ap(out), in_=ap(a)), [rg(a)], [rg(out)])
 
-    def ms(out, v):
-        op("v", g.vector.memset, dict(ap=ap(out), constant=v), [], [rg(out)])
+    def ms(out, v, rows=None):
+        o = real(out)
+        op("v", g.vector.memset, dict(ap=ap(out) if rows is None else T[o[0]][rows[0]:rows[1], o[1]:o[2]], constant=v), [], [rg(out)])
 
-    def act(out, a, f, bias=None, scale=None, accum=None):
-        d = dict(out=ap(out), in_=ap(a), func=f)
+    def act(out, a, f, bias=None, scale=None, accum=None, off=None):
+        rd, sc = columns(bias, scale)
+        d = dict(out=ap(out), in_=ap(a) if off is None else ind(a, off), func=f)
         wr = [rg(out)]
         if bias is not None:
-            d["bias"] = bias
+            d["bias"] = sc[0]
         if scale is not None:
-            d["scale"] = scale
+            d["scale"] = sc[1]
         if accum is not None:
             d["accum_out"] = ap(accum)
             wr.append(rg(accum))
-        op("s", g.scalar.activation, d, [rg(a)], wr)
+        op("s", g.scalar.activation, d, rd + [rg(a)] + ([] if off is None else [rg(off)]), wr)
 
-    def acti(out, win, off, f, bias=None, scale=None):
-        d = dict(out=ap(out), in_=ind(win, off), func=f)
-        if bias is not None:
-            d["bias"] = bias
-        if scale is not None:
-            d["scale"] = scale
-        op("s", g.scalar.activation, d, [rg(win), rg(off)], [rg(out)])
+    def iota(out, pattern, base, cm):
+        big = dict(allow_small_or_imprecise_dtypes=True) if SCRATCH[out[0]][2] == "float32" else {}
+        op("g", g.iota, dict(out=ap(out), pattern=pattern, base=base, channel_multiplier=cm, **big), [], [out])
 
     dma("d", T.VP32[:], T.vp[:], [], [("VP32", 0, 512)])
-    dma("s", T.MV32[:], T.mv[:], [], [("MV32", 0, 16)])
     dma("s", T.Z0B[:], T.z0[:], [], [("Z0B", 0, 256)])
-    dma("s", T.WT32[:], T.wt[:], [], [("WT32", 0, 1)])
+    dma("s", T.MV32[:], T.mv[:], [], [("MV32", 0, 16)])
+    dma("d", T.WT32[:], T.wt[:], [], [("WT32", 0, 1)])
     dma("d", T.RT[:, 0:4096], T.strat[:], [], [("RT", 0, 4096)])
+    dma("d", T.RT[:, 4096:RW], T.strat[:, 0:RW - 4096], [], [("RT", 4096, RW)])
 
-    big = dict(allow_small_or_imprecise_dtypes=True)
-    op("g", g.iota, dict(out=T.PI[:], pattern=[[0, 1]], base=0, channel_multiplier=1), [], [("PI", 0, 1)])
-    op("g", g.iota, dict(out=T.JI[:], pattern=[[1, 128]], base=0, channel_multiplier=0), [], [("JI", 0, 128)])
-    op("g", g.iota, dict(out=T.DIF[:], pattern=[[1, 128]], base=0, channel_multiplier=-1, **big), [], [("DIF", 0, 128)])
-    op("g", g.iota, dict(out=T.PB0[:], pattern=[[0, 2], [256, 8]], base=0, channel_multiplier=0), [], [("PB0", 0, 16)])
-    op("g", g.iota, dict(out=T.NF[:], pattern=[[1, 256]], base=512, channel_multiplier=0, **big), [], [("NF", 0, 256)])
+    iota(full("PI", 1), [[0, 1]], 0, 1)
+    iota(full("JI"), [[1, 128]], 0, 0)
+    iota(full("DIF"), [[1, 128]], 0, -1)
+    iota(full("NF", 256), [[1, 256]], 512, 0)
+    iota(full("ELI", 8), [[16, 8]], 15, 0)
+    iota(full("EPI"), [[1, 16], [16, 8]], 0, -1)
 
-    GP, KK, P16, K0, K14, KL, K37, E16, AK = [("COL", i, i + 1) for i in range(9)]
+    GP, KK, PF, RV, K0, K37, K37A, MP, P16, RA, AK, N1, N2, N3 = [("COL", i, i + 1) for i in range(14)]
     ts(full("PG", 1), full("PI", 1), 4, A.arith_shift_right)
     ts(full("PK", 1), full("PI", 1), 15, A.bitwise_and)
+    ms(full("MX", 2048), 1.0)
+    ms(("MX", 0, 2048, 16), 0.0)
     ts(full("JS"), full("JI"), 4, A.arith_shift_right)
     tc(GP, full("PG", 1))
     tc(KK, full("PK", 1))
-    ts(K37, KK, 37.0, A.mult)
-    ts(full("BLK"), full("JS"), GP, A.is_equal)
-    ts(full("IH"), full("DIF"), 0.0, A.is_equal, 0.5, A.mult)
-    ts(full("T1"), full("BLK"), 1000.0, A.mult, 1000.0, A.subtract)
-    ms(full("ONE"), 1.0)
-    ms(full("C32"), 0.25)
-    tt(full("DB"), full("DIF"), full("T1"), A.add)
-    op("v", g.vector.memset, dict(ap=T.CU[0:64, :], constant=-32.0), [], [("CU", 0, 64)])
-    op("v", g.vector.memset, dict(ap=T.CU[64:128, :], constant=0.0078125), [], [("CU", 64, 128)])
-    ts(full("T0"), full("DB"), -1.0, A.is_equal)
+    tc(PF, full("PI", 1))
     ts(full("IB"), full("DIF"), 0.0, A.is_equal)
+    ts(full("BLK"), full("JS"), GP, A.is_equal)
+    ts(K0, KK, 0.0, A.is_equal)
 
     tc(full("MV16", 16), full("MV32", 16))
+    ts(("ZO", 0, 256), full("Z0B", 256), 0.5, A.mult, 512.0, A.add)
+    send("z00", "ZO00", 0, 128)
     for c in range(2):
-        mo = "MO0%d" % c
-        tc((mo, 0, 128), ("Z0B", 128 * c, 128 * c + 128))
+        lo, off = full("LU0%d" % c), ("MV16", 8 * c, 8 * c + 8)
+        op("v", g.vector.tensor_copy, dict(out=ap(lo), in_=ind(("VP32", 0, 512), off)), [("VP32", 0, 512), off], [rg(lo)])
+        send("l0%d" % c, *lo)
         if c == 0:
-            send("z00", mo, 0, 128)
-    for c in range(2):
-        mo, off = "MO0%d" % c, ("MV16", 8 * c, 8 * c + 8)
-        op("v", g.vector.tensor_copy, dict(out=ap((mo, 128, 256)), in_=ind(("VP32", 0, 512), off)), [("VP32", 0, 512), off], [rg((mo, 128, 256))])
-        send("m0%d" % c, mo, 128, 256)
-        if c == 0:
-            send("z01", "MO01", 0, 128)
-    dma("d", T.VO32[:], T.vo[:], [("MO", 384, 512)], [("VO32", 0, 512)])
-    tt(full("DLM"), full("T0"), full("IB"), A.subtract)
-    ts(full("NIB"), full("DIF"), 0.0, A.is_equal, -1.0, A.mult)
-    tc(full("WTF", 1), full("WT32", 1))
-    ts(full("WB"), full("BLK"), full("WTF", 1), A.mult)
-    ms(full("MX", 2048), 1.0)
-    op("v", g.vector.memset, dict(ap=T.MX[:, 0:2048:16], constant=0.0), [], [("MX", 0, 2048)])
+            send("z01", "ZO01", 0, 128)
+    dma("d", T.VO32[:], T.vo[:], [rg(full("LU01"))], [("VO32", 0, 512)])
+
+    for n, v in (("IH", 0.5), ("NH", -0.5), ("NI4", -4096.0), ("I4", 4096.0), ("NIF", -1.0)):
+        act(full(n), full("IB"), F.Copy, scale=v)
     act(full("MN", 2048), full("MX", 2048), F.Identity, bias=512.0, scale=-512.0)
-    act(("RT", 4096, RW), ("RT", 0, RW - 4096), F.Copy)
-    tc(full("PV", 512), full("VP32", 512))
-
-    def const_a():
-        ts(full("NH"), full("DIF"), 0.0, A.is_equal, -0.5, A.mult)
-        ts(full("JM"), full("JI"), 15, A.bitwise_and)
-        ts(full("QB", 8), ("JI", 0, 8), GP, A.is_equal)
-        ts(full("QBH", 8), ("JI", 0, 8), GP, A.is_equal, 0.5, A.mult)
-        for c in range(2):
-            ts(full("C8%d" % c), full("JM"), KS[c] - 0.5, A.is_gt, 0.0625, A.mult)
-        ts(KL, KK, 15.0, A.is_lt)
-        ts(K0, KK, 0.0, A.is_equal)
-        ts(P16, full("PI", 1), 16.0, A.mult)
-        ts(K14, KK, 14.0, A.is_equal)
-        ts(E16, KK, 16.0, A.mult)
-        ts(full("B14"), full("BLK"), KL, A.mult)
-
-    def const_b():
-        ts(full("SH1"), full("DB"), 1.0, A.is_equal)
-        ts(full("BF"), full("BLK"), KL, A.mult)
-        ts(full("S0"), full("BLK"), K0, A.mult)
-        for i in range(2):
-            ts(("MK", 128 * i, 128 * i + 128), full("JM"), KK, A.is_equal)
-        ts(full("QF", 8), ("JI", 0, 8), GP, A.is_equal)
-        ts(full("QH", 8), ("JI", 0, 8), GP, A.is_equal)
-        ts(full("MB"), ("MK", 0, 128), P16, A.mult)
-        ts(full("NC0", 256), full("NF", 256), 0.0, A.add, K0, A.mult)
-        ts(full("PB", 16), full("PB0", 16), E16, A.add)
-
-    def const_c():
-        for t in range(1, 4):
-            ts(full("NC%d" % t, 256), full("NF", 256), 256.0 * t, A.add, K0, A.mult)
-        ts(full("SH2"), full("DB"), 2.0, A.is_equal)
-        ts(full("R14"), full("DIF"), 0.0, A.mult, K14, A.add)
-        ts(full("ROW1"), full("JM"), 1.0, A.is_equal)
-
-    def const_d():
-        ts(full("ROW0"), full("JM"), 0.0, A.is_equal)
-        ts(full("Q8", 8), ("JI", 0, 8), GP, A.is_equal, KL, A.mult)
-
-    for t in range(4):
-        for c in range(2):
-            arrives("m%d%d" % (t, c), -1, "MI%d%d" % (t, c), 0 if t else 128, 256)
-            arrives("y%d%d" % (t, c), 1 + t, "KI%d" % t, 128 * c, 128 * c + 128)
-            if t == 1:
-                arrives("h1%d" % c, -2, "HL1", 128 * c, 128 * c + 128)
-            if t >= 2:
-                arrives("h%d%d" % (t, c), -2, "HB%d" % t, 128 * c, 128 * c + 128)
-        arrives("v%d" % t, -1 - t, "VI%d" % t, 0, 512)
+    tc(full("WTF", 1), full("WT32", 1))
+    ts(full("WB"), full("BLK"), full("WTF", 1), A.mult, 2.0, A.mult)
+    ms(full("ONE"), 1.0)
+    ms(full("ONB"), 1.0)
+    ms(full("C5"), -512.0)
+    ms(full("C10"), -1024.0)
+    for rows, v in (((0, 32), 2.0 ** 17), ((32, 64), 2.0 ** 7), ((64, 128), 0.5)):
+        ms(full("CB"), v, rows)
+    ts(K37, KK, 37.0, A.mult)
+    ts(full("JM"), full("JI"), 15, A.bitwise_and)
+    ts(RV, GP, 32.0, A.mult, PF, A.subtract)
+    ts(full("KC"), full("JM"), 32.0, A.mult, 480.0, A.subtract)
+    ts(full("MK"), full("JM"), KK, A.is_equal)
+    ts(full("REV"), full("JI"), 15.0, A.subtract, RV, A.is_equal)
+    act(full("NM"), full("MK"), F.Identity, bias=-2.0 ** 23, scale=2.0 ** 23)
+    ts(full("QB", 8), ("JI", 0, 8), GP, A.is_equal, BIG, A.mult)
+    ts(full("QBH", 8), ("JI", 0, 8), GP, A.is_equal, BIG / 2, A.mult)
     for c in range(2):
-        arrives("h0%d" % c, -4, "HL3", 128 * c, 128 * c + 128)
-        arrives("w%d" % c, 4, "L3I", 128 * c, 128 * c + 128)
-        arrives("z0%d" % c, -1, "MI0%d" % c, 0, 128)
-        arrives("m4%d" % c, 4, "ZF", 128 * c, 128 * c + 128)
-        arrives("e4%d" % c, 4, "EF", 128 * c, 128 * c + 128)
+        ts(full("C8%d" % c), full("JM"), 15.5 - KS[c], A.is_gt, -8 * BIG / 128, A.mult)
+    ts(full("C8", 256), full("C8", 256), -2.5 * BIG / 128, A.add)
+    ms(("C8", 0, 256, 16), BIG / 128)
+    tc(full("EL", 8), full("ELI", 8))
+    for a, v in ((0, -1.0 / 4096), (8, -1.0 / 4096), (16, 1.0)):
+        ts(("QF", a, a + 8), ("JI", 0, 8), GP, A.is_equal, v, A.mult)
+    for a in (("RC", 0, 8), ("PC", 0, 8), ("PC", 8, 16)):
+        ts(a, ("JI", 0, 8), 2.0, A.mult)
+    ms(("RC", 8, 16), 0.0)
+    ms(("RC", 16, 24), -32.0 * 129)
+    ts(MP, KK, 16.0, A.mult, M23, A.add)
+    ts(P16, KK, 16.0, A.mult, 7.5, A.add)
+    ts(full("T1"), full("BLK"), 1000.0, A.mult, 1000.0, A.subtract)
+    tt(full("DB"), full("DIF"), full("T1"), A.add)
+    ts(full("SH1"), full("DB"), 1.0, A.is_equal)
+    act(full("NC0", 256), full("NF", 256), F.Copy, scale=K0)
+    act(full("PV", 512), full("VP32", 512), F.Copy)
+    act(full("OV", 512), full("VO32", 512), F.Copy)
+    send("v0", "OV", 0, 512)
+    send("v1", "PV", 0, 512)
+    send("h1", "LU00", 0, 256)
+    send("v2", "OV", 0, 512)
+    send("v3", "PV", 0, 512)
+    send("h0", "LU00", 0, 256)
+    for t, n in ((1, N1), (2, N2), (3, N3)):
+        ts(n, K0, 256.0 * t, A.mult)
+        act(full("NC%d" % t, 256), full("NF", 256), F.Identity, scale=K0, bias=n)
+    ms(full("H5"), 0.5)
+    ms(full("CA", 2), -127.5 / 128)
+    ts(K37A, KK, 37.0, A.mult, 127.5, A.add)
+    ts(full("SH2"), full("DB"), 2.0, A.is_equal)
+    ts(full("ROW1"), full("JM"), 1.0, A.is_equal)
+    ts(full("ROW0"), full("JM"), 0.0, A.is_equal)
+    ts(full("EP"), full("EPI"), 0.0, A.is_equal)
 
-    def pre_u(t, c):
-        z, l, pz = ("MI%d%d" % (t, c), 0, 128), ("MI%d%d" % (t, c), 128, 256), "pZ%d" % c
-        u, um = ("pU", 0, 128), ("pU", 128, 256)
-        mm(u, full("WB"), z, True, False)
-        mm(u, full("CU"), full("ONE"), False, True)
-        act(full("U1%d" % c), u, F.Identity, bias=M35)
-        act(full("U2%d" % c), full("U1%d" % c), F.Identity, bias=-M35)
-        mm((pz, 0, 128), full("IH"), z, True, True)
-        mm((pz, 128, 256), full("DLM"), l, True, True)
-        mm(um, full("WB"), z, True, False)
-        mm(um, full("C32"), full("ONE"), False, False)
-        mm(um, full("NIB"), full("U2%d" % c), False, True)
-        if t < TURNS - 1:
-            mm((pz, 256, 384), z, full("WB"), True, True)
+    def zi(t, c):
+        return full("ZI%d%d" % (t, c))
 
-    def offs(t, c):
-        ts(full("OF%d" % c), full("AS%d" % c), K37 if t == 0 else AK, A.add)
+    def li(t, c):
+        return full("LI%d%d" % (t, c))
 
-    def place_u(t, c):
-        if t < TURNS - 1:
-            tt(full("ZU%d" % c), ("pZ%d" % c, 256, 384), ("MK", 0, 128), A.mult)
-            mm(("pU", 400 + 8 * c, 408 + 8 * c), full("ZU%d" % c), full("QF", 8), True, True)
+    def u_sum(t, c):
+        mm(("pX", 256, 384), full("WB"), full("C5"), True, False)
+        mm(("pX", 256, 384), full("WB"), zi(t, c), False, True)
+        u = ("pU", 128 * c, 128 * c + 128)
+        mm(u, full("WB"), full("C5"), True, False)
+        mm(u, full("CB"), full("ONB"), False, False)
+        mm(u, full("WB"), zi(t, c), False, False)
 
-    def place_steps():
-        return [lambda: tc(full("PLI", 16), ("pU", 400, 416)), lambda: ts(full("PLA", 16), full("PLI", 16), 15, A.bitwise_and),
-                lambda: tt(full("PLB", 16), full("PLA", 16), full("PB", 16), A.add), lambda: tc(full("PL", 16), full("PLB", 16))]
+    def u_mod(t, c):
+        act(full("U2%d" % c), ("pX", 256, 384), F.Identity, bias=1024.5 + 2.0 ** -13, scale=1.0 / 4096)
+        mm(("pU", 128 * c, 128 * c + 128), full("NI4"), full("U2%d" % c), False, True)
+
+    def address(t, c):
+        return [lambda: tt(full("AT%d" % c), li(t, c), ("pU", 128 * c, 128 * c + 128), A.mult),
+                lambda: ts(full("AS%d" % c), full("AT%d" % c), 5, A.arith_shift_right, 4095, A.bitwise_and),
+                lambda: ts(full("OF%d" % c), full("AS%d" % c), K37 if t == 0 else AK, A.add)]
+
+    def z_psum(t, c):
+        o = ("pZ", 128 * c, 128 * c + 128)
+        mm(o, full("IH"), full("C5"), True, False)
+        mm(o, full("IH"), zi(t, c), False, True)
+
+    def key_t(t, c):
+        mm(("pX", 0, 128), full("ONE"), full("KC"), True, False)
+        mm(("pX", 0, 128), li(t, c), full("REV"), False, True)
+
+    def key_s(c):
+        act(full("BT%d" % c), ("pX", 0, 128), F.Copy)
+
+    def place_t(t, c):
+        mm(("pW", 0, 128), full("IB"), full("NM"), True, False)
+        mm(("pW", 0, 128), zi(t, c), full("WB"), False, True)
+
+    def place_s(c):
+        act(full("ZU%d" % c), ("pW", 0, 128), F.Relu, bias=-7.5)
+
+    def place_sum():
+        for c in range(2):
+            mm(("pW", 256 + 8 * c, 264 + 8 * c), full("ZU%d" % c), ("QF", 16, 24), True, True)
+        act(("RR", 16, 32), ("pW", 256, 272), F.Identity, bias=M27)
+        act(full("RR", 16), ("RR", 16, 32), F.Identity, bias=-M27)
+        mm(("pU", 256, 272), full("ONE"), full("PC", 16), True, False)
+        for c in range(2):
+            mm(("pU", 256 + 8 * c, 264 + 8 * c), full("ZU%d" % c), ("QF", 16, 24), False, False)
+        mm(("pU", 256, 272), full("NIF"), full("RR", 16), False, True)
+
+    def place_out():
+        ts(full("PL", 16), ("pU", 256, 272), P16, A.add)
+
+    def old(c):
+        act(full("OLD%d" % c), ("RT", 2048 * c, 2048 * c + 2048), F.Identity, bias=-0.5, off=("PL", 8 * c, 8 * c + 8))
+        o = ("pZ", 256 + 128 * c, 384 + 128 * c)
+        mm(o, full("IH"), full("C10"), True, False)
+        mm(o, full("IH"), full("OLD%d" % c), False, True)
 
     def gather(c, a, b, q):
-        if a >= b:
-            return
         y, of, w = ("Y%d" % c, 16 * a, 16 * b), ("OF%d" % c, a, b), ("RT", 0, RW)
         if q == "s":
-            acti(y, w, of, F.Copy, scale=0.5)
+            act(y, w, F.Copy, scale=0.25, off=of)
         else:
-            op("v", g.vector.tensor_scalar, dict(out=ap(y), in0=ind(w, of), scalar1=0.5, scalar2=None, op0=A.mult), [w, rg(of)], [rg(y)])
+            op("v", g.vector.tensor_scalar, dict(out=ap(y), in0=ind(w, of), scalar1=0.25, scalar2=None, op0=A.mult), [w, rg(of)], [rg(y)])
 
-    def compare_s(t, c):
-        y, b, z = "Y%d" % c, "B%d" % c, ("MI%d%d" % (t, c), 0, 128)
-        for i, k0 in enumerate(range(KS[c], 16, 4)):
-            k1 = min(k0 + 4, 16)
-            pd = "pD%d" % (i % 2)
-            for k in range(k0, k1):
-                o = (pd, 128 * (k - k0), 128 * (k - k0) + 128)
-                mm(o, full("IB"), (y, k, 2048, 16), True, False)
-                mm(o, full("NH"), z, False, True)
-            act((b, 128 * k0, 128 * k1), (pd, 0, 128 * (k1 - k0)), F.Sign, bias=-0.25)
+    def blocks(c):
+        k = [KS[c], KS[c] + FIRST]
+        while k[-1] < 15:
+            k.append(min(15, k[-1] + 4))
+        return list(zip(k[:-1], k[1:]))
 
-    def compare_v(t, c):
+    def diff_t(t, c, i):
+        k0, k1 = blocks(c)[i]
+        for k in range(k0, k1):
+            o = ("pD%d" % (i % 2), 128 * (k - k0), 128 * (k - k0) + 128)
+            mm(o, full("NH"), zi(t, c), True, False)
+            mm(o, full("IB"), ("Y%d" % c, k, 2048, 16), False, True)
+
+    def sign_s(c, i):
+        k0, k1 = blocks(c)[i]
+        act(("B%d" % c, 128 * k0, 128 * k1), ("pD%d" % (i % 2), 0, 128 * (k1 - k0)), F.Sign, bias=256.0 - 0.125)
+
+    def compare_v(c):
         for k in range(KS[c]):
-            tt(("B%d" % c, 128 * k, 128 * k + 128), ("Y%d" % c, k, 2048, 16), ("pZ%d" % c, 0, 128), A.is_gt)
+            tt(("B%d" % c, 128 * k, 128 * k + 128), ("Y%d" % c, k, 2048, 16), ("pZ", 128 * c, 128 * c + 128), A.is_gt)
 
-    def beats(c):
-        mm(("pC", 0, 128), full("ONE"), full("C8%d" % c), True, False)
-        for k in range(16):
-            mm(("pC", k, 128, 16), ("B%d" % c, 128 * k, 128 * k + 128), full("QB" if k < KS[c] else "QBH", 8), False, k == 15)
+    def beats(c, ks, first, last):
+        if first:
+            mm(("pC", 128 * c, 128 * c + 128), full("ONE"), full("C8%d" % c), True, False)
+        for k in ks:
+            mm(("pC", 128 * c + 15 - k, 128 * c + 128, 16), ("B%d" % c, 128 * k, 128 * k + 128), full("QB" if k < KS[c] else "QBH", 8), False, last and k == ks[-1])
 
-    def scan(c, hi):
-        o, y = full(("HI%d" if hi else "LO%d") % c, 2048), full("Y%d" % c, 2048)
-        m = full("MX" if hi else "MN", 2048)
+    def compare(t, c, between):
+        bl = blocks(c)
+        diff_t(t, c, 0)
+        diff_t(t, c, 1)
+        for i in range(len(bl)):
+            sign_s(c, i)
+            if i + 2 < len(bl):
+                diff_t(t, c, i + 2)
+            ks = list(range(*bl[i]))
+            if i == len(bl) - 2:
+                ks = list(range(KS[c])) + ks
+            beats(c, ks, i == 0, i == len(bl) - 1)
+            for f in between.get(i, []):
+                f()
+
+    def scan(c, hi, a=0, b=H):
+        o, y = (("HI%d" if hi else "LO%d") % c, 16 * a, 16 * b), ("Y%d" % c, 16 * a, 16 * b)
+        m = ("MX" if hi else "MN", 16 * a, 16 * b)
         op("v", g.vector.tensor_tensor_scan, dict(out=ap(o), data0=ap(m), data1=ap(y), initial=0.0,
                                                   op0=A.mult if hi else A.add, op1=A.max if hi else A.min), [m, rg(y)], [rg(o)])
 
-    def verdict_v(c):
-        o, m = full("CM%d" % c), full("MX")
-        op("v", g.vector.tensor_tensor_scan, dict(out=ap(o), data0=ap(m), data1=ap(("pC", 0, 128)), initial=0.0, op0=A.mult, op1=A.max),
-           [m, ("pC", 0, 128)], [rg(o)])
-        ts(full("RN%d" % c), o, 10.5, A.is_lt)
-        mm(("pC", 128, 256), full("RN%d" % c), full("IB"), True, True)
+    def verdict(c):
+        o, d = full("PS%d" % c), ("pC", 128 * c, 128 * c + 128)
+        op("v", g.vector.tensor_tensor_scan, dict(out=ap(o), data0=ap(d), data1=ap(full("BT%d" % c)), initial=0.0, op0=A.max, op1=A.min),
+           [d, rg(full("BT%d" % c))], [rg(o)])
 
-    def verdict_s(t, c):
-        run = ("RUN%d" % t, 128 * c, 128 * c + 128)
-        act(run, ("pC", 128, 256), F.Copy, accum=full("ACC%d" % c, 1))
-        mm(("pR", 128, 256), run, full("B14"), True, True)
+    def spread(c):
+        tti(full("KX%d" % c), full("PS%d" % c), full("EL", 8), full("MK"), A.mult)
+        mm(("pR", 0, 16), full("ONE"), full("RC", 16), True, False)
+        mm(("pR", 0, 16), full("KX%d" % c), full("QF", 16), False, True)
+        mm(("pC", 256, 264), full("ONE"), ("RC", 16, 24), True, False)
+        mm(("pC", 256, 264), full("KX%d" % c), ("QF", 16, 24), False, False)
 
-    def named(t, c):
-        run = ("RUN%d" % t, 128 * c, 128 * c + 128)
-        tt(full("P%d" % c), run, ("pZ%d" % c, 128, 256), A.mult)
-        mm(("pR", 0, 128), ("MI%d%d" % (t, c), 128, 256), full("S0"), True, False)
-        mm(("pR", 0, 128), full("P%d" % c), full("BF"), False, True)
+    def list_k(c):
+        ts(full("LK%d" % c, 8), ("pR", 0, 8), MP, A.add, M23, A.subtract)
 
-    def lists(t, c):
-        zm = "ZM%d" % c
-        tt(full(zm, 256), ("pR", 0, 256), full("MK", 256), A.mult)
-        mm(("pR", 256, 264), (zm, 0, 128), full("QH", 8), True, True)
-        mm(("pR", 264, 272), (zm, 128, 256), full("QH", 8), True, False)
-        mm(("pR", 264, 272), full("MB"), full("QH", 8), False, True)
+    def kappa(t, c):
+        k = ("KO", 16 * t + 8 * c, 16 * t + 8 * c + 8)
+        act(k, ("pR", 8, 16), F.Identity, bias=129.0)
+        mm(("pC", 256, 264), full("I4"), k, False, True)
 
-    def lists_out(t, c):
-        tc(full("LS%d" % c, 16), ("pR", 256, 272))
+    def list_n(c):
+        tc(full("LN%d" % c, 8), ("pC", 256, 264))
 
-    def select_hi(t, c):
-        acti(full("HG%d" % c), full("HI%d" % c, 2048), ("LS%d" % c, 8, 16), F.Identity, bias=-0.25)
+    def pick_hi(c):
+        act(full("HG%d" % c), full("HI%d" % c, 2048), F.Identity, bias=512.0 - 0.125, off=full("LK%d" % c, 8))
 
-    def select_steps(t, c):
-        kap, nam = ("LS%d" % c, 8, 16), ("LS%d" % c, 0, 8)
-        mo = "MO%d%d" % (t + 1, c)
-        half = (128 * c, 128 * c + 128)
-        z, l = ((mo, 0, 128), (mo, 128, 256)) if t < TURNS - 1 else (("ZO",) + half, ("EO",) + half)
+    def new_z(t, c):
+        z = full("ZO%d%d" % (t + 1, c))
+        tti(z, full("LO%d" % c, 2048), full("LK%d" % c, 8), full("HG%d" % c), A.add)
+        if t == TURNS - 1:
+            o = ("ZL", 128 * c, 128 * c + 128)
+            ts(o, z, 2.0, A.mult, 1024.0, A.subtract)
+            z = o
+        send("z%d%d" % (t + 1, c), *z)
 
-        def views():
-            tti(l, full("TAB%d" % t, 512 + 256 * t), nam, ("NC%d" % t,) + half, A.add)
-            if t == TURNS - 1:
-                send("e4%d" % c, *l)
+    def views(t, c):
+        l = full("LU%d%d" % (t + 1, c)) if t < TURNS - 1 else ("EO", 128 * c, 128 * c + 128)
+        tti(l, full("TAB%d" % t, 512 + 256 * t), full("LN%d" % c, 8), ("NC%d" % t, 128 * c, 128 * c + 128), A.add)
+        send("l%d%d" % (t + 1, c), *l)
 
-        def out():
-            ts(z, full("SM%d" % c), M23, A.add, M23, A.subtract)
-            if t == TURNS - 1:
-                send("m4%d" % c, *z)
-                return
-            send("m%d%d" % (t + 1, c), mo, 0, 256)
-            if t < 2:
-                send("h%d%d" % (t + 2, c), *l)
-        return [views, lambda: tti(full("SM%d" % c), full("LO%d" % c, 2048), kap, full("HG%d" % c), A.add), out]
+    def mean(t, c):
+        tt(full("RZ%d" % c), ("pZ", 256 + 128 * c, 384 + 128 * c), full("ZO%d%d" % (t + 1, c)), A.add)
 
-    def update_steps(t, c):
+    def scatter(c):
         win, off = ("RT", 2048 * c, 2048 * c + 2048), ("PL", 8 * c, 8 * c + 8)
+        op("v", g.vector.tensor_copy, dict(out=ind(win, off), in_=ap(full("RZ%d" % c))), [off, rg(full("RZ%d" % c))], [win])
 
-        def out():
-            op("v", g.vector.tensor_copy, dict(out=ind(win, off), in_=ap(full("RZ%d" % c))), [off, rg(full("RZ%d" % c))], [win])
-            if c == 0:
-                act(("RT", 4096, RW), ("RT", 0, RW - 4096), F.Copy)
-        return [lambda: tti(full("RY%d" % c), win, off, ("MO%d%d" % (t + 1, c), 0, 128), A.add),
-                lambda: ts(full("RZ%d" % c), full("RY%d" % c), 1, A.arith_shift_right), out]
+    def behind():
+        act(("RT", 4096, RW), ("RT", 0, RW - 4096), F.Copy)
 
-    def count_t():
-        for c in range(2):
-            mm(("pC", 256, 257), full("R14"), full("ACC%d" % c, 1), c == 0, c == 1)
+    def count():
+        act(full("SG", 16), ("PS", 15, 256, 16), F.Sign, bias=58000.0, accum=full("ACC", 1))
+        mm(("pD0", 0, 1), full("ONE"), ("CA", 0, 1), True, False)
+        mm(("pD0", 0, 1), full("H5"), full("ACC", 1), False, True)
 
-    def count_steps():
-        return [lambda: ts(full("AI", 1), ("pC", 256, 257), -1.0, A.mult), lambda: ts(full("AJ", 1), full("AI", 1), 255, A.bitwise_and),
-                lambda: ts(AK, full("AJ", 1), K37, A.add)]
+    def count_a():
+        ts(RA, ("pD0", 0, 1), M31, A.add, M31, A.subtract)
 
-    def pre_steps(t, c):
-        return [lambda: tt(full("AT%d" % c), ("MI%d%d" % (t, c), 128, 256), ("pU", 128, 256), A.mult),
-                lambda: ts(full("AS%d" % c), full("AT%d" % c), 5, A.arith_shift_right, 4095, A.bitwise_and), lambda: offs(t, c)]
-
-    def pre_v(t, c):
-        for f in pre_steps(t, c)[:2]:
-            f()
-
-    def select(t, c):
-        for f in select_steps(t, c):
-            f()
+    def count_b():
+        ts(AK, ("pD0", 0, 1), RA, A.subtract, K37A, A.add)
 
     parts = {(0, 0): [(0, 0, "VI0", 1, 0)], (0, 1): [(1, 0, "VI1", 1, 0)], (1, 0): [(1, 512, "HL1", 2, 0), (3, 512, "HL3", 2, 0)],
              (1, 1): [(2, 0, "VI2", 1, 0)], (2, 0): [(2, 512, "HB2", 1, 0), (2, 768, "HB2", 2, 1)], (2, 1): [(3, 0, "VI3", 1, 0)],
              (3, 0): [(3, 768, "HB3", 1, 0), (3, 1024, "HB3", 2, 2)]}
 
-    def table_t(key):
+    def table(key):
         a = 0
         for tb, c0, src, sh, n in parts.get(key, []):
             wd = 512 if src[0] == "V" else 256
@@ -555,117 +572,126 @@ def rank_program(g, core, T, topo):
             if sh == 2:
                 mm1(w, full("ROW1"), full("NC%d" % n, 256), False, True)
             a += wd
-
-    def table_s(key):
         a = 0
         for tb, c0, src, sh, n in parts.get(key, []):
             wd = 512 if src[0] == "V" else 256
             act(("TAB%d" % tb, c0, c0 + wd), ("pW", a, a + wd), F.Copy)
             a += wd
 
-    def run_out(t, c):
-        send("y%d%d" % (t, c), "RUN%d" % t, 128 * c, 128 * c + 128)
+    def verdicts_out(a, b):
+        w = 16 * (b - a)
+        for p in range(16):
+            op("t", g.tensor.matmul, dict(out=T.pW[0:8, p:w:16], lhsT=T.EP[:, 8 * p:8 * p + 8], rhs=T.KI[:, a:b], start=True, stop=True),
+               [full("EP"), ("KI", a, b)], [("pW", 0, w)])
+        op("s", g.scalar.activation, dict(out=T.YKS[:, 16 * a:16 * b], in_=T.pW[0:8, 0:w], func=F.Identity, bias=-129.0), [("pW", 0, w)], [("YKS", 16 * a, 16 * b)])
+        dma("d", T.yk[:, 16 * a:16 * b], T.YKS[:, 16 * a:16 * b], [("YKS", 16 * a, 16 * b)], [("yk", 16 * a, 16 * b)])
 
     def turn(t):
         last = t == TURNS - 1
+        z_psum(t, 0)
+        key_t(t, 0)
+        if not last:
+            place_t(t, 0)
         gather(0, 0, GS[0], "s")
         gather(0, GS[0], H, "v")
-        compare_s(t, 0)
-        pre_u(t, 1)
-        compare_v(t, 0)
-        beats(0)
-        scan(0, True)
-        scan(0, False)
-        pre_v(t, 1)
-        offs(t, 1)
-        gather(1, 0, CUTS[0], "s")
-        gather(1, GS[1], H, "v")
-        table_t((t, 0))
-        verdict_v(0)
-        place_u(t, 0)
-        verdict_s(t, 0)
-        named(t, 0)
-        gather(1, CUTS[0], CUTS[1], "s")
-        table_s((t, 0))
-        lists(t, 0)
-        place_u(t, 1)
-        lists_out(t, 0)
-        select_hi(t, 0)
-        gather(1, CUTS[1], GS[1], "s")
-        select(t, 0)
-        run_out(t, 0)
-        if last:
-            for c in range(2):
-                send("w%d" % c, "MI3%d" % c, 128, 256)
-        compare_s(t, 1)
-        compare_v(t, 1)
-        beats(1)
-        table_t((t, 1))
-        scan(1, True)
-        scan(1, False)
-        verdict_v(1)
-        verdict_s(t, 1)
-        pl = [] if last else place_steps()
-        for f in pl[:2]:
-            f()
-        named(t, 1)
-        table_s((t, 1))
-        for f in pl[2:]:
-            f()
-        lists(t, 1)
+        key_s(0)
         if not last:
-            u0 = update_steps(t, 0)
-            u0[0]()
-            u0[1]()
-        lists_out(t, 1)
-        select_hi(t, 1)
+            place_s(0)
+        compare_v(0)
+        scan(0, True)
+        compare(t, 0, {})
+        u_sum(t, 1)
+        u_mod(t, 1)
+        ad = address(t, 1)
+        verdict(0)
+        spread(0)
+        ad[0]()
+        key_t(t, 1)
+        key_s(1)
+        list_k(0)
+        ad[1]()
+        kappa(t, 0)
+        ad[2]()
+        pick_hi(0)
+        list_n(0)
+        if not last:
+            place_t(t, 1)
+            place_s(1)
+            place_sum()
+        scan(0, False)
+        if t == 0:
+            table((0, 0))
+        gather(1, 0, GS[1], "s")
+        z_psum(t, 1)
+        new_z(t, 0)
+        views(t, 0)
         if last:
-            run_out(t, 1)
-            select(t, 1)
+            send("y30", "KO", 48, 56)
+            send("w", "LI30", 0, 256)
+        gather(1, GS[1], H, "v")
+        if last:
+            compare_v(1)
+            scan(1, True)
+            compare(t, 1, {})
+            verdict(1)
+            spread(1)
+            list_k(1)
+            kappa(t, 1)
+            pick_hi(1)
+            send("y31", "KO", 56, 64)
+            list_n(1)
+            views(t, 1)
+            scan(1, False)
+            new_z(t, 1)
             return
-        count_t()
-        pre_u(t + 1, 0)
-        z = select_steps(t, 1)
-        u = update_steps(t, 1)
-        n = count_steps()
-        for f in (z[0], n[0], z[1], n[1], z[2], n[2], u0[2], u[0]):
-            f()
-        p = pre_steps(t + 1, 0)
-        for f in (p[0], u[1], p[1], u[2], p[2]):
-            f()
-        run_out(t, 1)
+        place_out()
+        old(0)
+        compare_v(1)
+        mean(t, 0)
+        scan(1, True)
+        compare(t, 1, {})
+        old(1)
+        verdict(1)
+        spread(1)
+        count()
+        scatter(0)
+        u_sum(t + 1, 0)
+        u_mod(t + 1, 0)
+        ad = address(t + 1, 0)
+        list_k(1)
+        pick_hi(1)
+        kappa(t, 1)
+        behind()
+        scan(1, False)
+        new_z(t, 1)
+        list_n(1)
+        count_a()
+        mean(t, 1)
+        views(t, 1)
+        scatter(1)
+        ad[0]()
+        count_b()
+        ad[1]()
+        ad[2]()
+        table((t, 1))
+        table((t + 1, 0))
+        if t < 2:
+            send("h%d" % (t + 2), "LU%d0" % (t + 1), 0, 256)
+        send("y%d" % t, "KO", 16 * t, 16 * t + 16)
 
-    const_a()
-    const_b()
-    tc(full("OV", 512), full("VO32", 512))
-    send("v0", "OV", 0, 512)
-    send("v1", "PV", 0, 512)
-    for c in range(2):
-        send("h1%d" % c, "MO0%d" % c, 128, 256)
-    send("v2", "OV", 0, 512)
-    send("v3", "PV", 0, 512)
-    for c in range(2):
-        send("h0%d" % c, "MO0%d" % c, 128, 256)
-    const_c()
-    const_d()
-    pre_u(0, 0)
-    pre_v(0, 0)
-    offs(0, 0)
+    u_sum(0, 0)
+    u_mod(0, 0)
+    for f in address(0, 0):
+        f()
     for t in range(TURNS):
         turn(t)
 
-    for t in range(TURNS):
-        w = T.pW[0:8, 0:256]
-        op("t", g.tensor.matmul, dict(out=w, lhsT=T.Q8[:], rhs=T["KI%d" % t][:], start=True, stop=True),
-           [full("Q8", 8), full("KI%d" % t, 256)], [("pW", 0, 256)])
-        op("s", g.scalar.activation, dict(out=T.YKS[:, 256 * t:256 * t + 256], in_=w, func=F.Copy), [("pW", 0, 256)], [("YKS", 256 * t, 256 * t + 256)])
-        if t == 2:
-            dma("d", T.yk[:, 0:768], T.YKS[:, 0:768], [("YKS", 0, 768)], [("yk", 0, 768)])
-            mm(("pC", 0, 256), full("SH1"), full("L3I", 256), True, False)
-            mm1(("pC", 0, 256), full("ROW0"), full("NC3", 256), False, True)
-            act(full("YOS", 256), ("pC", 0, 256), F.Copy)
-            dma("d", T.yo[:], T.YOS[:], [full("YOS", 256)], [("yo", 0, 256)])
-    dma("d", T.yk[:, 768:1024], T.YKS[:, 768:1024], [("YKS", 768, 1024)], [("yk", 768, 1024)])
+    mm(("pC", 0, 256), full("SH1"), full("L3I", 256), True, False)
+    mm1(("pC", 0, 256), full("ROW0"), full("NC3", 256), False, True)
+    act(full("YOS", 256), ("pC", 0, 256), F.Copy)
+    dma("d", T.yo[:], T.YOS[:], [full("YOS", 256)], [("yo", 0, 256)])
+    verdicts_out(0, 32)
+    verdicts_out(32, 64)
     for c in range(2):
         a, b = 128 * c, 128 * c + 128
         dma("d", T.yp[:, a:b], T.EF[:, a:b], [("EF", a, b)], [("yp", a, b)])

@@ -2,8 +2,14 @@ from concourse.mybir import AluOpType as A, ActivationFunctionType as F
 
 N, TURNS, H = 8, 4, 128
 RW = 4096 + 816
-GS = (64, 96)
-KS = (6, 6)
+EARLY = 1536
+GS = (64, 80)
+CUTS = (32, 56)
+HC = ((0, 64, 128), (0, 56, 80, 128))
+LC = ((0, 64, 96, 128), (0, 56, 80, 128))
+ON_S = ("mean0", "place_out", "list_n0", "list_n1")
+ORDER = """gather_s0 out_k0 gather_v0 diff00 lo0c hi0a compare_v0 sign00 diff01 sign01 diff02 u_sum1 lo0b beats00 u_mod1 diff03 sign02 sign03 place_t1 bulk lo0a product1 shift1 diff13 offsets1 beats01 place_s1 beats02 beats03 verdict0 z_psum1 gather_s1c table_0 spread0 hi0b gather_s1b out_k1 place_sum list_k0 gather_v1 kappa0 pick_hi0 list_n0 new_z0 key_t1 gather_s1a lo1b table_a diff10 views0 sign13 last_l compare_v1 hi1b sign10 hi1c diff11 key_s1 beats10 place_out sign11 diff12 sign12 old0 hi1a last0 lo1a beats11 beats13 beats12 mean0 verdict1 spread1 out_c0 count scatter0 kappa1 old1 list_n1 n_place_t behind list_k1 n_u_sum pick_hi1 n_place_s last1 lo1c views1 new_z1 count_a n_u_mod mean1 table_b history n_z_psum scatter1 out_o n_key_t n_key_s n_product count_b n_shift n_offsets""".split()
+KS = (3, 5)
 FIRST = 2
 M31, M27, M23 = 1.5 * 2.0 ** 31, 1.5 * 2.0 ** 27, 1.5 * 2.0 ** 23
 BIG = 2.0 ** 17
@@ -23,7 +29,7 @@ SCRATCH = {
     "BLK": ("sbuf", [128, 128], "bfloat16"), "T1": ("sbuf", [128, 128], "bfloat16"), "EPI": ("sbuf", [128, 128], "float32"),
     "IB": ("sbuf", [128, 128], "bfloat16"), "I4": ("sbuf", [128, 128], "bfloat16"), "IH": ("sbuf", [128, 128], "float16"),
     "NH": ("sbuf", [128, 128], "float16"), "NI4": ("sbuf", [128, 128], "float16"), "NIF": ("sbuf", [128, 128], "float32"),
-    "WB": ("sbuf", [128, 128], "float16"), "REV": ("sbuf", [128, 128], "float16"), "KC": ("sbuf", [128, 128], "float16"),
+    "IF": ("sbuf", [128, 128], "float16"), "WB": ("sbuf", [128, 128], "float16"), "REV": ("sbuf", [128, 128], "float16"), "KC": ("sbuf", [128, 128], "float16"),
     "SH1": ("sbuf", [128, 128], "float16"), "SH2": ("sbuf", [128, 128], "float16"), "EP": ("sbuf", [128, 128], "bfloat16"),
     "MK": ("sbuf", [128, 128], "float32"), "NM": ("sbuf", [128, 128], "bfloat16"),
     "QF": ("sbuf", [128, 32], "float32"), "QB": ("sbuf", [128, 8], "bfloat16"), "QBH": ("sbuf", [128, 8], "bfloat16"),
@@ -62,7 +68,7 @@ for _n, _w, _d in (("Y", 2048, "bfloat16"), ("B", 2048, "bfloat16"), ("HI", 2048
     for _c in range(2):
         ALIAS["%s%d" % (_n, _c)] = (_n, _w * _c)
 
-SEMAPHORES = (["qg", "qt", "qv", "qs", "ls"] + ["d%d" % i for i in range(28)]
+SEMAPHORES = (["qg", "qt", "qv", "qs", "ls", "l0"] + ["d%d" % i for i in range(28)]
               + ["%s%d%d" % (n, t, c) for n in "zl" for t in range(5) for c in range(2)] + ["v%d" % t for t in range(4)]
               + ["h%d" % t for t in range(4)] + ["y0", "y1", "y2", "y30", "y31", "w"])
 
@@ -150,7 +156,7 @@ def rank_program(g, core, T, topo):
     cnt = {"g": 0, "t": 0, "v": 0, "s": 0}
     known = {q: {} for q in Q}
     acc, bank, used = {}, {}, {}
-    state = {"d": 0, "ls": 0}
+    state = {"d": 0, "sent": {"ls": 0, "l0": 0}}
 
     def need(q, tok):
         sem, val, clk = tok
@@ -216,15 +222,15 @@ def rank_program(g, core, T, topo):
 
     plan = {m[0]: m for m in messages(core, T, topo)}
 
-    def send(sem, buf, a, b):
+    def send(sem, buf, a, b, left="ls"):
         _, dst, rel, ob, oa, oe, es = plan[sem]
         buf, a, b = real((buf, a, b))
         deps("g", [(buf, a, b)], [])
         to = dst if rel is None else rel
         m = mask_of(core, to, es, topo)
         rid, pid = topo.addr(to, core)
-        g.remote_dma(T[ob][:, oa:oe], T[buf][:, a:b], T.sem[sem], T.sem.ls, pid, rid, m)
-        state["ls"] += bits(m)
+        g.remote_dma(T[ob][:, oa:oe], T[buf][:, a:b], T.sem[sem], T.sem[left], pid, rid, m)
+        state["sent"][left] += bits(m)
 
     def ap(o):
         o = real(o)
@@ -288,12 +294,11 @@ def rank_program(g, core, T, topo):
         big = dict(allow_small_or_imprecise_dtypes=True) if SCRATCH[out[0]][2] == "float32" else {}
         op("g", g.iota, dict(out=ap(out), pattern=pattern, base=base, channel_multiplier=cm, **big), [], [out])
 
-    dma("d", T.VP32[:], T.vp[:], [], [("VP32", 0, 512)])
     dma("s", T.Z0B[:], T.z0[:], [], [("Z0B", 0, 256)])
+    dma("d", T.VP32[:], T.vp[:], [], [("VP32", 0, 512)])
     dma("s", T.MV32[:], T.mv[:], [], [("MV32", 0, 16)])
     dma("d", T.WT32[:], T.wt[:], [], [("WT32", 0, 1)])
-    dma("d", T.RT[:, 0:4096], T.strat[:], [], [("RT", 0, 4096)])
-    dma("d", T.RT[:, 4096:RW], T.strat[:, 0:RW - 4096], [], [("RT", 4096, RW)])
+    dma("d", T.RT[:, 0:EARLY], T.strat[:, 0:EARLY], [], [("RT", 0, EARLY)])
 
     iota(full("PI", 1), [[0, 1]], 0, 1)
     iota(full("JI"), [[1, 128]], 0, 0)
@@ -305,8 +310,6 @@ def rank_program(g, core, T, topo):
     GP, KK, PF, RV, K0, K37, K37A, MP, P16, RA, AK, N1, N2, N3 = [("COL", i, i + 1) for i in range(14)]
     ts(full("PG", 1), full("PI", 1), 4, A.arith_shift_right)
     ts(full("PK", 1), full("PI", 1), 15, A.bitwise_and)
-    ms(full("MX", 2048), 1.0)
-    ms(("MX", 0, 2048, 16), 0.0)
     ts(full("JS"), full("JI"), 4, A.arith_shift_right)
     tc(GP, full("PG", 1))
     tc(KK, full("PK", 1))
@@ -315,18 +318,22 @@ def rank_program(g, core, T, topo):
     ts(full("BLK"), full("JS"), GP, A.is_equal)
     ts(K0, KK, 0.0, A.is_equal)
 
-    tc(full("MV16", 16), full("MV32", 16))
     ts(("ZO", 0, 256), full("Z0B", 256), 0.5, A.mult, 512.0, A.add)
-    send("z00", "ZO00", 0, 128)
+    send("z00", "ZO00", 0, 128, "l0")
+    tc(full("MV16", 16), full("MV32", 16))
     for c in range(2):
         lo, off = full("LU0%d" % c), ("MV16", 8 * c, 8 * c + 8)
         op("v", g.vector.tensor_copy, dict(out=ap(lo), in_=ind(("VP32", 0, 512), off)), [("VP32", 0, 512), off], [rg(lo)])
         send("l0%d" % c, *lo)
         if c == 0:
             send("z01", "ZO01", 0, 128)
-    dma("d", T.VO32[:], T.vo[:], [rg(full("LU01"))], [("VO32", 0, 512)])
+    g.sync.wait_ge(T.sem.l0, state["sent"]["l0"])
+    dma("d", T.VO32[:], T.vo[:], [], [("VO32", 0, 512)])
+    dma("d", T.RT[:, EARLY:4096], T.strat[:, EARLY:4096], [], [("RT", EARLY, 4096)])
 
-    for n, v in (("IH", 0.5), ("NH", -0.5), ("NI4", -4096.0), ("I4", 4096.0), ("NIF", -1.0)):
+    ms(full("MX", 2048), 1.0)
+    ms(("MX", 0, 2048, 16), 0.0)
+    for n, v in (("IH", 0.5), ("NH", -0.5), ("NI4", -4096.0), ("I4", 4096.0), ("NIF", -1.0), ("IF", 1.0)):
         act(full(n), full("IB"), F.Copy, scale=v)
     act(full("MN", 2048), full("MX", 2048), F.Identity, bias=512.0, scale=-512.0)
     tc(full("WTF", 1), full("WT32", 1))
@@ -366,11 +373,15 @@ def rank_program(g, core, T, topo):
     act(full("PV", 512), full("VP32", 512), F.Copy)
     act(full("OV", 512), full("VO32", 512), F.Copy)
     send("v0", "OV", 0, 512)
-    send("v1", "PV", 0, 512)
-    send("h1", "LU00", 0, 256)
-    send("v2", "OV", 0, 512)
-    send("v3", "PV", 0, 512)
-    send("h0", "LU00", 0, 256)
+    act(("RT", 4096, RW), ("RT", 0, RW - 4096), F.Copy)
+
+    def bulk():
+        send("v1", "PV", 0, 512)
+        send("h1", "LU00", 0, 256)
+        send("v2", "OV", 0, 512)
+        send("v3", "PV", 0, 512)
+        send("h0", "LU00", 0, 256)
+
     for t, n in ((1, N1), (2, N2), (3, N3)):
         ts(n, K0, 256.0 * t, A.mult)
         act(full("NC%d" % t, 256), full("NF", 256), F.Identity, scale=K0, bias=n)
@@ -403,7 +414,8 @@ def rank_program(g, core, T, topo):
     def address(t, c):
         return [lambda: tt(full("AT%d" % c), li(t, c), ("pU", 128 * c, 128 * c + 128), A.mult),
                 lambda: ts(full("AS%d" % c), full("AT%d" % c), 5, A.arith_shift_right, 4095, A.bitwise_and),
-                lambda: ts(full("OF%d" % c), full("AS%d" % c), K37 if t == 0 else AK, A.add)]
+                lambda: (act(full("OF%d" % c), full("AS%d" % c), F.Identity, bias=K37 if t == 0 else AK) if "offsets%d" % c in ON_S else
+                         ts(full("OF%d" % c), full("AS%d" % c), K37 if t == 0 else AK, A.add))]
 
     def z_psum(t, c):
         o = ("pZ", 128 * c, 128 * c + 128)
@@ -435,13 +447,17 @@ def rank_program(g, core, T, topo):
         mm(("pU", 256, 272), full("NIF"), full("RR", 16), False, True)
 
     def place_out():
-        ts(full("PL", 16), ("pU", 256, 272), P16, A.add)
+        if "place_out" in ON_S:
+            act(full("PL", 16), ("pU", 256, 272), F.Identity, bias=P16)
+        else:
+            ts(full("PL", 16), ("pU", 256, 272), P16, A.add)
 
     def old(c):
         act(full("OLD%d" % c), ("RT", 2048 * c, 2048 * c + 2048), F.Identity, bias=-0.5, off=("PL", 8 * c, 8 * c + 8))
-        o = ("pZ", 256 + 128 * c, 384 + 128 * c)
-        mm(o, full("IH"), full("C10"), True, False)
-        mm(o, full("IH"), full("OLD%d" % c), False, True)
+        if "mean%d" % c not in ON_S:
+            o = (("pR", "pZ")[c], 256, 384)
+            mm(o, full("IH"), full("C10"), True, False)
+            mm(o, full("IH"), full("OLD%d" % c), False, True)
 
     def gather(c, a, b, q):
         y, of, w = ("Y%d" % c, 16 * a, 16 * b), ("OF%d" % c, a, b), ("RT", 0, RW)
@@ -477,21 +493,6 @@ def rank_program(g, core, T, topo):
         for k in ks:
             mm(("pC", 128 * c + 15 - k, 128 * c + 128, 16), ("B%d" % c, 128 * k, 128 * k + 128), full("QB" if k < KS[c] else "QBH", 8), False, last and k == ks[-1])
 
-    def compare(t, c, between):
-        bl = blocks(c)
-        diff_t(t, c, 0)
-        diff_t(t, c, 1)
-        for i in range(len(bl)):
-            sign_s(c, i)
-            if i + 2 < len(bl):
-                diff_t(t, c, i + 2)
-            ks = list(range(*bl[i]))
-            if i == len(bl) - 2:
-                ks = list(range(KS[c])) + ks
-            beats(c, ks, i == 0, i == len(bl) - 1)
-            for f in between.get(i, []):
-                f()
-
     def scan(c, hi, a=0, b=H):
         o, y = (("HI%d" if hi else "LO%d") % c, 16 * a, 16 * b), ("Y%d" % c, 16 * a, 16 * b)
         m = ("MX" if hi else "MN", 16 * a, 16 * b)
@@ -519,7 +520,10 @@ def rank_program(g, core, T, topo):
         mm(("pC", 256, 264), full("I4"), k, False, True)
 
     def list_n(c):
-        tc(full("LN%d" % c, 8), ("pC", 256, 264))
+        if "list_n%d" % c in ON_S:
+            act(full("LN%d" % c, 8), ("pC", 256, 264), F.Copy)
+        else:
+            tc(full("LN%d" % c, 8), ("pC", 256, 264))
 
     def pick_hi(c):
         act(full("HG%d" % c), full("HI%d" % c, 2048), F.Identity, bias=512.0 - 0.125, off=full("LK%d" % c, 8))
@@ -539,14 +543,20 @@ def rank_program(g, core, T, topo):
         send("l%d%d" % (t + 1, c), *l)
 
     def mean(t, c):
-        tt(full("RZ%d" % c), ("pZ", 256 + 128 * c, 384 + 128 * c), full("ZO%d%d" % (t + 1, c)), A.add)
+        if "mean%d" % c in ON_S:
+            o = ("pW", 384, 512)
+            mm(o, full("IH"), full("OLD%d" % c), True, False)
+            mm(o, full("IF"), full("ZO%d%d" % (t + 1, c)), False, True)
+            act(full("RZ%d" % c), o, F.Identity, bias=-512.0)
+        else:
+            tt(full("RZ%d" % c), (("pR", "pZ")[c], 256, 384), full("ZO%d%d" % (t + 1, c)), A.add)
 
     def scatter(c):
         win, off = ("RT", 2048 * c, 2048 * c + 2048), ("PL", 8 * c, 8 * c + 8)
         op("v", g.vector.tensor_copy, dict(out=ind(win, off), in_=ap(full("RZ%d" % c))), [off, rg(full("RZ%d" % c))], [win])
 
     def behind():
-        act(("RT", 4096, RW), ("RT", 0, RW - 4096), F.Copy)
+        dma("d", T.RT[:, 4096:RW], T.RT[:, 0:RW - 4096], [("RT", 0, RW - 4096)], [("RT", 4096, RW)])
 
     def count():
         act(full("SG", 16), ("PS", 15, 256, 16), F.Sign, bias=58000.0, accum=full("ACC", 1))
@@ -586,117 +596,89 @@ def rank_program(g, core, T, topo):
         op("s", g.scalar.activation, dict(out=T.YKS[:, 16 * a:16 * b], in_=T.pW[0:8, 0:w], func=F.Identity, bias=-129.0), [("pW", 0, w)], [("YKS", 16 * a, 16 * b)])
         dma("d", T.yk[:, 16 * a:16 * b], T.YKS[:, 16 * a:16 * b], [("YKS", 16 * a, 16 * b)], [("yk", 16 * a, 16 * b)])
 
-    def turn(t):
-        last = t == TURNS - 1
-        z_psum(t, 0)
-        key_t(t, 0)
-        if not last:
-            place_t(t, 0)
-        gather(0, 0, GS[0], "s")
-        gather(0, GS[0], H, "v")
-        key_s(0)
-        if not last:
-            place_s(0)
-        compare_v(0)
-        scan(0, True)
-        compare(t, 0, {})
-        u_sum(t, 1)
-        u_mod(t, 1)
-        ad = address(t, 1)
-        verdict(0)
-        spread(0)
-        ad[0]()
-        key_t(t, 1)
-        key_s(1)
-        list_k(0)
-        ad[1]()
-        kappa(t, 0)
-        ad[2]()
-        pick_hi(0)
-        list_n(0)
-        if not last:
-            place_t(t, 1)
-            place_s(1)
-            place_sum()
-        scan(0, False)
-        if t == 0:
-            table((0, 0))
-        gather(1, 0, GS[1], "s")
-        z_psum(t, 1)
-        new_z(t, 0)
-        views(t, 0)
-        if last:
-            send("y30", "KO", 48, 56)
-            send("w", "LI30", 0, 256)
-        gather(1, GS[1], H, "v")
-        if last:
-            compare_v(1)
-            scan(1, True)
-            compare(t, 1, {})
-            verdict(1)
-            spread(1)
-            list_k(1)
-            kappa(t, 1)
-            pick_hi(1)
-            send("y31", "KO", 56, 64)
-            list_n(1)
-            views(t, 1)
-            scan(1, False)
-            new_z(t, 1)
-            return
-        place_out()
-        old(0)
-        compare_v(1)
-        mean(t, 0)
-        scan(1, True)
-        compare(t, 1, {})
-        old(1)
-        verdict(1)
-        spread(1)
-        count()
-        scatter(0)
-        u_sum(t + 1, 0)
-        u_mod(t + 1, 0)
-        ad = address(t + 1, 0)
-        list_k(1)
-        pick_hi(1)
-        kappa(t, 1)
-        behind()
-        scan(1, False)
-        new_z(t, 1)
-        list_n(1)
-        count_a()
-        mean(t, 1)
-        views(t, 1)
-        scatter(1)
-        ad[0]()
-        count_b()
-        ad[1]()
-        ad[2]()
-        table((t, 1))
-        table((t + 1, 0))
+    def count_block(c, i):
+        bl = blocks(c)
+        ks = list(range(*bl[i]))
+        if i == len(bl) - 2:
+            ks = list(range(KS[c])) + ks
+        beats(c, ks, i == 0, i == len(bl) - 1)
+
+    def history(t):
         if t < 2:
             send("h%d" % (t + 2), "LU%d0" % (t + 1), 0, 256)
         send("y%d" % t, "KO", 16 * t, 16 * t + 16)
 
-    u_sum(0, 0)
-    u_mod(0, 0)
-    for f in address(0, 0):
-        f()
-    for t in range(TURNS):
-        turn(t)
+    def views_out():
+        mm(("pW", 0, 256), full("SH1"), full("L3I", 256), True, False)
+        mm1(("pW", 0, 256), full("ROW0"), full("NC3", 256), False, True)
+        act(full("YOS", 256), ("pW", 0, 256), F.Copy)
+        dma("d", T.yo[:], T.YOS[:], [full("YOS", 256)], [("yo", 0, 256)])
 
-    mm(("pC", 0, 256), full("SH1"), full("L3I", 256), True, False)
-    mm1(("pC", 0, 256), full("ROW0"), full("NC3", 256), False, True)
-    act(full("YOS", 256), ("pC", 0, 256), F.Copy)
-    dma("d", T.yo[:], T.YOS[:], [full("YOS", 256)], [("yo", 0, 256)])
-    verdicts_out(0, 32)
-    verdicts_out(32, 64)
-    for c in range(2):
+    def chunk_out(c, qp, qz):
         a, b = 128 * c, 128 * c + 128
-        dma("d", T.yp[:, a:b], T.EF[:, a:b], [("EF", a, b)], [("yp", a, b)])
-        dma("s", T.yz[:, a:b], T.ZF[:, a:b], [("ZF", a, b)], [("yz", a, b)])
-    used["ls"] = state["ls"]
+        dma(qp, T.yp[:, a:b], T.EF[:, a:b], [("EF", a, b)], [("yp", a, b)])
+        dma(qz, T.yz[:, a:b], T.ZF[:, a:b], [("ZF", a, b)], [("yz", a, b)])
+
+    def steps(t):
+        last = t == TURNS - 1
+        s = {}
+        for c in range(2):
+            n = str(c)
+            s["gather_v" + n] = lambda c=c: gather(c, GS[c], H, "v")
+            s["compare_v" + n] = lambda c=c: compare_v(c)
+            for i, (a, b) in enumerate(zip(HC[c][:-1], HC[c][1:])):
+                s["hi%d%s" % (c, "abc"[i])] = lambda c=c, a=a, b=b: scan(c, True, a, b)
+            for i, (a, b) in enumerate(zip(LC[c][:-1], LC[c][1:])):
+                s["lo%d%s" % (c, "abc"[i])] = lambda c=c, a=a, b=b: scan(c, False, a, b)
+            for i in range(len(blocks(c))):
+                s["diff%d%d" % (c, i)] = lambda c=c, i=i: diff_t(t, c, i)
+                s["sign%d%d" % (c, i)] = lambda c=c, i=i: sign_s(c, i)
+                s["beats%d%d" % (c, i)] = lambda c=c, i=i: count_block(c, i)
+            for name, f in (("verdict", verdict), ("spread", spread), ("list_k", list_k), ("pick_hi", pick_hi), ("list_n", list_n)):
+                s[name + n] = lambda c=c, f=f: f(c)
+            for name, f in (("kappa", kappa), ("new_z", new_z), ("views", views)):
+                s[name + n] = lambda c=c, f=f: f(t, c)
+            if not last:
+                s["old" + n] = lambda c=c: old(c)
+                s["mean" + n] = lambda c=c: mean(t, c)
+                s["scatter" + n] = lambda c=c: scatter(c)
+        s["gather_s0"] = lambda: gather(0, 0, GS[0], "s")
+        cut = (0,) + CUTS + (GS[1],)
+        for i in range(3):
+            s["gather_s1" + "abc"[i]] = lambda i=i: gather(1, cut[i], cut[i + 1], "s")
+        for n, (tn, c) in (("%s1", (t, 1)), ("n_%s", (t + 1, 0))):
+            if tn < TURNS:
+                for name, f in (("u_sum", u_sum), ("u_mod", u_mod), ("key_t", key_t), ("z_psum", z_psum)):
+                    s[n % name] = lambda tn=tn, c=c, f=f: f(tn, c)
+                s[n % "key_s"] = lambda c=c: key_s(c)
+                for name, f in zip(("product", "shift", "offsets"), address(tn, c)):
+                    s[n % name] = f
+                if tn < TURNS - 1:
+                    s[n % "place_t"] = lambda tn=tn, c=c: place_t(tn, c)
+                    s[n % "place_s"] = lambda c=c: place_s(c)
+        if not last:
+            s.update(place_sum=place_sum, place_out=place_out, behind=behind, count=count, count_a=count_a, count_b=count_b,
+                     table_a=lambda: table((t, 1)), table_b=lambda: table((t + 1, 0)), history=lambda: history(t))
+        else:
+            s.update(last0=lambda: send("y30", "KO", 48, 56), last1=lambda: send("y31", "KO", 56, 64), last_l=lambda: send("w", "LI30", 0, 256),
+                     out_k0=lambda: verdicts_out(0, 32), out_k1=lambda: verdicts_out(32, 48), out_o=views_out, out_c0=lambda: chunk_out(0, "d", "d"))
+        if t == 0:
+            s.update(table_0=lambda: table((0, 0)), bulk=bulk)
+        return s
+
+    first = steps(-1)
+    for n in ("u_sum", "u_mod", "product", "shift", "offsets", "key_t", "key_s", "place_t", "place_s", "z_psum"):
+        first["n_" + n]()
+    for t in range(TURNS):
+        s = steps(t)
+        for n in ORDER:
+            if n in s:
+                s.pop(n)()
+        assert not s
+
+    verdicts_out(48, 64)
+    chunk_out(1, "d", "s")
+    used.update(state["sent"])
     for s in sorted(used):
         if known["g"].get(s, 0) < used[s]:
             g.wait_ge(T.sem[s], used[s])

@@ -1,18 +1,20 @@
 from concourse.mybir import AluOpType as A, ActivationFunctionType as F
 
-N, TURNS, H = 8, 4, 128
+N, TURNS = 8, 4
+CH = (0, 128, 256)
 RW = 4096 + 816
 EARLY = 1536
-GS = (64, 80)
-CUTS = (32, 56)
-HC = ((0, 64, 128), (0, 56, 80, 128))
-LC = ((0, 64, 96, 128), (0, 56, 80, 128))
-ON_S = ("mean0", "place_out", "list_n0", "list_n1")
-ORDER = """gather_s0 out_k0 gather_v0 diff00 lo0c hi0a compare_v0 sign00 diff01 sign01 diff02 u_sum1 lo0b beats00 u_mod1 diff03 sign02 sign03 place_t1 bulk lo0a product1 shift1 diff13 offsets1 beats01 place_s1 beats02 beats03 verdict0 z_psum1 gather_s1c table_0 spread0 hi0b gather_s1b out_k1 place_sum list_k0 gather_v1 kappa0 pick_hi0 list_n0 new_z0 key_t1 gather_s1a lo1b table_a diff10 views0 sign13 last_l compare_v1 hi1b sign10 hi1c diff11 key_s1 beats10 place_out sign11 diff12 sign12 old0 hi1a last0 lo1a beats11 beats13 beats12 mean0 verdict1 spread1 out_c0 count scatter0 kappa1 old1 list_n1 n_place_t behind list_k1 n_u_sum pick_hi1 n_place_s last1 lo1c views1 new_z1 count_a n_u_mod mean1 table_b history n_z_psum scatter1 out_o n_key_t n_key_s n_product count_b n_shift n_offsets""".split()
-KS = (3, 5)
-FIRST = 2
+GS = ((64,), (24, 48, 72))
+KB = ((4, 7, 11, 15), (5, 7, 11, 15))
+ON_S = ("mean0", "offsets0", "count", "list_k0", "list_k1")
+FIRST = """place_t0 gather_v0 gather_s0a u_sum1 u_mod1 diff00 u_off1 compare_v0 diff01 place_s0 sign00 sign01 diff02 z_psum1 place_t1 beats00 product1 sign02 hi0b shift1 key_t1 lo0b offsets1 beats01 lo0a place_s1 gather_s1b bulk gather_s1a gather_s1c beats02 verdict0 hi0a spread0 lists0 place_sum list_k0 place_up pick_hi0 kappa0 place_down table_0 named0 gather_v1 diff10 place_mod table_0s diff11 new_z0 compare_v1 list_n0 place_out sign10 views0 diff12 beats10 key_s1 sign11 sign12 old0 beats11 beats12 lo1b hi1a old1 lo1a verdict1 count spread1 old_t0 mean0 hi1b scatter0 lists1 old_t1 list_k1 table_a kappa1 count_t pick_hi1 table_as count_a named1 n_u_sum behind n_u_mod count_b table_b new_z1 list_n1 n_u_off mean1 scatter1 n_key_t n_product table_bs n_shift views1 history n_key_s n_offsets n_z_psum""".split()
+ORDER = """gather_v0 gather_s0a table_a diff00 diff01 table_as place_t0 lo0b compare_v0 sign00 sign01 diff02 beats00 sign02 lo0a beats01 hi0b hi0a u_sum1 beats02 place_s0 u_mod1 place_t1 u_off1 verdict0 spread0 product1 place_s1 place_sum place_up lists0 shift1 kappa0 list_k0 offsets1 named0 place_down pick_hi0 list_n0 place_mod new_z0 key_t1 z_psum1 views0 gather_v1 gather_s1c gather_s1a gather_s1b place_out diff10 key_s1 diff11 old0 sign10 old_t0 sign11 diff12 compare_v1 hi1a hi1b mean0 scatter0 beats10 sign12 old1 beats11 beats12 verdict1 count spread1 table_b lo1b lo1a lists1 count_t behind list_k1 kappa1 n_u_sum named1 pick_hi1 list_n1 n_u_mod n_z_psum n_u_off old_t1 new_z1 n_key_t table_bs views1 n_product mean1 history n_shift count_a n_key_s scatter1 count_b n_offsets""".split()
+LAST = """gather_v0 gather_s0a hi0b diff00 diff01 lo0b lo0a compare_v0 sign00 hi0a sign01 beats00 out_k0 u_sum1 diff02 u_mod1 sign02 u_off1 last_l product1 shift1 out_k1 offsets1 beats01 gather_s1c gather_s1a beats02 verdict0 spread0 key_t1 lists0 kappa0 gather_s1b named0 list_n0 z_psum1 list_k0 gather_v1 hi1b key_s1 last0 diff10 views0 compare_v1 diff11 sign10 pick_hi0 new_z0 diff12 sign11 sign12 out_o beats10 beats11 hi1a beats12 verdict1 spread1 lists1 kappa1 lo1b lo1a list_k1 named1 list_n1 last1 pick_hi1 out_c0 views1 new_z1""".split()
 M31, M27, M23 = 1.5 * 2.0 ** 31, 1.5 * 2.0 ** 27, 1.5 * 2.0 ** 23
 BIG = 2.0 ** 17
+NCH = len(CH) - 1
+SIZE = [CH[c + 1] - CH[c] for c in range(NCH)]
+PIECE = 16 * max(max(GS[c][-1], SIZE[c] - GS[c][-1]) for c in range(NCH))
 
 SCRATCH = {
     "RT": ("sbuf", [128, RW], "bfloat16"),
@@ -22,16 +24,16 @@ SCRATCH = {
     "PV": ("sbuf", [128, 512], "float16"), "OV": ("sbuf", [128, 512], "float16"),
     "HL1": ("sbuf", [128, 256], "float16"), "HL3": ("sbuf", [128, 256], "float16"),
     "HB2": ("sbuf", [128, 256], "float16"), "HB3": ("sbuf", [128, 256], "float16"), "L3I": ("sbuf", [128, 256], "float16"),
-    "MX": ("sbuf", [128, 2048], "bfloat16"), "MN": ("sbuf", [128, 2048], "bfloat16"),
+    "MX": ("sbuf", [128, PIECE], "bfloat16"), "MN": ("sbuf", [128, PIECE], "bfloat16"),
     "DIF": ("sbuf", [128, 128], "float32"), "DB": ("sbuf", [128, 128], "float32"), "JI": ("sbuf", [128, 128], "int32"),
     "JS": ("sbuf", [128, 128], "int32"), "JM": ("sbuf", [128, 128], "int32"), "PI": ("sbuf", [128, 1], "int32"),
     "PG": ("sbuf", [128, 1], "int32"), "PK": ("sbuf", [128, 1], "int32"), "COL": ("sbuf", [128, 16], "float32"),
     "BLK": ("sbuf", [128, 128], "bfloat16"), "T1": ("sbuf", [128, 128], "bfloat16"), "EPI": ("sbuf", [128, 128], "float32"),
     "IB": ("sbuf", [128, 128], "bfloat16"), "I4": ("sbuf", [128, 128], "bfloat16"), "IH": ("sbuf", [128, 128], "float16"),
     "NH": ("sbuf", [128, 128], "float16"), "NI4": ("sbuf", [128, 128], "float16"), "NIF": ("sbuf", [128, 128], "float32"),
-    "IF": ("sbuf", [128, 128], "float16"), "WB": ("sbuf", [128, 128], "float16"), "REV": ("sbuf", [128, 128], "float16"), "KC": ("sbuf", [128, 128], "float16"),
-    "SH1": ("sbuf", [128, 128], "float16"), "SH2": ("sbuf", [128, 128], "float16"), "EP": ("sbuf", [128, 128], "bfloat16"),
-    "MK": ("sbuf", [128, 128], "float32"), "NM": ("sbuf", [128, 128], "bfloat16"),
+    "IF": ("sbuf", [128, 128], "float16"), "WB": ("sbuf", [128, 128], "float16"), "REV": ("sbuf", [128, 128], "float16"),
+    "KC": ("sbuf", [128, 128], "float16"), "SH1": ("sbuf", [128, 128], "float16"), "SH2": ("sbuf", [128, 128], "float16"),
+    "EP": ("sbuf", [128, 128], "bfloat16"), "MK": ("sbuf", [128, 128], "float32"), "NM": ("sbuf", [128, 128], "bfloat16"),
     "QF": ("sbuf", [128, 32], "float32"), "QB": ("sbuf", [128, 8], "bfloat16"), "QBH": ("sbuf", [128, 8], "bfloat16"),
     "RC": ("sbuf", [128, 24], "float16"), "PC": ("sbuf", [128, 16], "float16"), "CA": ("sbuf", [128, 2], "float16"),
     "H5": ("sbuf", [128, 128], "float32"), "ROW0": ("sbuf", [128, 128], "float16"), "ROW1": ("sbuf", [128, 128], "float16"),
@@ -39,8 +41,9 @@ SCRATCH = {
     "C5": ("sbuf", [128, 128], "float16"), "C10": ("sbuf", [128, 128], "float16"),
     "NF": ("sbuf", [128, 256], "float32"), "NC": ("sbuf", [128, 1024], "float16"),
     "ELI": ("sbuf", [128, 8], "int32"), "EL": ("sbuf", [128, 8], "uint16"),
-    "RR": ("sbuf", [128, 32], "float32"), "PL": ("sbuf", [128, 16], "uint16"),
-    "SG": ("sbuf", [128, 16], "bfloat16"), "ACC": ("sbuf", [128, 1], "float32"),
+    "RR": ("sbuf", [128, 32], "float32"), "ZU": ("sbuf", [128, 256], "float32"),
+    "PL": ("sbuf", [128, 16], "uint16"), "LK": ("sbuf", [128, 16], "uint16"), "LN": ("sbuf", [128, 16], "uint16"),
+    "SG": ("sbuf", [128, 8 * NCH], "bfloat16"), "ACC": ("sbuf", [128, 1], "float32"), "AQ": ("sbuf", [128, 1], "int32"),
     "YKS": ("sbuf", [8, 1024], "float32"), "YOS": ("sbuf", [128, 256], "float32"),
     "KO": ("sbuf", [128, 64], "bfloat16"), "KI": ("sbuf", [128, 64], "bfloat16"),
     "ZL": ("sbuf", [128, 256], "bfloat16"), "ZF": ("sbuf", [128, 256], "bfloat16"),
@@ -53,31 +56,28 @@ for _n in ("pU", "pZ", "pD0", "pD1", "pC", "pR", "pW", "pX"):
 for _t in range(4):
     SCRATCH["VI%d" % _t] = ("sbuf", [128, 512], "float16")
     SCRATCH["TAB%d" % _t] = ("sbuf", [128, 512 + 256 * _t], "float32")
-ALIAS = {}
-for _t in range(5):
-    ALIAS["NC%d" % _t] = ("NC", 256 * _t)
-    for _c in range(2):
-        for _n in ("ZI", "LI", "ZO", "LU"):
-            ALIAS["%s%d%d" % (_n, _t, _c)] = (_n, 256 * _t + 128 * _c)
-for _n, _w, _d in (("Y", 2048, "bfloat16"), ("B", 2048, "bfloat16"), ("HI", 2048, "bfloat16"), ("LO", 2048, "bfloat16"),
-                   ("U2", 128, "float16"), ("AT", 128, "int32"), ("AS", 128, "int32"), ("OF", 128, "uint16"),
-                   ("BT", 128, "float32"), ("PS", 128, "float32"), ("KX", 128, "float32"), ("ZU", 128, "float32"),
-                   ("LK", 8, "uint16"), ("LN", 8, "uint16"), ("HG", 128, "float32"), ("OLD", 128, "float16"), ("RZ", 128, "int32"),
-                   ("C8", 128, "float16")):
-    SCRATCH[_n] = ("sbuf", [128, 2 * _w], _d)
-    for _c in range(2):
-        ALIAS["%s%d" % (_n, _c)] = (_n, _w * _c)
+for _n, _d in (("Y", "bfloat16"), ("B", "bfloat16"), ("HI", "bfloat16"), ("LO", "bfloat16")):
+    SCRATCH[_n] = ("sbuf", [128, 4096], _d)
+for _n, _d in (("U2", "float16"), ("AT", "int32"), ("AS", "int32"), ("OF", "uint16"), ("HG", "float32"), ("OLD", "float16"), ("RZ", "int32")):
+    SCRATCH[_n] = ("sbuf", [128, 256], _d)
+for _n, _d in (("BT", "float32"), ("PS", "float32"), ("KX", "float32"), ("C8", "float16")):
+    SCRATCH[_n] = ("sbuf", [128, 128 * NCH], _d)
 
 SEMAPHORES = (["qg", "qt", "qv", "qs", "ls", "l0"] + ["d%d" % i for i in range(28)]
-              + ["%s%d%d" % (n, t, c) for n in "zl" for t in range(5) for c in range(2)] + ["v%d" % t for t in range(4)]
-              + ["h%d" % t for t in range(4)] + ["y0", "y1", "y2", "y30", "y31", "w"])
+              + ["%s%d%d" % (n, t, c) for n in "zl" for t in range(5) for c in range(NCH)] + ["v%d" % t for t in range(4)]
+              + ["h%d" % t for t in range(4)] + ["y0", "y1", "y2", "w"] + ["y3%d" % c for c in range(NCH)])
 
 
-def real(o):
-    if o[0] in ALIAS:
-        n, a = ALIAS[o[0]]
-        return (n, o[1] + a, o[2] + a) + tuple(o[3:])
-    return o
+def games(buf, c, t=0, w=1):
+    return (buf, w * (256 * t + CH[c]), w * (256 * t + CH[c + 1]))
+
+
+def listed(buf, c, t=0):
+    return (buf, 16 * t + CH[c] // 16, 16 * t + CH[c + 1] // 16)
+
+
+def wide(buf, c):
+    return (buf, 128 * c, 128 * c + 128)
 
 
 def bits(m):
@@ -96,50 +96,39 @@ def messages(core, T, topo):
     r = T.rank_of(core)
     out = []
 
-    def add(sem, off, buf, a, b, n, near):
+    def add(sem, off, where, n, near):
         dst = T.cores[(r + off) % N]
-        buf, a, b = real((buf, a, b))
-        out.append((sem, dst, relay_of(core, dst, n, near, topo), buf, a, b, n))
-    for c in range(2):
-        add("z0%d" % c, 1, "ZI0%d" % c, 0, 128, 0, True)
-        add("l0%d" % c, 1, "LI0%d" % c, 0, 128, 1, True)
-    add("v0", 1, "VI0", 0, 512, 0, False)
-    add("v1", 2, "VI1", 0, 512, 0, False)
-    add("v2", 3, "VI2", 0, 512, 1, False)
-    add("v3", 4, "VI3", 0, 512, 0, False)
-    add("h1", 2, "HL1", 0, 256, 0, False)
-    add("h0", 4, "HL3", 0, 256, 0, False)
+        out.append((sem, dst, relay_of(core, dst, n, near, topo)) + where)
     for t in range(4):
-        for c in range(2):
-            if t < 3:
-                add("z%d%d" % (t + 1, c), 1, "ZI%d%d" % (t + 1, c), 0, 128, 0, True)
-                add("l%d%d" % (t + 1, c), 1, "LI%d%d" % (t + 1, c), 0, 128, 1, True)
-            else:
-                add("z4%d" % c, -4, "ZF", 128 * c, 128 * c + 128, 0, True)
-                add("l4%d" % c, -4, "EF", 128 * c, 128 * c + 128, 0, True)
-                add("y3%d" % c, -4, "KI", 48 + 8 * c, 56 + 8 * c, 0, False)
+        for c in range(NCH):
+            add("z%d%d" % (t, c), 1, games("ZI", c, t), 0, True)
+            add("l%d%d" % (t, c), 1, games("LI", c, t), 1, True)
+    add("v0", 1, ("VI0", 0, 512), 0, False)
+    add("v1", 2, ("VI1", 0, 512), 0, False)
+    add("v2", 3, ("VI2", 0, 512), 1, False)
+    add("v3", 4, ("VI3", 0, 512), 0, False)
+    add("h1", 2, ("HL1", 0, 256), 0, False)
+    add("h0", 4, ("HL3", 0, 256), 0, False)
+    for t in range(3):
         if t < 2:
-            add("h%d" % (t + 2), 2, "HB%d" % (t + 2), 0, 256, 0, False)
-        if t < 3:
-            add("y%d" % t, -1 - t, "KI", 16 * t, 16 * t + 16, 0, False)
-    add("w", -4, "L3I", 0, 256, 0, False)
+            add("h%d" % (t + 2), 2, ("HB%d" % (t + 2), 0, 256), 0, False)
+        add("y%d" % t, -1 - t, ("KI", 16 * t, 16 * t + 16), 0, False)
+    for c in range(NCH):
+        add("z4%d" % c, -4, games("ZF", c), 0, True)
+        add("l4%d" % c, -4, games("EF", c), 0, True)
+        add("y3%d" % c, -4, listed("KI", c, 3), 0, False)
+    add("w", -4, ("L3I", 0, 256), 0, False)
     return out
-
-
-def mask_of(src, dst, n, topo):
-    e = topo.engines(src, dst)
-    a = (8 * n) % len(e)
-    return sum(1 << x for x in e[a:a + 8])
 
 
 def hand_on(g, core, T, topo):
     own = [x for x in topo.cores_of(core) if T.rank_of(x) is not None]
     n = 0
     for rc in own:
-        for sem, dst, rel, buf, a, b, es in messages(rc, T, topo):
+        for sem, dst, rel, buf, a, b in messages(rc, T, topo):
             if rel == core:
-                g.wait_ge(T.sem[sem], bits(mask_of(rc, core, es, topo)))
-                m = mask_of(core, dst, es, topo)
+                g.wait_ge(T.sem[sem], bits(topo.mask(rc, core)))
+                m = topo.mask(core, dst)
                 rid, pid = topo.addr(dst, core)
                 g.remote_dma(T[buf][:, a:b], T[buf][:, a:b], T.sem[sem], T.sem.ls, pid, rid, m)
                 n += bits(m)
@@ -215,31 +204,26 @@ def rank_program(g, core, T, topo):
 
     for off in range(1, N):
         src = T.cores[(rank + off) % N]
-        for sem, dst, rel, bf, a, b, es in messages(src, T, topo):
+        for sem, dst, rel, bf, a, b in messages(src, T, topo):
             if dst == core:
-                used[sem] = bits(mask_of(rel if rel is not None else src, core, es, topo))
+                used[sem] = bits(topo.mask(rel if rel is not None else src, core))
                 note("x", [], [(bf, a, b)], (sem, used[sem], {}))
 
     plan = {m[0]: m for m in messages(core, T, topo)}
 
     def send(sem, buf, a, b, left="ls"):
-        _, dst, rel, ob, oa, oe, es = plan[sem]
-        buf, a, b = real((buf, a, b))
+        _, dst, rel, ob, oa, oe = plan[sem]
         deps("g", [(buf, a, b)], [])
         to = dst if rel is None else rel
-        m = mask_of(core, to, es, topo)
+        m = topo.mask(core, to)
         rid, pid = topo.addr(to, core)
         g.remote_dma(T[ob][:, oa:oe], T[buf][:, a:b], T.sem[sem], T.sem[left], pid, rid, m)
         state["sent"][left] += bits(m)
 
-    def ap(o):
-        o = real(o)
+    def ap(o, p=128):
         if len(o) == 4:
-            return T[o[0]][:, o[1]:o[2]:o[3]]
-        return T[o[0]][:, o[1]:o[2]]
-
-    def rg(o):
-        return real(o)[:3]
+            return T[o[0]][0:p, o[1]:o[2]:o[3]]
+        return T[o[0]][0:p, o[1]:o[2]]
 
     def ind(win, off):
         return ap(win).indirect(ap(off))
@@ -247,48 +231,46 @@ def rank_program(g, core, T, topo):
     def full(n, w=128):
         return (n, 0, w)
 
-    def mm(out, l, r, start, stop):
-        op("t", g.tensor.matmul, dict(out=ap(out), lhsT=ap(l), rhs=ap(r), start=start, stop=stop), [rg(l), rg(r)], [rg(out)])
-
-    def mm1(out, l, r, start, stop):
-        l, r = real(l), real(r)
-        op("t", g.tensor.matmul, dict(out=ap(out), lhsT=T[l[0]][0:1, l[1]:l[2]], rhs=T[r[0]][0:1, r[1]:r[2]], start=start, stop=stop), [l, r], [rg(out)])
+    def mm(out, l, r, start, stop, k=128):
+        op("t", g.tensor.matmul, dict(out=ap(out, l[2] - l[1]), lhsT=ap(l, k), rhs=ap(r, k), start=start, stop=stop), [l[:3], r[:3]], [out[:3]])
 
     def tt(out, a, b, o):
-        op("v", g.vector.tensor_tensor, dict(out=ap(out), in0=ap(a), in1=ap(b), op=o), [rg(a), rg(b)], [rg(out)])
+        op("v", g.vector.tensor_tensor, dict(out=ap(out), in0=ap(a), in1=ap(b), op=o), [a[:3], b[:3]], [out[:3]])
 
     def tti(out, win, off, b, o):
-        op("v", g.vector.tensor_tensor, dict(out=ap(out), in0=ind(win, off), in1=ap(b), op=o), [rg(win), rg(off), rg(b)], [rg(out)])
+        op("v", g.vector.tensor_tensor, dict(out=ap(out), in0=ind(win, off), in1=ap(b), op=o), [win, off, b], [out])
 
     def columns(*xs):
-        return [rg(x) for x in xs if isinstance(x, tuple)], [ap(x) if isinstance(x, tuple) else x for x in xs]
+        return [x for x in xs if isinstance(x, tuple)], [ap(x) if isinstance(x, tuple) else x for x in xs]
 
     def ts(out, a, s1, o1, s2=None, o2=None):
         rd, sc = columns(s1, s2)
         d = dict(out=ap(out), in0=ap(a), scalar1=sc[0], scalar2=sc[1], op0=o1)
         if o2 is not None:
             d["op1"] = o2
-        op("v", g.vector.tensor_scalar, d, rd + [rg(a)], [rg(out)])
+        op("v", g.vector.tensor_scalar, d, rd + [a[:3]], [out[:3]])
 
     def tc(out, a):
-        op("v", g.vector.tensor_copy, dict(out=ap(out), in_=ap(a)), [rg(a)], [rg(out)])
+        op("v", g.vector.tensor_copy, dict(out=ap(out), in_=ap(a)), [a], [out])
 
     def ms(out, v, rows=None):
-        o = real(out)
-        op("v", g.vector.memset, dict(ap=ap(out) if rows is None else T[o[0]][rows[0]:rows[1], o[1]:o[2]], constant=v), [], [rg(out)])
+        op("v", g.vector.memset, dict(ap=ap(out) if rows is None else T[out[0]][rows[0]:rows[1], out[1]:out[2]], constant=v), [], [out[:3]])
 
-    def act(out, a, f, bias=None, scale=None, accum=None, off=None):
+    def scan(out, d0, d1, o0, o1, p=128):
+        op("v", g.vector.tensor_tensor_scan, dict(out=ap(out, p), data0=ap(d0, p), data1=ap(d1, p), initial=0.0, op0=o0, op1=o1), [d0, d1], [out])
+
+    def act(out, a, f, bias=None, scale=None, accum=None, off=None, p=128):
         rd, sc = columns(bias, scale)
-        d = dict(out=ap(out), in_=ap(a) if off is None else ind(a, off), func=f)
-        wr = [rg(out)]
+        d = dict(out=ap(out, p), in_=ap(a, p) if off is None else ind(a, off), func=f)
+        wr = [out]
         if bias is not None:
             d["bias"] = sc[0]
         if scale is not None:
             d["scale"] = sc[1]
         if accum is not None:
             d["accum_out"] = ap(accum)
-            wr.append(rg(accum))
-        op("s", g.scalar.activation, d, rd + [rg(a)] + ([] if off is None else [rg(off)]), wr)
+            wr.append(accum)
+        op("s", g.scalar.activation, d, rd + [a[:3]] + ([] if off is None else [off]), wr)
 
     def iota(out, pattern, base, cm):
         big = dict(allow_small_or_imprecise_dtypes=True) if SCRATCH[out[0]][2] == "float32" else {}
@@ -307,267 +289,297 @@ def rank_program(g, core, T, topo):
     iota(full("ELI", 8), [[16, 8]], 15, 0)
     iota(full("EPI"), [[1, 16], [16, 8]], 0, -1)
 
-    GP, KK, PF, RV, K0, K37, K37A, MP, P16, RA, AK, N1, N2, N3 = [("COL", i, i + 1) for i in range(14)]
+    GP, KK, PF, RV, K0, K37, K37A, MP, P16, RA, AK, N1, N2, N3, P4 = [("COL", i, i + 1) for i in range(15)]
+    ms(full("MX", PIECE), 1.0)
     ts(full("PG", 1), full("PI", 1), 4, A.arith_shift_right)
     ts(full("PK", 1), full("PI", 1), 15, A.bitwise_and)
-    ts(full("JS"), full("JI"), 4, A.arith_shift_right)
+    ms(("MX", 0, PIECE, 16), 0.0)
     tc(GP, full("PG", 1))
     tc(KK, full("PK", 1))
     tc(PF, full("PI", 1))
     ts(full("IB"), full("DIF"), 0.0, A.is_equal)
-    ts(full("BLK"), full("JS"), GP, A.is_equal)
-    ts(K0, KK, 0.0, A.is_equal)
+    ts(full("JM"), full("JI"), 15, A.bitwise_and)
 
     ts(("ZO", 0, 256), full("Z0B", 256), 0.5, A.mult, 512.0, A.add)
-    send("z00", "ZO00", 0, 128, "l0")
-    tc(full("MV16", 16), full("MV32", 16))
-    for c in range(2):
-        lo, off = full("LU0%d" % c), ("MV16", 8 * c, 8 * c + 8)
-        op("v", g.vector.tensor_copy, dict(out=ap(lo), in_=ind(("VP32", 0, 512), off)), [("VP32", 0, 512), off], [rg(lo)])
-        send("l0%d" % c, *lo)
-        if c == 0:
-            send("z01", "ZO01", 0, 128)
-    g.sync.wait_ge(T.sem.l0, state["sent"]["l0"])
-    dma("d", T.VO32[:], T.vo[:], [], [("VO32", 0, 512)])
-    dma("d", T.RT[:, EARLY:4096], T.strat[:, EARLY:4096], [], [("RT", EARLY, 4096)])
-
-    ms(full("MX", 2048), 1.0)
-    ms(("MX", 0, 2048, 16), 0.0)
-    for n, v in (("IH", 0.5), ("NH", -0.5), ("NI4", -4096.0), ("I4", 4096.0), ("NIF", -1.0), ("IF", 1.0)):
-        act(full(n), full("IB"), F.Copy, scale=v)
-    act(full("MN", 2048), full("MX", 2048), F.Identity, bias=512.0, scale=-512.0)
-    tc(full("WTF", 1), full("WT32", 1))
-    ts(full("WB"), full("BLK"), full("WTF", 1), A.mult, 2.0, A.mult)
-    ms(full("ONE"), 1.0)
-    ms(full("ONB"), 1.0)
-    ms(full("C5"), -512.0)
-    ms(full("C10"), -1024.0)
-    for rows, v in (((0, 32), 2.0 ** 17), ((32, 64), 2.0 ** 7), ((64, 128), 0.5)):
-        ms(full("CB"), v, rows)
+    send("z00", *games("ZO", 0), "l0")
     ts(K37, KK, 37.0, A.mult)
-    ts(full("JM"), full("JI"), 15, A.bitwise_and)
     ts(RV, GP, 32.0, A.mult, PF, A.subtract)
     ts(full("KC"), full("JM"), 32.0, A.mult, 480.0, A.subtract)
     ts(full("MK"), full("JM"), KK, A.is_equal)
     ts(full("REV"), full("JI"), 15.0, A.subtract, RV, A.is_equal)
+    tc(full("MV16", 16), full("MV32", 16))
+    for c in range(NCH):
+        lo, off = games("LU", c), listed("MV16", c)
+        op("v", g.vector.tensor_copy, dict(out=ap(lo), in_=ind(("VP32", 0, 512), off)), [("VP32", 0, 512), off], [lo])
+        if c:
+            send("z0%d" % c, *games("ZO", c))
+        send("l0%d" % c, *lo)
+    g.sync.wait_ge(T.sem.l0, state["sent"]["l0"])
+    dma("d", T.VO32[:], T.vo[:], [], [("VO32", 0, 512)])
+    dma("d", T.RT[:, EARLY:4096], T.strat[:, EARLY:4096], [], [("RT", EARLY, 4096)])
+
+    ts(full("JS"), full("JI"), 4, A.arith_shift_right)
+    ts(K0, KK, 0.0, A.is_equal)
+    for n, v in (("ONE", 1.0), ("ONB", 1.0), ("C5", -512.0), ("C10", -1024.0)):
+        ms(full(n), v)
+    ts(full("BLK"), full("JS"), GP, A.is_equal)
+    tc(full("WTF", 1), full("WT32", 1))
+    ms(full("CB"), 2.0 ** 17, (0, 32))
+    act(full("MN", PIECE), full("MX", PIECE), F.Identity, bias=512.0, scale=-512.0)
+    for n, v in (("IH", 0.5), ("NH", -0.5), ("NI4", -4096.0), ("I4", 4096.0), ("NIF", -1.0), ("IF", 1.0)):
+        act(full(n), full("IB"), F.Copy, scale=v)
     act(full("NM"), full("MK"), F.Identity, bias=-2.0 ** 23, scale=2.0 ** 23)
+    act(full("PV", 512), full("VP32", 512), F.Copy)
+    act(("RT", 4096, RW), ("RT", 0, RW - 4096), F.Copy)
+    for t, n in enumerate((0.0, N1, N2, N3)):
+        if t:
+            ts(n, K0, 256.0 * t, A.mult)
+        act(("NC", 256 * t, 256 * t + 256), full("NF", 256), F.Identity, scale=K0, bias=n)
+    ts(full("WB"), full("BLK"), full("WTF", 1), A.mult, 2.0, A.mult)
+    ms(full("CB"), 2.0 ** 7, (32, 64))
     ts(full("QB", 8), ("JI", 0, 8), GP, A.is_equal, BIG, A.mult)
     ts(full("QBH", 8), ("JI", 0, 8), GP, A.is_equal, BIG / 2, A.mult)
-    for c in range(2):
-        ts(full("C8%d" % c), full("JM"), 15.5 - KS[c], A.is_gt, -8 * BIG / 128, A.mult)
-    ts(full("C8", 256), full("C8", 256), -2.5 * BIG / 128, A.add)
-    ms(("C8", 0, 256, 16), BIG / 128)
+    for c in range(NCH):
+        ts(wide("C8", c), full("JM"), 15.5 - KB[c][0], A.is_gt, -8 * BIG / 128, A.mult)
+    ms(full("CB"), 0.5, (64, 128))
+    if min(SIZE) < 128:
+        ms(full("PS", 128 * NCH), -65536.0)
+    ts(full("C8", 128 * NCH), full("C8", 128 * NCH), -2.5 * BIG / 128, A.add)
+    ts(full("T1"), full("BLK"), 1000.0, A.mult, 1000.0, A.subtract)
     tc(full("EL", 8), full("ELI", 8))
+    ms(("C8", 0, 128 * NCH, 16), BIG / 128)
     for a, v in ((0, -1.0 / 4096), (8, -1.0 / 4096), (16, 1.0)):
         ts(("QF", a, a + 8), ("JI", 0, 8), GP, A.is_equal, v, A.mult)
-    for a in (("RC", 0, 8), ("PC", 0, 8), ("PC", 8, 16)):
-        ts(a, ("JI", 0, 8), 2.0, A.mult)
+    ts(("RC", 0, 8), ("JI", 0, 8), 2.0, A.mult)
+    for c in range(NCH):
+        ts(listed("PC", c), ("JI", 0, SIZE[c] // 16), 2.0, A.mult)
     ms(("RC", 8, 16), 0.0)
     ms(("RC", 16, 24), -32.0 * 129)
     ts(MP, KK, 16.0, A.mult, M23, A.add)
     ts(P16, KK, 16.0, A.mult, 7.5, A.add)
-    ts(full("T1"), full("BLK"), 1000.0, A.mult, 1000.0, A.subtract)
+    ts(P4, KK, 16.0, A.mult, 0.4, A.add)
     tt(full("DB"), full("DIF"), full("T1"), A.add)
-    ts(full("SH1"), full("DB"), 1.0, A.is_equal)
-    act(full("NC0", 256), full("NF", 256), F.Copy, scale=K0)
-    act(full("PV", 512), full("VP32", 512), F.Copy)
-    act(full("OV", 512), full("VO32", 512), F.Copy)
-    send("v0", "OV", 0, 512)
-    act(("RT", 4096, RW), ("RT", 0, RW - 4096), F.Copy)
-
-    def bulk():
-        send("v1", "PV", 0, 512)
-        send("h1", "LU00", 0, 256)
-        send("v2", "OV", 0, 512)
-        send("v3", "PV", 0, 512)
-        send("h0", "LU00", 0, 256)
-
-    for t, n in ((1, N1), (2, N2), (3, N3)):
-        ts(n, K0, 256.0 * t, A.mult)
-        act(full("NC%d" % t, 256), full("NF", 256), F.Identity, scale=K0, bias=n)
     ms(full("H5"), 0.5)
     ms(full("CA", 2), -127.5 / 128)
+    ts(full("SH1"), full("DB"), 1.0, A.is_equal)
     ts(K37A, KK, 37.0, A.mult, 127.5, A.add)
     ts(full("SH2"), full("DB"), 2.0, A.is_equal)
     ts(full("ROW1"), full("JM"), 1.0, A.is_equal)
     ts(full("ROW0"), full("JM"), 0.0, A.is_equal)
     ts(full("EP"), full("EPI"), 0.0, A.is_equal)
+    act(full("OV", 512), full("VO32", 512), F.Copy)
+    send("v0", "OV", 0, 512)
 
-    def zi(t, c):
-        return full("ZI%d%d" % (t, c))
-
-    def li(t, c):
-        return full("LI%d%d" % (t, c))
+    def bulk():
+        send("v1", "PV", 0, 512)
+        send("h1", "LU", 0, 256)
+        send("v2", "OV", 0, 512)
+        send("v3", "PV", 0, 512)
+        send("h0", "LU", 0, 256)
 
     def u_sum(t, c):
-        mm(("pX", 256, 384), full("WB"), full("C5"), True, False)
-        mm(("pX", 256, 384), full("WB"), zi(t, c), False, True)
-        u = ("pU", 128 * c, 128 * c + 128)
-        mm(u, full("WB"), full("C5"), True, False)
-        mm(u, full("CB"), full("ONB"), False, False)
-        mm(u, full("WB"), zi(t, c), False, False)
+        n, z = SIZE[c], games("ZI", c, t)
+        mm(("pX", 256, 256 + n), full("WB"), full("C5", n), True, False)
+        mm(("pX", 256, 256 + n), full("WB"), z, False, True)
+        u = games("pU", c)
+        mm(u, full("WB"), full("C5", n), True, False)
+        mm(u, full("CB"), full("ONB", n), False, False)
+        mm(u, full("WB"), z, False, False)
 
     def u_mod(t, c):
-        act(full("U2%d" % c), ("pX", 256, 384), F.Identity, bias=1024.5 + 2.0 ** -13, scale=1.0 / 4096)
-        mm(("pU", 128 * c, 128 * c + 128), full("NI4"), full("U2%d" % c), False, True)
+        act(games("U2", c), ("pX", 256, 256 + SIZE[c]), F.Identity, bias=1024.5 + 2.0 ** -13, scale=1.0 / 4096)
 
-    def address(t, c):
-        return [lambda: tt(full("AT%d" % c), li(t, c), ("pU", 128 * c, 128 * c + 128), A.mult),
-                lambda: ts(full("AS%d" % c), full("AT%d" % c), 5, A.arith_shift_right, 4095, A.bitwise_and),
-                lambda: (act(full("OF%d" % c), full("AS%d" % c), F.Identity, bias=K37 if t == 0 else AK) if "offsets%d" % c in ON_S else
-                         ts(full("OF%d" % c), full("AS%d" % c), K37 if t == 0 else AK, A.add))]
+    def u_off(t, c):
+        mm(games("pU", c), full("NI4"), games("U2", c), False, True)
+
+    def product(t, c):
+        tt(games("AT", c), games("LI", c, t), games("pU", c), A.mult)
+
+    def shift(t, c):
+        ts(games("AS", c), games("AT", c), 5, A.arith_shift_right, 4095, A.bitwise_and)
+
+    def offsets(t, c):
+        if "offsets%d" % c in ON_S:
+            act(games("OF", c), games("AS", c), F.Identity, bias=K37 if t == 0 else AK)
+        else:
+            ts(games("OF", c), games("AS", c), K37 if t == 0 else AK, A.add)
 
     def z_psum(t, c):
-        o = ("pZ", 128 * c, 128 * c + 128)
-        mm(o, full("IH"), full("C5"), True, False)
-        mm(o, full("IH"), zi(t, c), False, True)
+        mm(games("pZ", c), full("IH"), full("C5", SIZE[c]), True, False)
+        mm(games("pZ", c), full("IH"), games("ZI", c, t), False, True)
 
     def key_t(t, c):
-        mm(("pX", 0, 128), full("ONE"), full("KC"), True, False)
-        mm(("pX", 0, 128), li(t, c), full("REV"), False, True)
+        mm(("pX", 0, 128), full("ONE", SIZE[c]), full("KC"), True, False)
+        mm(("pX", 0, 128), games("LI", c, t), full("REV"), False, True)
 
-    def key_s(c):
-        act(full("BT%d" % c), ("pX", 0, 128), F.Copy)
+    def key_s(t, c):
+        act(wide("BT", c), ("pX", 0, 128), F.Copy, p=SIZE[c])
 
-    def place_t(t, c):
+    def place_t(t, h):
         mm(("pW", 0, 128), full("IB"), full("NM"), True, False)
-        mm(("pW", 0, 128), zi(t, c), full("WB"), False, True)
+        mm(("pW", 0, 128), ("ZI", 256 * t + 128 * h, 256 * t + 128 * h + 128), full("WB"), False, True)
 
-    def place_s(c):
-        act(full("ZU%d" % c), ("pW", 0, 128), F.Relu, bias=-7.5)
+    def place_s(h):
+        act(wide("ZU", h), ("pW", 0, 128), F.Relu, bias=-7.5)
 
     def place_sum():
-        for c in range(2):
-            mm(("pW", 256 + 8 * c, 264 + 8 * c), full("ZU%d" % c), ("QF", 16, 24), True, True)
+        for h in range(2):
+            mm(("pW", 256 + 8 * h, 264 + 8 * h), wide("ZU", h), ("QF", 16, 24), True, True)
+
+    def place_up():
         act(("RR", 16, 32), ("pW", 256, 272), F.Identity, bias=M27)
+
+    def place_down():
         act(full("RR", 16), ("RR", 16, 32), F.Identity, bias=-M27)
+
+    def place_mod():
         mm(("pU", 256, 272), full("ONE"), full("PC", 16), True, False)
-        for c in range(2):
-            mm(("pU", 256 + 8 * c, 264 + 8 * c), full("ZU%d" % c), ("QF", 16, 24), False, False)
+        for h in range(2):
+            mm(("pU", 256 + 8 * h, 264 + 8 * h), wide("ZU", h), ("QF", 16, 24), False, False)
         mm(("pU", 256, 272), full("NIF"), full("RR", 16), False, True)
 
     def place_out():
-        if "place_out" in ON_S:
-            act(full("PL", 16), ("pU", 256, 272), F.Identity, bias=P16)
-        else:
-            ts(full("PL", 16), ("pU", 256, 272), P16, A.add)
+        act(full("PL", 16), ("pU", 256, 272), F.Identity, bias=P16)
 
-    def old(c):
-        act(full("OLD%d" % c), ("RT", 2048 * c, 2048 * c + 2048), F.Identity, bias=-0.5, off=("PL", 8 * c, 8 * c + 8))
-        if "mean%d" % c not in ON_S:
-            o = (("pR", "pZ")[c], 256, 384)
-            mm(o, full("IH"), full("C10"), True, False)
-            mm(o, full("IH"), full("OLD%d" % c), False, True)
+    def old_bank(c):
+        return ("pZ", 256, 256 + SIZE[c])
+
+    def old(t, c):
+        act(games("OLD", c), games("RT", c, 0, 16), F.Identity, bias=-0.5, off=listed("PL", c))
+
+    def old_t(t, c):
+        if "mean%d" % c in ON_S:
+            o = ("pW", 384, 384 + SIZE[c])
+            mm(o, full("IH"), games("OLD", c), True, False)
+            mm(o, full("IF"), games("ZO", c, t + 1), False, True)
+        else:
+            mm(old_bank(c), full("IH"), full("C10", SIZE[c]), True, False)
+            mm(old_bank(c), full("IH"), games("OLD", c), False, True)
 
     def gather(c, a, b, q):
-        y, of, w = ("Y%d" % c, 16 * a, 16 * b), ("OF%d" % c, a, b), ("RT", 0, RW)
+        a, b = CH[c] + a, CH[c] + b
+        y, of, w = ("Y", 16 * a, 16 * b), ("OF", a, b), ("RT", 0, RW)
         if q == "s":
             act(y, w, F.Copy, scale=0.25, off=of)
         else:
-            op("v", g.vector.tensor_scalar, dict(out=ap(y), in0=ind(w, of), scalar1=0.25, scalar2=None, op0=A.mult), [w, rg(of)], [rg(y)])
+            op("v", g.vector.tensor_scalar, dict(out=ap(y), in0=ind(w, of), scalar1=0.25, scalar2=None, op0=A.mult), [w, of], [y])
 
-    def blocks(c):
-        k = [KS[c], KS[c] + FIRST]
-        while k[-1] < 15:
-            k.append(min(15, k[-1] + 4))
-        return list(zip(k[:-1], k[1:]))
+    def row(c, k):
+        return ("Y", 16 * CH[c] + k, 16 * CH[c + 1], 16)
 
-    def diff_t(t, c, i):
-        k0, k1 = blocks(c)[i]
+    def beat(c, k0, k1):
+        return ("B", 16 * CH[c] + SIZE[c] * k0, 16 * CH[c] + SIZE[c] * k1)
+
+    def diff(t, c, i):
+        k0, k1, n = KB[c][i], KB[c][i + 1], SIZE[c]
         for k in range(k0, k1):
-            o = ("pD%d" % (i % 2), 128 * (k - k0), 128 * (k - k0) + 128)
-            mm(o, full("NH"), zi(t, c), True, False)
-            mm(o, full("IB"), ("Y%d" % c, k, 2048, 16), False, True)
+            o = ("pD%d" % (i % 2), n * (k - k0), n * (k - k0 + 1))
+            mm(o, full("NH"), games("ZI", c, t), True, False)
+            mm(o, full("IB"), row(c, k), False, True)
 
-    def sign_s(c, i):
-        k0, k1 = blocks(c)[i]
-        act(("B%d" % c, 128 * k0, 128 * k1), ("pD%d" % (i % 2), 0, 128 * (k1 - k0)), F.Sign, bias=256.0 - 0.125)
+    def sign(t, c, i):
+        k0, k1 = KB[c][i], KB[c][i + 1]
+        act(beat(c, k0, k1), ("pD%d" % (i % 2), 0, SIZE[c] * (k1 - k0)), F.Sign, bias=256.0 - 0.125)
 
-    def compare_v(c):
-        for k in range(KS[c]):
-            tt(("B%d" % c, 128 * k, 128 * k + 128), ("Y%d" % c, k, 2048, 16), ("pZ", 128 * c, 128 * c + 128), A.is_gt)
+    def compare_v(t, c):
+        for k in range(KB[c][0]):
+            tt(beat(c, k, k + 1), row(c, k), games("pZ", c), A.is_gt)
 
-    def beats(c, ks, first, last):
-        if first:
-            mm(("pC", 128 * c, 128 * c + 128), full("ONE"), full("C8%d" % c), True, False)
+    def beats(t, c, i):
+        ks = list(range(KB[c][i], KB[c][i + 1]))
+        if i == len(KB[c]) - 3:
+            ks = list(range(KB[c][0])) + ks
+        if i == 0:
+            mm(wide("pC", c), full("ONE", SIZE[c]), wide("C8", c), True, False)
         for k in ks:
-            mm(("pC", 128 * c + 15 - k, 128 * c + 128, 16), ("B%d" % c, 128 * k, 128 * k + 128), full("QB" if k < KS[c] else "QBH", 8), False, last and k == ks[-1])
+            mm(("pC", 128 * c + 15 - k, 128 * c + 128, 16), beat(c, k, k + 1), full("QB" if k < KB[c][0] else "QBH", 8), False, k == 14)
 
-    def scan(c, hi, a=0, b=H):
-        o, y = (("HI%d" if hi else "LO%d") % c, 16 * a, 16 * b), ("Y%d" % c, 16 * a, 16 * b)
-        m = ("MX" if hi else "MN", 16 * a, 16 * b)
-        op("v", g.vector.tensor_tensor_scan, dict(out=ap(o), data0=ap(m), data1=ap(y), initial=0.0,
-                                                  op0=A.mult if hi else A.add, op1=A.max if hi else A.min), [m, rg(y)], [rg(o)])
+    def running(c, hi, a, b):
+        y = ("Y", 16 * (CH[c] + a), 16 * (CH[c] + b))
+        if hi:
+            scan(("HI",) + y[1:], ("MX", 0, 16 * (b - a)), y, A.mult, A.max)
+        else:
+            scan(("LO",) + y[1:], ("MN", 0, 16 * (b - a)), y, A.add, A.min)
 
-    def verdict(c):
-        o, d = full("PS%d" % c), ("pC", 128 * c, 128 * c + 128)
-        op("v", g.vector.tensor_tensor_scan, dict(out=ap(o), data0=ap(d), data1=ap(full("BT%d" % c)), initial=0.0, op0=A.max, op1=A.min),
-           [d, rg(full("BT%d" % c))], [rg(o)])
+    def verdict(t, c):
+        scan(wide("PS", c), wide("pC", c), wide("BT", c), A.max, A.min, SIZE[c])
 
-    def spread(c):
-        tti(full("KX%d" % c), full("PS%d" % c), full("EL", 8), full("MK"), A.mult)
+    def spread(t, c):
+        tti(wide("KX", c), wide("PS", c), full("EL", 8), full("MK"), A.mult)
+
+    def lists(t, c):
+        n = SIZE[c]
         mm(("pR", 0, 16), full("ONE"), full("RC", 16), True, False)
-        mm(("pR", 0, 16), full("KX%d" % c), full("QF", 16), False, True)
-        mm(("pC", 256, 264), full("ONE"), ("RC", 16, 24), True, False)
-        mm(("pC", 256, 264), full("KX%d" % c), ("QF", 16, 24), False, False)
+        mm(("pR", 0, 16), wide("KX", c), full("QF", 16), False, True, n)
 
-    def list_k(c):
-        ts(full("LK%d" % c, 8), ("pR", 0, 8), MP, A.add, M23, A.subtract)
+    def list_k(t, c):
+        if "list_k%d" % c in ON_S:
+            act(listed("LK", c), ("pR", 0, SIZE[c] // 16), F.Identity, bias=P4)
+        else:
+            ts(listed("LK", c), ("pR", 0, SIZE[c] // 16), MP, A.add, M23, A.subtract)
 
     def kappa(t, c):
-        k = ("KO", 16 * t + 8 * c, 16 * t + 8 * c + 8)
-        act(k, ("pR", 8, 16), F.Identity, bias=129.0)
-        mm(("pC", 256, 264), full("I4"), k, False, True)
+        k, n = listed("KO", c, t), SIZE[c] // 16
+        act(k, ("pR", 8, 8 + n), F.Identity, bias=129.0)
 
-    def list_n(c):
-        if "list_n%d" % c in ON_S:
-            act(full("LN%d" % c, 8), ("pC", 256, 264), F.Copy)
-        else:
-            tc(full("LN%d" % c, 8), ("pC", 256, 264))
+    def named(t, c):
+        k, n = listed("KO", c, t), SIZE[c] // 16
+        mm(("pX", 128, 128 + n), full("ONE"), ("RC", 16, 16 + n), True, False)
+        mm(("pX", 128, 128 + n), wide("KX", c), ("QF", 16, 16 + n), False, False, SIZE[c])
+        mm(("pX", 128, 128 + n), full("I4"), k, False, True)
 
-    def pick_hi(c):
-        act(full("HG%d" % c), full("HI%d" % c, 2048), F.Identity, bias=512.0 - 0.125, off=full("LK%d" % c, 8))
+    def list_n(t, c):
+        act(listed("LN", c), ("pX", 128, 128 + SIZE[c] // 16), F.Copy)
+
+    def pick_hi(t, c):
+        act(games("HG", c), games("HI", c, 0, 16), F.Identity, bias=512.0 - 0.125, off=listed("LK", c))
 
     def new_z(t, c):
-        z = full("ZO%d%d" % (t + 1, c))
-        tti(z, full("LO%d" % c, 2048), full("LK%d" % c, 8), full("HG%d" % c), A.add)
+        z = games("ZO", c, t + 1)
+        tti(z, games("LO", c, 0, 16), listed("LK", c), games("HG", c), A.add)
         if t == TURNS - 1:
-            o = ("ZL", 128 * c, 128 * c + 128)
-            ts(o, z, 2.0, A.mult, 1024.0, A.subtract)
-            z = o
+            ts(games("ZL", c), z, 2.0, A.mult, 1024.0, A.subtract)
+            z = games("ZL", c)
         send("z%d%d" % (t + 1, c), *z)
 
     def views(t, c):
-        l = full("LU%d%d" % (t + 1, c)) if t < TURNS - 1 else ("EO", 128 * c, 128 * c + 128)
-        tti(l, full("TAB%d" % t, 512 + 256 * t), full("LN%d" % c, 8), ("NC%d" % t, 128 * c, 128 * c + 128), A.add)
+        l = games("LU", c, t + 1) if t < TURNS - 1 else games("EO", c)
+        tti(l, full("TAB%d" % t, 512 + 256 * t), listed("LN", c), games("NC", c, t), A.add)
         send("l%d%d" % (t + 1, c), *l)
 
     def mean(t, c):
+        n, z = SIZE[c], games("ZO", c, t + 1)
         if "mean%d" % c in ON_S:
-            o = ("pW", 384, 512)
-            mm(o, full("IH"), full("OLD%d" % c), True, False)
-            mm(o, full("IF"), full("ZO%d%d" % (t + 1, c)), False, True)
-            act(full("RZ%d" % c), o, F.Identity, bias=-512.0)
+            act(games("RZ", c), ("pW", 384, 384 + n), F.Identity, bias=-512.0)
         else:
-            tt(full("RZ%d" % c), (("pR", "pZ")[c], 256, 384), full("ZO%d%d" % (t + 1, c)), A.add)
+            tt(games("RZ", c), old_bank(c), z, A.add)
 
-    def scatter(c):
-        win, off = ("RT", 2048 * c, 2048 * c + 2048), ("PL", 8 * c, 8 * c + 8)
-        op("v", g.vector.tensor_copy, dict(out=ind(win, off), in_=ap(full("RZ%d" % c))), [off, rg(full("RZ%d" % c))], [win])
+    def scatter(t, c):
+        win, off = games("RT", c, 0, 16), listed("PL", c)
+        op("v", g.vector.tensor_copy, dict(out=ind(win, off), in_=ap(games("RZ", c))), [off, games("RZ", c)], [win])
 
     def behind():
         dma("d", T.RT[:, 4096:RW], T.RT[:, 0:RW - 4096], [("RT", 0, RW - 4096)], [("RT", 4096, RW)])
 
     def count():
-        act(full("SG", 16), ("PS", 15, 256, 16), F.Sign, bias=58000.0, accum=full("ACC", 1))
+        act(full("SG", 8 * NCH), ("PS", 15, 128 * NCH, 16), F.Sign, bias=58000.0, accum=full("ACC", 1))
+
+    def count_t():
         mm(("pD0", 0, 1), full("ONE"), ("CA", 0, 1), True, False)
         mm(("pD0", 0, 1), full("H5"), full("ACC", 1), False, True)
 
     def count_a():
-        ts(RA, ("pD0", 0, 1), M31, A.add, M31, A.subtract)
+        if "count" in ON_S:
+            act(full("AQ", 1), ("pD0", 0, 1), F.Identity, scale=1.0 / 256)
+            act(RA, ("pD0", 0, 1), F.Identity, bias=K37A)
+        else:
+            ts(RA, ("pD0", 0, 1), M31, A.add, M31, A.subtract)
 
     def count_b():
-        ts(AK, ("pD0", 0, 1), RA, A.subtract, K37A, A.add)
+        if "count" in ON_S:
+            act(AK, full("AQ", 1), F.Identity, bias=RA, scale=-256.0)
+        else:
+            ts(AK, ("pD0", 0, 1), RA, A.subtract, K37A, A.add)
 
     parts = {(0, 0): [(0, 0, "VI0", 1, 0)], (0, 1): [(1, 0, "VI1", 1, 0)], (1, 0): [(1, 512, "HL1", 2, 0), (3, 512, "HL3", 2, 0)],
              (1, 1): [(2, 0, "VI2", 1, 0)], (2, 0): [(2, 512, "HB2", 1, 0), (2, 768, "HB2", 2, 1)], (2, 1): [(3, 0, "VI3", 1, 0)],
@@ -575,109 +587,96 @@ def rank_program(g, core, T, topo):
 
     def table(key):
         a = 0
-        for tb, c0, src, sh, n in parts.get(key, []):
+        for tb, c0, src, sh, n in parts[key]:
             wd = 512 if src[0] == "V" else 256
             w = ("pW", a, a + wd)
             mm(w, full("SH%d" % sh), full(src, wd), True, sh == 1)
             if sh == 2:
-                mm1(w, full("ROW1"), full("NC%d" % n, 256), False, True)
+                mm(w, full("ROW1"), ("NC", 256 * n, 256 * n + 256), False, True, 1)
             a += wd
-        a = 0
-        for tb, c0, src, sh, n in parts.get(key, []):
-            wd = 512 if src[0] == "V" else 256
-            act(("TAB%d" % tb, c0, c0 + wd), ("pW", a, a + wd), F.Copy)
-            a += wd
+
+    def table_s(key):
+        (tb, c0), (tb2, _) = parts[key][0][:2], parts[key][-1][:2]
+        if tb == tb2:
+            act(("TAB%d" % tb, c0, c0 + 512), full("pW", 512), F.Copy)
+        else:
+            for a, x in ((0, tb), (256, tb2)):
+                act(("TAB%d" % x, c0, c0 + 256), ("pW", a, a + 256), F.Copy)
 
     def verdicts_out(a, b):
         w = 16 * (b - a)
         for p in range(16):
-            op("t", g.tensor.matmul, dict(out=T.pW[0:8, p:w:16], lhsT=T.EP[:, 8 * p:8 * p + 8], rhs=T.KI[:, a:b], start=True, stop=True),
-               [full("EP"), ("KI", a, b)], [("pW", 0, w)])
-        op("s", g.scalar.activation, dict(out=T.YKS[:, 16 * a:16 * b], in_=T.pW[0:8, 0:w], func=F.Identity, bias=-129.0), [("pW", 0, w)], [("YKS", 16 * a, 16 * b)])
+            mm(("pW", p, w, 16), ("EP", 8 * p, 8 * p + 8), ("KI", a, b), True, True)
+        act(("YKS", 16 * a, 16 * b), ("pW", 0, w), F.Identity, bias=-129.0, p=8)
         dma("d", T.yk[:, 16 * a:16 * b], T.YKS[:, 16 * a:16 * b], [("YKS", 16 * a, 16 * b)], [("yk", 16 * a, 16 * b)])
-
-    def count_block(c, i):
-        bl = blocks(c)
-        ks = list(range(*bl[i]))
-        if i == len(bl) - 2:
-            ks = list(range(KS[c])) + ks
-        beats(c, ks, i == 0, i == len(bl) - 1)
 
     def history(t):
         if t < 2:
-            send("h%d" % (t + 2), "LU%d0" % (t + 1), 0, 256)
+            send("h%d" % (t + 2), "LU", 256 * t + 256, 256 * t + 512)
         send("y%d" % t, "KO", 16 * t, 16 * t + 16)
 
     def views_out():
         mm(("pW", 0, 256), full("SH1"), full("L3I", 256), True, False)
-        mm1(("pW", 0, 256), full("ROW0"), full("NC3", 256), False, True)
+        mm(("pW", 0, 256), full("ROW0"), ("NC", 768, 1024), False, True, 1)
         act(full("YOS", 256), ("pW", 0, 256), F.Copy)
         dma("d", T.yo[:], T.YOS[:], [full("YOS", 256)], [("yo", 0, 256)])
 
     def chunk_out(c, qp, qz):
-        a, b = 128 * c, 128 * c + 128
+        a, b = CH[c], CH[c + 1]
         dma(qp, T.yp[:, a:b], T.EF[:, a:b], [("EF", a, b)], [("yp", a, b)])
         dma(qz, T.yz[:, a:b], T.ZF[:, a:b], [("ZF", a, b)], [("yz", a, b)])
 
     def steps(t):
         last = t == TURNS - 1
         s = {}
-        for c in range(2):
-            n = str(c)
-            s["gather_v" + n] = lambda c=c: gather(c, GS[c], H, "v")
-            s["compare_v" + n] = lambda c=c: compare_v(c)
-            for i, (a, b) in enumerate(zip(HC[c][:-1], HC[c][1:])):
-                s["hi%d%s" % (c, "abc"[i])] = lambda c=c, a=a, b=b: scan(c, True, a, b)
-            for i, (a, b) in enumerate(zip(LC[c][:-1], LC[c][1:])):
-                s["lo%d%s" % (c, "abc"[i])] = lambda c=c, a=a, b=b: scan(c, False, a, b)
-            for i in range(len(blocks(c))):
-                s["diff%d%d" % (c, i)] = lambda c=c, i=i: diff_t(t, c, i)
-                s["sign%d%d" % (c, i)] = lambda c=c, i=i: sign_s(c, i)
-                s["beats%d%d" % (c, i)] = lambda c=c, i=i: count_block(c, i)
-            for name, f in (("verdict", verdict), ("spread", spread), ("list_k", list_k), ("pick_hi", pick_hi), ("list_n", list_n)):
-                s[name + n] = lambda c=c, f=f: f(c)
-            for name, f in (("kappa", kappa), ("new_z", new_z), ("views", views)):
-                s[name + n] = lambda c=c, f=f: f(t, c)
-            if not last:
-                s["old" + n] = lambda c=c: old(c)
-                s["mean" + n] = lambda c=c: mean(t, c)
-                s["scatter" + n] = lambda c=c: scatter(c)
-        s["gather_s0"] = lambda: gather(0, 0, GS[0], "s")
-        cut = (0,) + CUTS + (GS[1],)
-        for i in range(3):
-            s["gather_s1" + "abc"[i]] = lambda i=i: gather(1, cut[i], cut[i + 1], "s")
-        for n, (tn, c) in (("%s1", (t, 1)), ("n_%s", (t + 1, 0))):
-            if tn < TURNS:
-                for name, f in (("u_sum", u_sum), ("u_mod", u_mod), ("key_t", key_t), ("z_psum", z_psum)):
-                    s[n % name] = lambda tn=tn, c=c, f=f: f(tn, c)
-                s[n % "key_s"] = lambda c=c: key_s(c)
-                for name, f in zip(("product", "shift", "offsets"), address(tn, c)):
-                    s[n % name] = f
-                if tn < TURNS - 1:
-                    s[n % "place_t"] = lambda tn=tn, c=c: place_t(tn, c)
-                    s[n % "place_s"] = lambda c=c: place_s(c)
+        ahead = dict(u_sum=u_sum, u_mod=u_mod, u_off=u_off, product=product, shift=shift, offsets=offsets, key_t=key_t, key_s=key_s, z_psum=z_psum)
+        every = dict(compare_v=compare_v, verdict=verdict, spread=spread, lists=lists, list_k=list_k, kappa=kappa, named=named, pick_hi=pick_hi,
+                     list_n=list_n, new_z=new_z, views=views)
         if not last:
-            s.update(place_sum=place_sum, place_out=place_out, behind=behind, count=count, count_a=count_a, count_b=count_b,
-                     table_a=lambda: table((t, 1)), table_b=lambda: table((t + 1, 0)), history=lambda: history(t))
+            every.update(old=old, old_t=old_t, mean=mean, scatter=scatter)
+            for name in ahead:
+                s["n_" + name] = lambda f=ahead[name]: f(t + 1, 0)
+        for c in range(NCH):
+            for name, f in list(every.items()) + (list(ahead.items()) if c else []):
+                s["%s%d" % (name, c)] = lambda c=c, f=f: f(t, c)
+            cut = (0,) + GS[c]
+            for i in range(len(GS[c])):
+                s["gather_s%d%s" % (c, "abc"[i])] = lambda c=c, a=cut[i], b=cut[i + 1]: gather(c, a, b, "s")
+            s["gather_v%d" % c] = lambda c=c: gather(c, GS[c][-1], SIZE[c], "v")
+            for x, a, b in (("a", 0, GS[c][-1]), ("b", GS[c][-1], SIZE[c])):
+                s["hi%d%s" % (c, x)] = lambda c=c, a=a, b=b: running(c, True, a, b)
+                s["lo%d%s" % (c, x)] = lambda c=c, a=a, b=b: running(c, False, a, b)
+            for i in range(len(KB[c]) - 1):
+                for name, f in (("diff", diff), ("sign", sign), ("beats", beats)):
+                    s["%s%d%d" % (name, c, i)] = lambda c=c, i=i, f=f: f(t, c, i)
+            if last:
+                s["last%d" % c] = lambda c=c: send("y3%d" % c, *listed("KO", c, 3))
+                if c < NCH - 1:
+                    s["out_c%d" % c] = lambda c=c: chunk_out(c, "d", "d")
+        if not last:
+            for h in range(2):
+                s["place_t%d" % h] = lambda h=h: place_t(t, h)
+                s["place_s%d" % h] = lambda h=h: place_s(h)
+            s.update(place_sum=place_sum, place_up=place_up, place_down=place_down, place_mod=place_mod, place_out=place_out, behind=behind,
+                     count=count, count_t=count_t, count_a=count_a, count_b=count_b, history=lambda: history(t),
+                     table_a=lambda: table((t, 1)), table_as=lambda: table_s((t, 1)), table_b=lambda: table((t + 1, 0)), table_bs=lambda: table_s((t + 1, 0)))
         else:
-            s.update(last0=lambda: send("y30", "KO", 48, 56), last1=lambda: send("y31", "KO", 56, 64), last_l=lambda: send("w", "LI30", 0, 256),
-                     out_k0=lambda: verdicts_out(0, 32), out_k1=lambda: verdicts_out(32, 48), out_o=views_out, out_c0=lambda: chunk_out(0, "d", "d"))
+            s.update(last_l=lambda: send("w", "LI", 768, 1024), out_k0=lambda: verdicts_out(0, 32), out_k1=lambda: verdicts_out(32, 48), out_o=views_out)
         if t == 0:
-            s.update(table_0=lambda: table((0, 0)), bulk=bulk)
+            s.update(table_0=lambda: table((0, 0)), table_0s=lambda: table_s((0, 0)), bulk=bulk)
         return s
 
-    first = steps(-1)
-    for n in ("u_sum", "u_mod", "product", "shift", "offsets", "key_t", "key_s", "place_t", "place_s", "z_psum"):
-        first["n_" + n]()
+    for f in (u_sum, u_mod, u_off, product, shift, offsets, key_t, key_s, z_psum):
+        f(0, 0)
     for t in range(TURNS):
         s = steps(t)
-        for n in ORDER:
+        for n in (FIRST, ORDER, ORDER, LAST)[t]:
             if n in s:
                 s.pop(n)()
         assert not s
 
     verdicts_out(48, 64)
-    chunk_out(1, "d", "s")
+    chunk_out(NCH - 1, "d", "s")
     used.update(state["sent"])
     for s in sorted(used):
         if known["g"].get(s, 0) < used[s]:

from concourse.mybir import AluOpType as A, ActivationFunctionType as F

N, TURNS = 8, 4
CH = (0, 128, 256)
RW = 4096 + 816
EARLY = 1536
GS = ((64,), (24, 48, 72))
KB = ((4, 7, 11, 15), (5, 7, 11, 15))
ON_S = ("mean0", "offsets0", "count", "list_k0", "list_k1")
FIRST = """place_t0 gather_v0 gather_s0a u_sum1 u_mod1 diff00 u_off1 compare_v0 diff01 place_s0 sign00 sign01 diff02 z_psum1 place_t1 beats00 product1 sign02 hi0b shift1 key_t1 lo0b offsets1 beats01 lo0a place_s1 gather_s1b bulk gather_s1a gather_s1c beats02 verdict0 hi0a spread0 lists0 place_sum list_k0 place_up pick_hi0 kappa0 place_down table_0 named0 gather_v1 diff10 place_mod table_0s diff11 new_z0 compare_v1 list_n0 place_out sign10 views0 diff12 beats10 key_s1 sign11 sign12 old0 beats11 beats12 lo1b hi1a old1 lo1a verdict1 count spread1 old_t0 mean0 hi1b scatter0 lists1 old_t1 list_k1 table_a kappa1 count_t pick_hi1 table_as count_a named1 n_u_sum behind n_u_mod count_b table_b new_z1 list_n1 n_u_off mean1 scatter1 n_key_t n_product table_bs n_shift views1 history n_key_s n_offsets n_z_psum""".split()
ORDER = """gather_v0 gather_s0a table_a diff00 diff01 table_as place_t0 lo0b compare_v0 sign00 sign01 diff02 beats00 sign02 lo0a beats01 hi0b hi0a u_sum1 beats02 place_s0 u_mod1 place_t1 u_off1 verdict0 spread0 product1 place_s1 place_sum place_up lists0 shift1 kappa0 list_k0 offsets1 named0 place_down pick_hi0 list_n0 place_mod new_z0 key_t1 z_psum1 views0 gather_v1 gather_s1c gather_s1a gather_s1b place_out diff10 key_s1 diff11 old0 sign10 old_t0 sign11 diff12 compare_v1 hi1a hi1b mean0 scatter0 beats10 sign12 old1 beats11 beats12 verdict1 count spread1 table_b lo1b lo1a lists1 count_t behind list_k1 kappa1 n_u_sum named1 pick_hi1 list_n1 n_u_mod n_z_psum n_u_off old_t1 new_z1 n_key_t table_bs views1 n_product mean1 history n_shift count_a n_key_s scatter1 count_b n_offsets""".split()
LAST = """gather_v0 gather_s0a hi0b diff00 diff01 lo0b lo0a compare_v0 sign00 hi0a sign01 beats00 out_k0 u_sum1 diff02 u_mod1 sign02 u_off1 last_l product1 shift1 out_k1 offsets1 beats01 gather_s1c gather_s1a beats02 verdict0 spread0 key_t1 lists0 kappa0 gather_s1b named0 list_n0 z_psum1 list_k0 gather_v1 hi1b key_s1 last0 diff10 views0 compare_v1 diff11 sign10 pick_hi0 new_z0 diff12 sign11 sign12 out_o beats10 beats11 hi1a beats12 verdict1 spread1 lists1 kappa1 lo1b lo1a list_k1 named1 list_n1 last1 pick_hi1 out_c0 views1 new_z1""".split()
M31, M27, M23 = 1.5 * 2.0 ** 31, 1.5 * 2.0 ** 27, 1.5 * 2.0 ** 23
BIG = 2.0 ** 17
NCH = len(CH) - 1
SIZE = [CH[c + 1] - CH[c] for c in range(NCH)]
PIECE = 16 * max(max(GS[c][-1], SIZE[c] - GS[c][-1]) for c in range(NCH))

SCRATCH = {
    "RT": ("sbuf", [128, RW], "bfloat16"),
    "VP32": ("sbuf", [128, 512], "int32"), "VO32": ("sbuf", [128, 512], "int32"),
    "MV32": ("sbuf", [128, 16], "int32"), "MV16": ("sbuf", [128, 16], "uint16"),
    "Z0B": ("sbuf", [128, 256], "bfloat16"), "WT32": ("sbuf", [128, 1], "int32"), "WTF": ("sbuf", [128, 1], "float32"),
    "PV": ("sbuf", [128, 512], "float16"), "OV": ("sbuf", [128, 512], "float16"),
    "HL1": ("sbuf", [128, 256], "float16"), "HL3": ("sbuf", [128, 256], "float16"),
    "HB2": ("sbuf", [128, 256], "float16"), "HB3": ("sbuf", [128, 256], "float16"), "L3I": ("sbuf", [128, 256], "float16"),
    "MX": ("sbuf", [128, PIECE], "bfloat16"), "MN": ("sbuf", [128, PIECE], "bfloat16"),
    "DIF": ("sbuf", [128, 128], "float32"), "DB": ("sbuf", [128, 128], "float32"), "JI": ("sbuf", [128, 128], "int32"),
    "JS": ("sbuf", [128, 128], "int32"), "JM": ("sbuf", [128, 128], "int32"), "PI": ("sbuf", [128, 1], "int32"),
    "PG": ("sbuf", [128, 1], "int32"), "PK": ("sbuf", [128, 1], "int32"), "COL": ("sbuf", [128, 16], "float32"),
    "BLK": ("sbuf", [128, 128], "bfloat16"), "T1": ("sbuf", [128, 128], "bfloat16"), "EPI": ("sbuf", [128, 128], "float32"),
    "IB": ("sbuf", [128, 128], "bfloat16"), "I4": ("sbuf", [128, 128], "bfloat16"), "IH": ("sbuf", [128, 128], "float16"),
    "NH": ("sbuf", [128, 128], "float16"), "NI4": ("sbuf", [128, 128], "float16"), "NIF": ("sbuf", [128, 128], "float32"),
    "IF": ("sbuf", [128, 128], "float16"), "WB": ("sbuf", [128, 128], "float16"), "REV": ("sbuf", [128, 128], "float16"),
    "KC": ("sbuf", [128, 128], "float16"), "SH1": ("sbuf", [128, 128], "float16"), "SH2": ("sbuf", [128, 128], "float16"),
    "EP": ("sbuf", [128, 128], "bfloat16"), "MK": ("sbuf", [128, 128], "float32"), "NM": ("sbuf", [128, 128], "bfloat16"),
    "QF": ("sbuf", [128, 32], "float32"), "QB": ("sbuf", [128, 8], "bfloat16"), "QBH": ("sbuf", [128, 8], "bfloat16"),
    "RC": ("sbuf", [128, 24], "float16"), "PC": ("sbuf", [128, 16], "float16"), "CA": ("sbuf", [128, 2], "float16"),
    "H5": ("sbuf", [128, 128], "float32"), "ROW0": ("sbuf", [128, 128], "float16"), "ROW1": ("sbuf", [128, 128], "float16"),
    "ONE": ("sbuf", [128, 128], "float16"), "ONB": ("sbuf", [128, 128], "bfloat16"), "CB": ("sbuf", [128, 128], "bfloat16"),
    "C5": ("sbuf", [128, 128], "float16"), "C10": ("sbuf", [128, 128], "float16"),
    "NF": ("sbuf", [128, 256], "float32"), "NC": ("sbuf", [128, 1024], "float16"),
    "ELI": ("sbuf", [128, 8], "int32"), "EL": ("sbuf", [128, 8], "uint16"),
    "RR": ("sbuf", [128, 32], "float32"), "ZU": ("sbuf", [128, 256], "float32"),
    "PL": ("sbuf", [128, 16], "uint16"), "LK": ("sbuf", [128, 16], "uint16"), "LN": ("sbuf", [128, 16], "uint16"),
    "SG": ("sbuf", [128, 8 * NCH], "bfloat16"), "ACC": ("sbuf", [128, 1], "float32"), "AQ": ("sbuf", [128, 1], "int32"),
    "YKS": ("sbuf", [8, 1024], "float32"), "YOS": ("sbuf", [128, 256], "float32"),
    "KO": ("sbuf", [128, 64], "bfloat16"), "KI": ("sbuf", [128, 64], "bfloat16"),
    "ZL": ("sbuf", [128, 256], "bfloat16"), "ZF": ("sbuf", [128, 256], "bfloat16"),
    "EO": ("sbuf", [128, 256], "float32"), "EF": ("sbuf", [128, 256], "float32"),
    "ZI": ("sbuf", [128, 1024], "float16"), "LI": ("sbuf", [128, 1024], "float16"),
    "ZO": ("sbuf", [128, 1280], "float16"), "LU": ("sbuf", [128, 1024], "float16"),
}
for _n in ("pU", "pZ", "pD0", "pD1", "pC", "pR", "pW", "pX"):
    SCRATCH[_n] = ("psum", [128, 512], "float32")
for _t in range(4):
    SCRATCH["VI%d" % _t] = ("sbuf", [128, 512], "float16")
    SCRATCH["TAB%d" % _t] = ("sbuf", [128, 512 + 256 * _t], "float32")
for _n, _d in (("Y", "bfloat16"), ("B", "bfloat16"), ("HI", "bfloat16"), ("LO", "bfloat16")):
    SCRATCH[_n] = ("sbuf", [128, 4096], _d)
for _n, _d in (("U2", "float16"), ("AT", "int32"), ("AS", "int32"), ("OF", "uint16"), ("HG", "float32"), ("OLD", "float16"), ("RZ", "int32")):
    SCRATCH[_n] = ("sbuf", [128, 256], _d)
for _n, _d in (("BT", "float32"), ("PS", "float32"), ("KX", "float32"), ("C8", "float16")):
    SCRATCH[_n] = ("sbuf", [128, 128 * NCH], _d)

SEMAPHORES = (["qg", "qt", "qv", "qs", "ls", "l0"] + ["d%d" % i for i in range(28)]
              + ["%s%d%d" % (n, t, c) for n in "zl" for t in range(5) for c in range(NCH)] + ["v%d" % t for t in range(4)]
              + ["h%d" % t for t in range(4)] + ["y0", "y1", "y2", "w"] + ["y3%d" % c for c in range(NCH)])


def games(buf, c, t=0, w=1):
    return (buf, w * (256 * t + CH[c]), w * (256 * t + CH[c + 1]))


def listed(buf, c, t=0):
    return (buf, 16 * t + CH[c] // 16, 16 * t + CH[c + 1] // 16)


def wide(buf, c):
    return (buf, 128 * c, 128 * c + 128)


def bits(m):
    return bin(m).count("1")


def relay_of(src, dst, n, near, topo):
    if topo.may_write(src, dst):
        return None
    c = [x for x in topo.cores_of(src) if x != src and topo.may_write(x, dst)]
    c = [x for x in c if (topo.die(x) == topo.die(src)) == near]
    return c[n % len(c)]


def messages(core, T, topo):
    r = T.rank_of(core)
    out = []

    def add(sem, off, where, n, near):
        dst = T.cores[(r + off) % N]
        out.append((sem, dst, relay_of(core, dst, n, near, topo)) + where)
    for t in range(4):
        for c in range(NCH):
            add("z%d%d" % (t, c), 1, games("ZI", c, t), 0, True)
            add("l%d%d" % (t, c), 1, games("LI", c, t), 1, True)
    add("v0", 1, ("VI0", 0, 512), 0, False)
    add("v1", 2, ("VI1", 0, 512), 0, False)
    add("v2", 3, ("VI2", 0, 512), 1, False)
    add("v3", 4, ("VI3", 0, 512), 0, False)
    add("h1", 2, ("HL1", 0, 256), 0, False)
    add("h0", 4, ("HL3", 0, 256), 0, False)
    for t in range(3):
        if t < 2:
            add("h%d" % (t + 2), 2, ("HB%d" % (t + 2), 0, 256), 0, False)
        add("y%d" % t, -1 - t, ("KI", 16 * t, 16 * t + 16), 0, False)
    for c in range(NCH):
        add("z4%d" % c, -4, games("ZF", c), 0, True)
        add("l4%d" % c, -4, games("EF", c), 0, True)
        add("y3%d" % c, -4, listed("KI", c, 3), 0, False)
    add("w", -4, ("L3I", 0, 256), 0, False)
    return out


def hand_on(g, core, T, topo):
    own = [x for x in topo.cores_of(core) if T.rank_of(x) is not None]
    n = 0
    for rc in own:
        for sem, dst, rel, buf, a, b in messages(rc, T, topo):
            if rel == core:
                g.wait_ge(T.sem[sem], bits(topo.mask(rc, core)))
                m = topo.mask(core, dst)
                rid, pid = topo.addr(dst, core)
                g.remote_dma(T[buf][:, a:b], T[buf][:, a:b], T.sem[sem], T.sem.ls, pid, rid, m)
                n += bits(m)
    if n:
        g.wait_ge(T.sem.ls, n)


def rank_program(g, core, T, topo):
    rank = T.rank_of(core)
    if rank is None:
        hand_on(g, core, T, topo)
        return
    Q = {"g": g, "t": g.tensor, "v": g.vector, "s": g.scalar, "d": g.sync}
    cnt = {"g": 0, "t": 0, "v": 0, "s": 0}
    known = {q: {} for q in Q}
    acc, bank, used = {}, {}, {}
    state = {"d": 0, "sent": {"ls": 0, "l0": 0}}

    def need(q, tok):
        sem, val, clk = tok
        k = known[q]
        if k.get(sem, 0) < val:
            Q[q].wait_ge(T.sem[sem], val)
            k[sem] = val
        for s2 in clk:
            if k.get(s2, 0) < clk[s2]:
                k[s2] = clk[s2]

    def deps(q, reads, writes):
        toks = []
        for w, lst in ((False, reads), (True, writes)):
            for nm, lo, hi in lst:
                if nm[0] == "p":
                    for q2 in bank.get(nm, {}):
                        if q2 != q:
                            toks.append(bank[nm][q2])
                    continue
                for lo2, hi2, w2, q2, tok in acc.get(nm, []):
                    if lo < hi2 and lo2 < hi and (w or w2) and not (q2 == q and w and not w2 and q in cnt):
                        toks.append(tok)
        best = {}
        for tok in toks:
            if tok[0] not in best or best[tok[0]][1] < tok[1]:
                best[tok[0]] = tok
        for tok in sorted(best.values(), key=lambda x: -len(x[2])):
            need(q, tok)

    def note(q, reads, writes, tok):
        for w, lst in ((False, reads), (True, writes)):
            for nm, lo, hi in lst:
                if nm[0] == "p":
                    bank.setdefault(nm, {})[q] = tok
                    continue
                l = acc.setdefault(nm, [])
                if w:
                    l[:] = [e for e in l if not (lo <= e[0] and e[1] <= hi)]
                l.append((lo, hi, w, q, tok))

    def op(q, fn, args, reads, writes):
        deps(q, reads, writes)
        fn(**args).then_inc(T.sem["q" + q], 1)
        cnt[q] += 1
        used["q" + q] = cnt[q]
        note(q, reads, writes, ("q" + q, cnt[q], dict(known[q])))

    def dma(q, out, in_, reads, writes):
        deps(q, reads, writes)
        s = "d%d" % state["d"]
        state["d"] += 1
        Q[q].dma_start(out, in_).then_inc(T.sem[s], 16)
        used[s] = 16
        note(q, reads, writes, (s, 16, dict(known[q])))

    for off in range(1, N):
        src = T.cores[(rank + off) % N]
        for sem, dst, rel, bf, a, b in messages(src, T, topo):
            if dst == core:
                used[sem] = bits(topo.mask(rel if rel is not None else src, core))
                note("x", [], [(bf, a, b)], (sem, used[sem], {}))

    plan = {m[0]: m for m in messages(core, T, topo)}

    def send(sem, buf, a, b, left="ls"):
        _, dst, rel, ob, oa, oe = plan[sem]
        deps("g", [(buf, a, b)], [])
        to = dst if rel is None else rel
        m = topo.mask(core, to)
        rid, pid = topo.addr(to, core)
        g.remote_dma(T[ob][:, oa:oe], T[buf][:, a:b], T.sem[sem], T.sem[left], pid, rid, m)
        state["sent"][left] += bits(m)

    def ap(o, p=128):
        if len(o) == 4:
            return T[o[0]][0:p, o[1]:o[2]:o[3]]
        return T[o[0]][0:p, o[1]:o[2]]

    def ind(win, off):
        return ap(win).indirect(ap(off))

    def full(n, w=128):
        return (n, 0, w)

    def mm(out, l, r, start, stop, k=128):
        op("t", g.tensor.matmul, dict(out=ap(out, l[2] - l[1]), lhsT=ap(l, k), rhs=ap(r, k), start=start, stop=stop), [l[:3], r[:3]], [out[:3]])

    def tt(out, a, b, o):
        op("v", g.vector.tensor_tensor, dict(out=ap(out), in0=ap(a), in1=ap(b), op=o), [a[:3], b[:3]], [out[:3]])

    def tti(out, win, off, b, o):
        op("v", g.vector.tensor_tensor, dict(out=ap(out), in0=ind(win, off), in1=ap(b), op=o), [win, off, b], [out])

    def columns(*xs):
        return [x for x in xs if isinstance(x, tuple)], [ap(x) if isinstance(x, tuple) else x for x in xs]

    def ts(out, a, s1, o1, s2=None, o2=None):
        rd, sc = columns(s1, s2)
        d = dict(out=ap(out), in0=ap(a), scalar1=sc[0], scalar2=sc[1], op0=o1)
        if o2 is not None:
            d["op1"] = o2
        op("v", g.vector.tensor_scalar, d, rd + [a[:3]], [out[:3]])

    def tc(out, a):
        op("v", g.vector.tensor_copy, dict(out=ap(out), in_=ap(a)), [a], [out])

    def ms(out, v, rows=None):
        op("v", g.vector.memset, dict(ap=ap(out) if rows is None else T[out[0]][rows[0]:rows[1], out[1]:out[2]], constant=v), [], [out[:3]])

    def scan(out, d0, d1, o0, o1, p=128):
        op("v", g.vector.tensor_tensor_scan, dict(out=ap(out, p), data0=ap(d0, p), data1=ap(d1, p), initial=0.0, op0=o0, op1=o1), [d0, d1], [out])

    def act(out, a, f, bias=None, scale=None, accum=None, off=None, p=128):
        rd, sc = columns(bias, scale)
        d = dict(out=ap(out, p), in_=ap(a, p) if off is None else ind(a, off), func=f)
        wr = [out]
        if bias is not None:
            d["bias"] = sc[0]
        if scale is not None:
            d["scale"] = sc[1]
        if accum is not None:
            d["accum_out"] = ap(accum)
            wr.append(accum)
        op("s", g.scalar.activation, d, rd + [a[:3]] + ([] if off is None else [off]), wr)

    def iota(out, pattern, base, cm):
        big = dict(allow_small_or_imprecise_dtypes=True) if SCRATCH[out[0]][2] == "float32" else {}
        op("g", g.iota, dict(out=ap(out), pattern=pattern, base=base, channel_multiplier=cm, **big), [], [out])

    dma("s", T.Z0B[:], T.z0[:], [], [("Z0B", 0, 256)])
    dma("d", T.VP32[:], T.vp[:], [], [("VP32", 0, 512)])
    dma("s", T.MV32[:], T.mv[:], [], [("MV32", 0, 16)])
    dma("d", T.WT32[:], T.wt[:], [], [("WT32", 0, 1)])
    dma("d", T.RT[:, 0:EARLY], T.strat[:, 0:EARLY], [], [("RT", 0, EARLY)])

    iota(full("PI", 1), [[0, 1]], 0, 1)
    iota(full("JI"), [[1, 128]], 0, 0)
    iota(full("DIF"), [[1, 128]], 0, -1)
    iota(full("NF", 256), [[1, 256]], 512, 0)
    iota(full("ELI", 8), [[16, 8]], 15, 0)
    iota(full("EPI"), [[1, 16], [16, 8]], 0, -1)

    GP, KK, PF, RV, K0, K37, K37A, MP, P16, RA, AK, N1, N2, N3, P4 = [("COL", i, i + 1) for i in range(15)]
    ms(full("MX", PIECE), 1.0)
    ts(full("PG", 1), full("PI", 1), 4, A.arith_shift_right)
    ts(full("PK", 1), full("PI", 1), 15, A.bitwise_and)
    ms(("MX", 0, PIECE, 16), 0.0)
    tc(GP, full("PG", 1))
    tc(KK, full("PK", 1))
    tc(PF, full("PI", 1))
    ts(full("IB"), full("DIF"), 0.0, A.is_equal)
    ts(full("JM"), full("JI"), 15, A.bitwise_and)

    ts(("ZO", 0, 256), full("Z0B", 256), 0.5, A.mult, 512.0, A.add)
    send("z00", *games("ZO", 0), "l0")
    ts(K37, KK, 37.0, A.mult)
    ts(RV, GP, 32.0, A.mult, PF, A.subtract)
    ts(full("KC"), full("JM"), 32.0, A.mult, 480.0, A.subtract)
    ts(full("MK"), full("JM"), KK, A.is_equal)
    ts(full("REV"), full("JI"), 15.0, A.subtract, RV, A.is_equal)
    tc(full("MV16", 16), full("MV32", 16))
    for c in range(NCH):
        lo, off = games("LU", c), listed("MV16", c)
        op("v", g.vector.tensor_copy, dict(out=ap(lo), in_=ind(("VP32", 0, 512), off)), [("VP32", 0, 512), off], [lo])
        if c:
            send("z0%d" % c, *games("ZO", c))
        send("l0%d" % c, *lo)
    g.sync.wait_ge(T.sem.l0, state["sent"]["l0"])
    dma("d", T.VO32[:], T.vo[:], [], [("VO32", 0, 512)])
    dma("d", T.RT[:, EARLY:4096], T.strat[:, EARLY:4096], [], [("RT", EARLY, 4096)])

    ts(full("JS"), full("JI"), 4, A.arith_shift_right)
    ts(K0, KK, 0.0, A.is_equal)
    for n, v in (("ONE", 1.0), ("ONB", 1.0), ("C5", -512.0), ("C10", -1024.0)):
        ms(full(n), v)
    ts(full("BLK"), full("JS"), GP, A.is_equal)
    tc(full("WTF", 1), full("WT32", 1))
    ms(full("CB"), 2.0 ** 17, (0, 32))
    act(full("MN", PIECE), full("MX", PIECE), F.Identity, bias=512.0, scale=-512.0)
    for n, v in (("IH", 0.5), ("NH", -0.5), ("NI4", -4096.0), ("I4", 4096.0), ("NIF", -1.0), ("IF", 1.0)):
        act(full(n), full("IB"), F.Copy, scale=v)
    act(full("NM"), full("MK"), F.Identity, bias=-2.0 ** 23, scale=2.0 ** 23)
    act(full("PV", 512), full("VP32", 512), F.Copy)
    act(("RT", 4096, RW), ("RT", 0, RW - 4096), F.Copy)
    for t, n in enumerate((0.0, N1, N2, N3)):
        if t:
            ts(n, K0, 256.0 * t, A.mult)
        act(("NC", 256 * t, 256 * t + 256), full("NF", 256), F.Identity, scale=K0, bias=n)
    ts(full("WB"), full("BLK"), full("WTF", 1), A.mult, 2.0, A.mult)
    ms(full("CB"), 2.0 ** 7, (32, 64))
    ts(full("QB", 8), ("JI", 0, 8), GP, A.is_equal, BIG, A.mult)
    ts(full("QBH", 8), ("JI", 0, 8), GP, A.is_equal, BIG / 2, A.mult)
    for c in range(NCH):
        ts(wide("C8", c), full("JM"), 15.5 - KB[c][0], A.is_gt, -8 * BIG / 128, A.mult)
    ms(full("CB"), 0.5, (64, 128))
    if min(SIZE) < 128:
        ms(full("PS", 128 * NCH), -65536.0)
    ts(full("C8", 128 * NCH), full("C8", 128 * NCH), -2.5 * BIG / 128, A.add)
    ts(full("T1"), full("BLK"), 1000.0, A.mult, 1000.0, A.subtract)
    tc(full("EL", 8), full("ELI", 8))
    ms(("C8", 0, 128 * NCH, 16), BIG / 128)
    for a, v in ((0, -1.0 / 4096), (8, -1.0 / 4096), (16, 1.0)):
        ts(("QF", a, a + 8), ("JI", 0, 8), GP, A.is_equal, v, A.mult)
    ts(("RC", 0, 8), ("JI", 0, 8), 2.0, A.mult)
    for c in range(NCH):
        ts(listed("PC", c), ("JI", 0, SIZE[c] // 16), 2.0, A.mult)
    ms(("RC", 8, 16), 0.0)
    ms(("RC", 16, 24), -32.0 * 129)
    ts(MP, KK, 16.0, A.mult, M23, A.add)
    ts(P16, KK, 16.0, A.mult, 7.5, A.add)
    ts(P4, KK, 16.0, A.mult, 0.4, A.add)
    tt(full("DB"), full("DIF"), full("T1"), A.add)
    ms(full("H5"), 0.5)
    ms(full("CA", 2), -127.5 / 128)
    ts(full("SH1"), full("DB"), 1.0, A.is_equal)
    ts(K37A, KK, 37.0, A.mult, 127.5, A.add)
    ts(full("SH2"), full("DB"), 2.0, A.is_equal)
    ts(full("ROW1"), full("JM"), 1.0, A.is_equal)
    ts(full("ROW0"), full("JM"), 0.0, A.is_equal)
    ts(full("EP"), full("EPI"), 0.0, A.is_equal)
    act(full("OV", 512), full("VO32", 512), F.Copy)
    send("v0", "OV", 0, 512)

    def bulk():
        send("v1", "PV", 0, 512)
        send("h1", "LU", 0, 256)
        send("v2", "OV", 0, 512)
        send("v3", "PV", 0, 512)
        send("h0", "LU", 0, 256)

    def u_sum(t, c):
        n, z = SIZE[c], games("ZI", c, t)
        mm(("pX", 256, 256 + n), full("WB"), full("C5", n), True, False)
        mm(("pX", 256, 256 + n), full("WB"), z, False, True)
        u = games("pU", c)
        mm(u, full("WB"), full("C5", n), True, False)
        mm(u, full("CB"), full("ONB", n), False, False)
        mm(u, full("WB"), z, False, False)

    def u_mod(t, c):
        act(games("U2", c), ("pX", 256, 256 + SIZE[c]), F.Identity, bias=1024.5 + 2.0 ** -13, scale=1.0 / 4096)

    def u_off(t, c):
        mm(games("pU", c), full("NI4"), games("U2", c), False, True)

    def product(t, c):
        tt(games("AT", c), games("LI", c, t), games("pU", c), A.mult)

    def shift(t, c):
        ts(games("AS", c), games("AT", c), 5, A.arith_shift_right, 4095, A.bitwise_and)

    def offsets(t, c):
        if "offsets%d" % c in ON_S:
            act(games("OF", c), games("AS", c), F.Identity, bias=K37 if t == 0 else AK)
        else:
            ts(games("OF", c), games("AS", c), K37 if t == 0 else AK, A.add)

    def z_psum(t, c):
        mm(games("pZ", c), full("IH"), full("C5", SIZE[c]), True, False)
        mm(games("pZ", c), full("IH"), games("ZI", c, t), False, True)

    def key_t(t, c):
        mm(("pX", 0, 128), full("ONE", SIZE[c]), full("KC"), True, False)
        mm(("pX", 0, 128), games("LI", c, t), full("REV"), False, True)

    def key_s(t, c):
        act(wide("BT", c), ("pX", 0, 128), F.Copy, p=SIZE[c])

    def place_t(t, h):
        mm(("pW", 0, 128), full("IB"), full("NM"), True, False)
        mm(("pW", 0, 128), ("ZI", 256 * t + 128 * h, 256 * t + 128 * h + 128), full("WB"), False, True)

    def place_s(h):
        act(wide("ZU", h), ("pW", 0, 128), F.Relu, bias=-7.5)

    def place_sum():
        for h in range(2):
            mm(("pW", 256 + 8 * h, 264 + 8 * h), wide("ZU", h), ("QF", 16, 24), True, True)

    def place_up():
        act(("RR", 16, 32), ("pW", 256, 272), F.Identity, bias=M27)

    def place_down():
        act(full("RR", 16), ("RR", 16, 32), F.Identity, bias=-M27)

    def place_mod():
        mm(("pU", 256, 272), full("ONE"), full("PC", 16), True, False)
        for h in range(2):
            mm(("pU", 256 + 8 * h, 264 + 8 * h), wide("ZU", h), ("QF", 16, 24), False, False)
        mm(("pU", 256, 272), full("NIF"), full("RR", 16), False, True)

    def place_out():
        act(full("PL", 16), ("pU", 256, 272), F.Identity, bias=P16)

    def old_bank(c):
        return ("pZ", 256, 256 + SIZE[c])

    def old(t, c):
        act(games("OLD", c), games("RT", c, 0, 16), F.Identity, bias=-0.5, off=listed("PL", c))

    def old_t(t, c):
        if "mean%d" % c in ON_S:
            o = ("pW", 384, 384 + SIZE[c])
            mm(o, full("IH"), games("OLD", c), True, False)
            mm(o, full("IF"), games("ZO", c, t + 1), False, True)
        else:
            mm(old_bank(c), full("IH"), full("C10", SIZE[c]), True, False)
            mm(old_bank(c), full("IH"), games("OLD", c), False, True)

    def gather(c, a, b, q):
        a, b = CH[c] + a, CH[c] + b
        y, of, w = ("Y", 16 * a, 16 * b), ("OF", a, b), ("RT", 0, RW)
        if q == "s":
            act(y, w, F.Copy, scale=0.25, off=of)
        else:
            op("v", g.vector.tensor_scalar, dict(out=ap(y), in0=ind(w, of), scalar1=0.25, scalar2=None, op0=A.mult), [w, of], [y])

    def row(c, k):
        return ("Y", 16 * CH[c] + k, 16 * CH[c + 1], 16)

    def beat(c, k0, k1):
        return ("B", 16 * CH[c] + SIZE[c] * k0, 16 * CH[c] + SIZE[c] * k1)

    def diff(t, c, i):
        k0, k1, n = KB[c][i], KB[c][i + 1], SIZE[c]
        for k in range(k0, k1):
            o = ("pD%d" % (i % 2), n * (k - k0), n * (k - k0 + 1))
            mm(o, full("NH"), games("ZI", c, t), True, False)
            mm(o, full("IB"), row(c, k), False, True)

    def sign(t, c, i):
        k0, k1 = KB[c][i], KB[c][i + 1]
        act(beat(c, k0, k1), ("pD%d" % (i % 2), 0, SIZE[c] * (k1 - k0)), F.Sign, bias=256.0 - 0.125)

    def compare_v(t, c):
        for k in range(KB[c][0]):
            tt(beat(c, k, k + 1), row(c, k), games("pZ", c), A.is_gt)

    def beats(t, c, i):
        ks = list(range(KB[c][i], KB[c][i + 1]))
        if i == len(KB[c]) - 3:
            ks = list(range(KB[c][0])) + ks
        if i == 0:
            mm(wide("pC", c), full("ONE", SIZE[c]), wide("C8", c), True, False)
        for k in ks:
            mm(("pC", 128 * c + 15 - k, 128 * c + 128, 16), beat(c, k, k + 1), full("QB" if k < KB[c][0] else "QBH", 8), False, k == 14)

    def running(c, hi, a, b):
        y = ("Y", 16 * (CH[c] + a), 16 * (CH[c] + b))
        if hi:
            scan(("HI",) + y[1:], ("MX", 0, 16 * (b - a)), y, A.mult, A.max)
        else:
            scan(("LO",) + y[1:], ("MN", 0, 16 * (b - a)), y, A.add, A.min)

    def verdict(t, c):
        scan(wide("PS", c), wide("pC", c), wide("BT", c), A.max, A.min, SIZE[c])

    def spread(t, c):
        tti(wide("KX", c), wide("PS", c), full("EL", 8), full("MK"), A.mult)

    def lists(t, c):
        n = SIZE[c]
        mm(("pR", 0, 16), full("ONE"), full("RC", 16), True, False)
        mm(("pR", 0, 16), wide("KX", c), full("QF", 16), False, True, n)

    def list_k(t, c):
        if "list_k%d" % c in ON_S:
            act(listed("LK", c), ("pR", 0, SIZE[c] // 16), F.Identity, bias=P4)
        else:
            ts(listed("LK", c), ("pR", 0, SIZE[c] // 16), MP, A.add, M23, A.subtract)

    def kappa(t, c):
        k, n = listed("KO", c, t), SIZE[c] // 16
        act(k, ("pR", 8, 8 + n), F.Identity, bias=129.0)

    def named(t, c):
        k, n = listed("KO", c, t), SIZE[c] // 16
        mm(("pX", 128, 128 + n), full("ONE"), ("RC", 16, 16 + n), True, False)
        mm(("pX", 128, 128 + n), wide("KX", c), ("QF", 16, 16 + n), False, False, SIZE[c])
        mm(("pX", 128, 128 + n), full("I4"), k, False, True)

    def list_n(t, c):
        act(listed("LN", c), ("pX", 128, 128 + SIZE[c] // 16), F.Copy)

    def pick_hi(t, c):
        act(games("HG", c), games("HI", c, 0, 16), F.Identity, bias=512.0 - 0.125, off=listed("LK", c))

    def new_z(t, c):
        z = games("ZO", c, t + 1)
        tti(z, games("LO", c, 0, 16), listed("LK", c), games("HG", c), A.add)
        if t == TURNS - 1:
            ts(games("ZL", c), z, 2.0, A.mult, 1024.0, A.subtract)
            z = games("ZL", c)
        send("z%d%d" % (t + 1, c), *z)

    def views(t, c):
        l = games("LU", c, t + 1) if t < TURNS - 1 else games("EO", c)
        tti(l, full("TAB%d" % t, 512 + 256 * t), listed("LN", c), games("NC", c, t), A.add)
        send("l%d%d" % (t + 1, c), *l)

    def mean(t, c):
        n, z = SIZE[c], games("ZO", c, t + 1)
        if "mean%d" % c in ON_S:
            act(games("RZ", c), ("pW", 384, 384 + n), F.Identity, bias=-512.0)
        else:
            tt(games("RZ", c), old_bank(c), z, A.add)

    def scatter(t, c):
        win, off = games("RT", c, 0, 16), listed("PL", c)
        op("v", g.vector.tensor_copy, dict(out=ind(win, off), in_=ap(games("RZ", c))), [off, games("RZ", c)], [win])

    def behind():
        dma("d", T.RT[:, 4096:RW], T.RT[:, 0:RW - 4096], [("RT", 0, RW - 4096)], [("RT", 4096, RW)])

    def count():
        act(full("SG", 8 * NCH), ("PS", 15, 128 * NCH, 16), F.Sign, bias=58000.0, accum=full("ACC", 1))

    def count_t():
        mm(("pD0", 0, 1), full("ONE"), ("CA", 0, 1), True, False)
        mm(("pD0", 0, 1), full("H5"), full("ACC", 1), False, True)

    def count_a():
        if "count" in ON_S:
            act(full("AQ", 1), ("pD0", 0, 1), F.Identity, scale=1.0 / 256)
            act(RA, ("pD0", 0, 1), F.Identity, bias=K37A)
        else:
            ts(RA, ("pD0", 0, 1), M31, A.add, M31, A.subtract)

    def count_b():
        if "count" in ON_S:
            act(AK, full("AQ", 1), F.Identity, bias=RA, scale=-256.0)
        else:
            ts(AK, ("pD0", 0, 1), RA, A.subtract, K37A, A.add)

    parts = {(0, 0): [(0, 0, "VI0", 1, 0)], (0, 1): [(1, 0, "VI1", 1, 0)], (1, 0): [(1, 512, "HL1", 2, 0), (3, 512, "HL3", 2, 0)],
             (1, 1): [(2, 0, "VI2", 1, 0)], (2, 0): [(2, 512, "HB2", 1, 0), (2, 768, "HB2", 2, 1)], (2, 1): [(3, 0, "VI3", 1, 0)],
             (3, 0): [(3, 768, "HB3", 1, 0), (3, 1024, "HB3", 2, 2)]}

    def table(key):
        a = 0
        for tb, c0, src, sh, n in parts[key]:
            wd = 512 if src[0] == "V" else 256
            w = ("pW", a, a + wd)
            mm(w, full("SH%d" % sh), full(src, wd), True, sh == 1)
            if sh == 2:
                mm(w, full("ROW1"), ("NC", 256 * n, 256 * n + 256), False, True, 1)
            a += wd

    def table_s(key):
        (tb, c0), (tb2, _) = parts[key][0][:2], parts[key][-1][:2]
        if tb == tb2:
            act(("TAB%d" % tb, c0, c0 + 512), full("pW", 512), F.Copy)
        else:
            for a, x in ((0, tb), (256, tb2)):
                act(("TAB%d" % x, c0, c0 + 256), ("pW", a, a + 256), F.Copy)

    def verdicts_out(a, b):
        w = 16 * (b - a)
        for p in range(16):
            mm(("pW", p, w, 16), ("EP", 8 * p, 8 * p + 8), ("KI", a, b), True, True)
        act(("YKS", 16 * a, 16 * b), ("pW", 0, w), F.Identity, bias=-129.0, p=8)
        dma("d", T.yk[:, 16 * a:16 * b], T.YKS[:, 16 * a:16 * b], [("YKS", 16 * a, 16 * b)], [("yk", 16 * a, 16 * b)])

    def history(t):
        if t < 2:
            send("h%d" % (t + 2), "LU", 256 * t + 256, 256 * t + 512)
        send("y%d" % t, "KO", 16 * t, 16 * t + 16)

    def views_out():
        mm(("pW", 0, 256), full("SH1"), full("L3I", 256), True, False)
        mm(("pW", 0, 256), full("ROW0"), ("NC", 768, 1024), False, True, 1)
        act(full("YOS", 256), ("pW", 0, 256), F.Copy)
        dma("d", T.yo[:], T.YOS[:], [full("YOS", 256)], [("yo", 0, 256)])

    def chunk_out(c, qp, qz):
        a, b = CH[c], CH[c + 1]
        dma(qp, T.yp[:, a:b], T.EF[:, a:b], [("EF", a, b)], [("yp", a, b)])
        dma(qz, T.yz[:, a:b], T.ZF[:, a:b], [("ZF", a, b)], [("yz", a, b)])

    def steps(t):
        last = t == TURNS - 1
        s = {}
        ahead = dict(u_sum=u_sum, u_mod=u_mod, u_off=u_off, product=product, shift=shift, offsets=offsets, key_t=key_t, key_s=key_s, z_psum=z_psum)
        every = dict(compare_v=compare_v, verdict=verdict, spread=spread, lists=lists, list_k=list_k, kappa=kappa, named=named, pick_hi=pick_hi,
                     list_n=list_n, new_z=new_z, views=views)
        if not last:
            every.update(old=old, old_t=old_t, mean=mean, scatter=scatter)
            for name in ahead:
                s["n_" + name] = lambda f=ahead[name]: f(t + 1, 0)
        for c in range(NCH):
            for name, f in list(every.items()) + (list(ahead.items()) if c else []):
                s["%s%d" % (name, c)] = lambda c=c, f=f: f(t, c)
            cut = (0,) + GS[c]
            for i in range(len(GS[c])):
                s["gather_s%d%s" % (c, "abc"[i])] = lambda c=c, a=cut[i], b=cut[i + 1]: gather(c, a, b, "s")
            s["gather_v%d" % c] = lambda c=c: gather(c, GS[c][-1], SIZE[c], "v")
            for x, a, b in (("a", 0, GS[c][-1]), ("b", GS[c][-1], SIZE[c])):
                s["hi%d%s" % (c, x)] = lambda c=c, a=a, b=b: running(c, True, a, b)
                s["lo%d%s" % (c, x)] = lambda c=c, a=a, b=b: running(c, False, a, b)
            for i in range(len(KB[c]) - 1):
                for name, f in (("diff", diff), ("sign", sign), ("beats", beats)):
                    s["%s%d%d" % (name, c, i)] = lambda c=c, i=i, f=f: f(t, c, i)
            if last:
                s["last%d" % c] = lambda c=c: send("y3%d" % c, *listed("KO", c, 3))
                if c < NCH - 1:
                    s["out_c%d" % c] = lambda c=c: chunk_out(c, "d", "d")
        if not last:
            for h in range(2):
                s["place_t%d" % h] = lambda h=h: place_t(t, h)
                s["place_s%d" % h] = lambda h=h: place_s(h)
            s.update(place_sum=place_sum, place_up=place_up, place_down=place_down, place_mod=place_mod, place_out=place_out, behind=behind,
                     count=count, count_t=count_t, count_a=count_a, count_b=count_b, history=lambda: history(t),
                     table_a=lambda: table((t, 1)), table_as=lambda: table_s((t, 1)), table_b=lambda: table((t + 1, 0)), table_bs=lambda: table_s((t + 1, 0)))
        else:
            s.update(last_l=lambda: send("w", "LI", 768, 1024), out_k0=lambda: verdicts_out(0, 32), out_k1=lambda: verdicts_out(32, 48), out_o=views_out)
        if t == 0:
            s.update(table_0=lambda: table((0, 0)), table_0s=lambda: table_s((0, 0)), bulk=bulk)
        return s

    for f in (u_sum, u_mod, u_off, product, shift, offsets, key_t, key_s, z_psum):
        f(0, 0)
    for t in range(TURNS):
        s = steps(t)
        for n in (FIRST, ORDER, ORDER, LAST)[t]:
            if n in s:
                s.pop(n)()
        assert not s

    verdicts_out(48, 64)
    chunk_out(NCH - 1, "d", "s")
    used.update(state["sent"])
    for s in sorted(used):
        if known["g"].get(s, 0) < used[s]:
            g.wait_ge(T.sem[s], used[s])
